import numpy as np, ml_dtypes
CORES = [35,38,43,46]
N = 4
import mx_ref
BF = ml_dtypes.bfloat16
def cols(t, e):
    v = np.concatenate([t.reshape(128, -1, 4), np.zeros((128, 1, 4), BF)], axis=1)
    return np.ascontiguousarray(v[:, e]).reshape(128, -1)
def pick(q, e):
    c = np.concatenate([q[0].reshape(128, -1, 4), np.zeros((128, 1, 4), np.uint8)], axis=1); s = np.concatenate([q[1], np.ones((16, 1), np.uint8)], axis=1)
    return (np.ascontiguousarray(c[:, e].reshape(128, -1)), np.ascontiguousarray(s[:, e]))
def join(*qs):
    return (np.concatenate([q[0] for q in qs], axis=1), np.concatenate([q[1] for q in qs], axis=1))
def put(q, e, v):
    c, s = q[0].reshape(128, -1, 4).copy(), q[1].copy(); c[:, e] = v[0].reshape(128, -1, 4); s[:, e] = v[1]
    return (c.reshape(128, -1), s)
def pk(c, s):
    return (np.ascontiguousarray(c), mx_ref.live(s))
def emit(q):
    return q[0], q[1]
def decode(q):
    o = []
    for b in range(4):
        e = np.zeros((128, 128, 4), np.float32); e[np.arange(128), np.arange(128), b] = 1
        o.append(mx_ref.matmul(mx_ref.quantize(e.reshape(128, 512).astype(BF)), q))
    return np.stack(o, axis=2).reshape(128, -1)
def f(rng, *shape):
    return mx_ref.flush((rng.standard_normal(shape, dtype=np.float32) * np.exp2(rng.integers(-2, 3, shape[:-1] + (1,)))).astype(BF))
def wide(rng, *shape, cols=0):
    v = rng.standard_normal(shape, dtype=np.float32) * np.exp2(rng.integers(-12, 13, shape)).astype(np.float32)
    if cols: v *= np.repeat(np.exp2(rng.integers(-cols, cols + 1, shape[:-2] + (1, shape[-1] // 4))) * (rng.random(shape[:-2] + (1, shape[-1] // 4)) > 0.0625), 4, axis=-1).astype(np.float32)
    return mx_ref.flush(v.astype(BF))
P, K, O = 256, 64, 1
def big(v):
    v = np.array(v.astype(np.float32))
    v[np.abs(v) < np.float32(2.0 ** -16)] = 0
    return v.astype(BF)
def sized(t, a):
    return big(t.astype(np.float32) * np.repeat(np.asarray(a, np.float32), 4, axis=-1))
def query(rng):
    v = np.zeros((N, 128, 512), BF)
    v[:, :, :4] = f(rng, 1, 128, 4)
    return v
def plain(rng):
    return {"lv": big(f(rng, N, 128, 4 * P)), "dm": big(f(rng, N, 128, 4 * P)), "nz": big(f(rng, N, 128, 4 * P)), "u": query(rng), "z": query(rng), "w": f(rng, N, 128, 512 * O)}
def positive(d):
    return {k: v if k == "w" else np.abs(v.astype(np.float32)).astype(BF) for k, v in d.items()}
def onto(t, e, rng):
    at, far = np.arange(N * P), e[e >= P]
    free = rng.permutation(np.setdiff1d(np.arange(P), e))[:far.size]
    at[free], at[far] = far, free
    return np.stack(np.split(cols(np.concatenate(t, axis=1), at), N, axis=1))
def setup_inputs(rng):
    return plain(rng)
def setup_inputs_ties(rng):
    d = plain(rng)
    for k in ("lv", "dm", "nz"):
        v = big((1 + rng.random((128, 48))) * 2.0 ** 27)
        d[k] = np.stack([big(cols(v, rng.permutation(np.arange(P) % 12)).astype(np.float32) * np.repeat(1 - 2 * rng.integers(0, 2, P), 4)) for r in range(N)])
    for k in ("u", "z"): d[k][:, :, :4] = big((1 + rng.random((1, 128, 4))) * 2.0 ** 29)
    return d
def setup_inputs_one(rng):
    d = positive(plain(rng))
    a, b = rng.permutation(N)[:2]
    g, h = np.ones((N, P)), np.ones((N, P))
    g[a, rng.permutation(P)[:K]] = 2.0 ** -8
    g[b, rng.permutation(P)[:K]] = 2.0 ** -4
    h[b, rng.permutation(P)[:K]] = 2.0 ** 8
    h[a, rng.permutation(P)[:K]] = 2.0 ** 4
    d["lv"], d["dm"] = sized(d["lv"], g[:, None]), sized(d["dm"], h[:, None])
    return d
def setup_inputs_again(rng):
    d = positive(plain(rng))
    n, top = K // N, (np.arange(128) < 64)[None, :, None]
    lt, lb, dt, db, nt = np.ones((5, N, P))
    for r in range(N):
        at, to = rng.permutation(P), rng.permutation(P)
        lt[r, at[:n]], lt[r, at[n:2 * n]] = 2.0 ** -6, 2.0 ** -3
        lb[r, at[:n:2]] = 2.0 ** 8
        nt[r, at[:n // 2]], nt[r, at[n // 2:n]] = 2.0 ** -8, 2.0 ** 4
        dt[r, to[:n]] = 2.0 ** -8
        db[r, to[:n]], db[r, to[n:2 * n]] = 2.0 ** 6, 2.0 ** 3
    d["lv"] = sized(d["lv"], np.where(top, lt[:, None], lb[:, None]))
    d["dm"] = sized(d["dm"], np.where(top, dt[:, None], db[:, None]))
    d["nz"] = sized(d["nz"], np.where(top, nt[:, None], 1.0))
    d["u"], d["z"] = big(d["u"].astype(np.float32) * top), big(d["z"].astype(np.float32) * ~top)
    return d
def setup_inputs_zero(rng):
    d = plain(rng)
    g, h, e = np.ones((3, N, P))
    for r in range(N):
        g[r, rng.permutation(P)[:3 * K // (2 * N)]] = 0
        h[r, rng.permutation(P)[K // (2 * N):]] = 0
        e[r, rng.permutation(P)[:P // 2]] = 0
    d["lv"], d["dm"], d["nz"] = sized(d["lv"], g[:, None]), sized(d["dm"], h[:, None]), sized(d["nz"], e[:, None])
    return d
def setup_inputs_spread(rng):
    d = plain(rng)
    d["lv"] = sized(wide(rng, N, 128, 4 * P), 32 * np.exp2(rng.integers(-6, 7, (N, 1, P))))
    for k in ("dm", "nz"): d[k] = sized(wide(rng, N, 128, 4 * P, cols=6), np.full((1, 1, P), 32.0))
    for k in ("u", "z"): d[k] = sized(d[k], np.full((1, 1, 128), 2.0 ** 24))
    low = np.concatenate([score(d["u"][r], mx_ref.quantize(np.ascontiguousarray(d["lv"][r]))) for r in range(N)])
    high = np.concatenate([score(d["z"][r], mx_ref.quantize(np.ascontiguousarray(d["dm"][r]))) for r in range(N)])
    d["lv"] = onto(d["lv"], np.argsort(low, kind="stable")[:K], rng)
    d["dm"] = onto(d["dm"], np.argsort(-high, kind="stable")[:K], rng)
    return d
def check_inputs(d):
    b = []
    for k, lo, hi in (("lv", -16, 28), ("dm", -16, 28), ("nz", -16, 28), ("u", -30, 30), ("z", -30, 30), ("w", -30, 30)):
        v = np.abs(d[k].astype(np.float32))
        if not (np.isfinite(v).all() and ((v == 0) | (v >= 2.0 ** lo) & (v <= 2.0 ** hi)).all()): b.append("a value of " + k)
    for k in ("u", "z"):
        v = d[k].astype(np.float32)
        if (v[:, :, 4:] != 0).any(): b.append(k + " has numbers behind its column 0")
        if (v != v[:1]).any(): b.append(k + " isn't the same on all ranks")
    return b
def score(t, q):
    return np.abs(mx_ref.matmul(mx_ref.quantize(np.ascontiguousarray(t)), q)[0]) + np.float32(0)
def reference(lv, dm, nz, u, z, w):
    L = [mx_ref.quantize(np.ascontiguousarray(lv[r])) for r in range(N)]
    X = [mx_ref.quantize(np.ascontiguousarray(dm[r])) for r in range(N)]
    noise = join(*[mx_ref.quantize(np.ascontiguousarray(nz[r])) for r in range(N)])
    oc, osc = np.zeros((N, 128, 8 * P), np.uint8), np.zeros((N, 16, 2 * P), np.uint8)
    sw, lw, y = np.zeros((N, 2, K), np.float32), np.zeros((N, 2, K), np.float32), np.zeros((N, 128, O * P), np.float32)
    for t in range(2):
        low = np.argsort(np.concatenate([score(u[r], L[r]) for r in range(N)]), kind="stable")[:K]
        high = np.argsort(-np.concatenate([score(z[r], X[r]) for r in range(N)]), kind="stable")[:K]
        lw[:, t], sw[:, t] = low, high
        gone, come = pick(join(*L), low), pick(join(*X), high)
        v = decode(come) * np.float32(0.5) + decode(pick(noise, low)) * np.float32(0.5)
        new = mx_ref.quantize(np.ascontiguousarray(v.astype(BF)))
        for r in range(N):
            a, b = np.flatnonzero(low // P == r), np.flatnonzero(high // P == r)
            L[r] = put(L[r], low[a] - P * r, pick(new, a))
            X[r] = put(X[r], high[b] - P * r, pick(gone, b))
    for r in range(N):
        oc[r], osc[r] = emit(join(L[r], X[r]))
        for o in range(O):
            y[r, :, P * o:P * o + P] = mx_ref.matmul(mx_ref.quantize(np.ascontiguousarray(w[r][:, 512 * o:512 * o + 512])), L[r])
    return {"oc": oc, "osc": osc, "sw": sw, "lw": lw, "y": y}

@@ -1,0 +1,474 @@
+from concourse.bass import DstId, RemoteDMATransfer
+from concourse.mybir import dt, AluOpType as A, AxisListType, ActivationFunctionType as AF
+
+F8 = "float8_e4m3fn_x4"
+TINY = 2.0 ** -118
+ROUNDS = 2
+
+SCRATCH = {
+    "t_lv": ("sbuf", [128, 1024], "bfloat16"), "t_dm": ("sbuf", [128, 1024], "bfloat16"),
+    "t_nz": ("sbuf", [128, 1024], "bfloat16"), "t_w": ("sbuf", [128, 512], "bfloat16"),
+    "u0": ("sbuf", [128, 4], "bfloat16"), "z0": ("sbuf", [128, 4], "bfloat16"),
+    "uz": ("sbuf", [128, 1024], "bfloat16"),
+    "qU": ("sbuf", [128, 256], F8), "sU": ("sbuf", [128, 256], "uint8"),
+    "qW": ("sbuf", [128, 128], F8), "sW": ("sbuf", [128, 128], "uint8"),
+    "ones": ("sbuf", [128, 128], "bfloat16"), "zer": ("sbuf", [128, 128], "bfloat16"),
+    "SS": ("sbuf", [128, 1024], "bfloat16"), "SI": ("sbuf", [128, 1536], "bfloat16"), "EE": ("sbuf", [128, 2048], "bfloat16"),
+    "qS": ("sbuf", [128, 256], F8), "sS": ("sbuf", [128, 256], "uint8"),
+    "qI": ("sbuf", [128, 384], F8), "sI": ("sbuf", [128, 384], "uint8"),
+    "qE": ("sbuf", [128, 512], F8), "sE": ("sbuf", [128, 512], "uint8"),
+    "pI": ("sbuf", [128, 1], "int32"), "ii": ("sbuf", [128, 8], "int32"), "fc": ("sbuf", [128, 8], "float32"),
+    "cc": ("sbuf", [128, 16], "float32"),
+    "dif": ("sbuf", [128, 256], "float32"), "Mneg": ("sbuf", [128, 256], "float32"), "Mtri": ("sbuf", [128, 256], "float32"),
+    "idt": ("sbuf", [128, 128], "bfloat16"),
+    "Kn": ("sbuf", [128, 128], "bfloat16"), "RC": ("sbuf", [128, 128], "float32"), "sel": ("sbuf", [128, 4], "float32"),
+    "io8": ("sbuf", [128, 8], "float32"), "kk8": ("sbuf", [128, 8], "float32"),
+    "io32": ("sbuf", [128, 32], "float32"), "DG": ("sbuf", [128, 32], "bfloat16"),
+    "VO": ("sbuf", [128, 96], "bfloat16"), "OE": ("sbuf", [128, 6], "float32"),
+    "plrow": ("sbuf", [128, 512], "float32"), "urow": ("sbuf", [128, 512], "float32"),
+    "pA": ("psum", [128, 512], "float32"), "pB": ("psum", [128, 512], "float32"), "pC": ("psum", [128, 2048], "float32"),
+    "pD": ("psum", [128, 512], "float32"), "pE": ("psum", [128, 512], "float32"),
+    "yt": ("sbuf", [128, 256], "float32"),
+    "FN": ("sbuf", [128, 512], F8), "FNs": ("sbuf", [128, 512], "uint8"),
+}
+ONCE = ("yd", "DD", "KX", "KT", "dk", "Dc", "tr2", "trU", "trX", "qH", "sH", "H", "Gs", "trG", "sC", "Vc", "rk", "trA", "wk",
+        "VT", "XR", "R", "pw", "ow", "ix", "own", "NEW", "iw", "lo16", "ky", "qF", "sF", "qG", "sG")
+for _n, _w, _d in (
+        ("SW", 768, F8), ("SWs", 768, "uint8"), ("LW", 704, F8), ("LWs", 704, "uint8"), ("XW", 384, F8), ("XWs", 384, "uint8"),
+        ("LN", 384, F8), ("LNs", 384, "uint8"), ("PS", 64, F8), ("PSs", 64, "uint8"), ("NP", 128, F8), ("NPs", 128, "uint8"),
+        ("qH", 128, F8), ("sH", 128, "uint8"), ("qF", 128, F8), ("sF", 128, "uint8"), ("qG", 128, F8), ("sG", 128, "uint8"),
+        ("H", 512, "bfloat16"), ("F", 2048, "bfloat16"), ("NEW", 512, "bfloat16"), ("VT", 96, "bfloat16"),
+        ("sC", 4, "float32"), ("Vc", 512, "float32"), ("yd", 512, "float32"), ("DD", 1024, "bfloat16"), ("rk", 4, "float32"),
+        ("trA", 128, "float32"), ("Gs", 128, "float32"), ("trG", 128, "float32"), ("M", 2, "float32"), ("MP", 2, "float32"),
+        ("dg", 8, "float32"), ("wk", 4, "float32"), ("own", 4, "float32"),
+        ("landM", 6, "float32"), ("landP", 6, "float32"), ("XR", 256, "float32"), ("R", 256, "float32"),
+        ("Dc", 768, "bfloat16"), ("cn", 4, "float32"), ("pw", 32, "float32"), ("ow", 16, "float32"),
+        ("tr2", 256, "float32"), ("ix", 32, "float32"), ("UL", 1408, "float32"), ("UX", 1408, "float32"),
+        ("trU", 512, "float32"), ("trX", 512, "float32"), ("lo16", 192, "uint16"), ("iw", 24, "int32"),
+        ("ky", 32, "float32"), ("KX", 128, "float32"), ("KT", 128, "float32"), ("dk", 256, "float32"), ("pt", 8, "float32")):
+    for _t in range(1 if _n in ONCE else ROUNDS):
+        SCRATCH[_n + str(_t)] = ("sbuf", [128, _w], _d)
+
+SEMAPHORES = ["v", "s", "p", "gc", "ls"] + ["d%d" % k for k in range(60)] + \
+    [n + str(t) for n in ("aM", "aP", "aC") for t in range(ROUNDS)]
+
+
+def rank_program(g, core, T, topo):
+    rank = T.rank_of(core)
+    if rank is None:
+        return
+    cores = list(T.cores)
+    others = [q for q in range(4) if q != rank]
+    Q = {"v": g.vector, "s": g.scalar, "p": g.tensor, "gc": g, "y": g.sync}
+    cnt, seen, top, nd = {}, {}, {}, [0]
+
+    def need(qn, deps):
+        for d in deps:
+            if d is None:
+                continue
+            if isinstance(d, list):
+                need(qn, d)
+            elif seen.get((qn, d[0]), 0) < d[1]:
+                Q[qn].wait_ge(T.sem[d[0]], d[1])
+                seen[(qn, d[0])] = d[1]
+                top[d[0]] = max(top.get(d[0], 0), d[1])
+
+    def do(qn, deps, f):
+        need(qn, deps)
+        f(Q[qn]).then_inc(T.sem[qn], 1)
+        cnt[qn] = cnt.get(qn, 0) + 1
+        return (qn, cnt[qn])
+
+    def dma(qn, deps, out, in_):
+        need(qn, deps)
+        s = "d%d" % nd[0]
+        nd[0] += 1
+        Q[qn].dma_start(out, in_).then_inc(T.sem[s], 16)
+        cnt[s] = 16
+        return (s, 16)
+
+    def B(n, t):
+        return T[n + ("0" if n in ONCE else str(t))]
+
+    dst = [cores[q] for q in others]
+    far = [c for c in dst if topo.chip(c) != topo.chip(core)]
+    fe = topo.engines(core, far[0])
+    eng = {}
+    for n, c in enumerate(far):
+        w = len(fe) // len(far)
+        eng[c] = fe[n * w:(n + 1) * w]
+    for c in dst:
+        if c not in eng:
+            eng[c] = [e for e in topo.engines(core, c) if e not in fe]
+    arrive = sum(len(e) for e in eng.values())
+
+    def send(deps, sem, view, land):
+        need("gc", deps)
+        tr = []
+        for q, c in zip(others, dst):
+            rid, pid, _ = topo.addr(c)
+            s = [x for x in range(4) if x != q].index(rank)
+            tr.append(RemoteDMATransfer(dst_ids=[DstId(rid=rid, pnc=pid)], dma_engine_mask=sum(1 << e for e in eng[c]),
+                                        remote_sem=T.sem[sem], src=view, dst=land(s)))
+        g.remote_dma_fused(tr, local_sem=T.sem["ls"])
+        cnt["ls"] = cnt.get("ls", 0) + arrive
+        cnt[sem] = cnt.get(sem, 0) + arrive
+
+    def ts(o, i, s1, s2, *ops):
+        if len(ops) == 1:
+            return lambda q: q.tensor_scalar(o, i, s1, None, ops[0])
+        return lambda q: q.tensor_scalar(o, i, s1, s2, ops[0], ops[1])
+
+    def tt(o, a, b, op):
+        return lambda q: q.tensor_tensor(o, a, b, op)
+
+    def cp(o, i):
+        return lambda q: q.tensor_copy(o, i)
+
+    def act(o, i, fn, **k):
+        return lambda q: q.activation(o, i, fn, **k)
+
+    def red(o, i, op=A.add):
+        return lambda q: q.tensor_reduce(o, i, AxisListType.X, op)
+
+    def trn(o, i):
+        return lambda q: q.transpose(o, i)
+
+    def fill(o, c):
+        return lambda q: q.memset(o, c)
+
+    def iota(o, pat, base=0, cm=0):
+        return lambda q: q.iota(o, pat, base, cm, allow_small_or_imprecise_dtypes=True)
+
+    def quant(o, s, i):
+        return lambda q: q.quantize_mx(o, s, i)
+
+    def mm(o, a, sa, b, sb, st=True, sp=True):
+        return lambda q: q.matmul_mx(o, a, sa, b, sb, st, sp)
+
+    U8, U32 = dt.uint8, dt.uint32
+
+    d_lv = dma("y", [], T.t_lv[:], T.lv[:])
+    d_u = dma("s", [], T.u0[:], T.u[:, 0:4])
+    d_z = dma("s", [], T.z0[:], T.z[:, 0:4])
+    d_dm = dma("y", [], T.t_dm[:], T.dm[:])
+    d_nz = dma("y", [], T.t_nz[:], T.nz[:])
+    d_w = dma("y", [], T.t_w[:], T.w[:])
+
+    i_p = do("gc", [], lambda q: q.iota(T.pI[:], [[0, 1]], 0, 1))
+    i_df = do("gc", [], iota(T.dif[:], [[0, 2], [-1, 128]], 0, 1))
+    i_kn = do("gc", [], iota(T.Kn[:], [[16, 4], [0, 2], [1, 16]]))
+    v_one = do("v", [], fill(T.ones[:], 1.0))
+    v_zer = do("v", [], fill(T.zer[:], 0.0))
+    v_ss = do("v", [], fill(T.SS[:], 0.0))
+    bits = []
+    for c, m in enumerate((127, 15, 31, 63, 32, 64, 48, 127)):
+        bits.append(do("v", [i_p], ts(T.ii[:, c:c + 1], T.pI[:, 0:1], m, None, A.bitwise_and)))
+    v_fc = do("v", bits, cp(T.fc[:], T.ii[:]))
+    F_ = lambda c: T.fc[:, c:c + 1]
+    C_ = lambda c: T.cc[:, c:c + 1]
+    SG, M1, M0, P4, PF, KB0, KB1, AQ, D4, H0, H1, PK = range(12)
+    v_m1 = do("v", [i_df], ts(T.Mtri[:], T.dif[:], 0.0, 2 * TINY, A.is_gt, A.mult))
+    v_mn = do("v", [v_m1], ts(T.Mneg[:], T.Mtri[:], -1.0, TINY, A.mult, A.add))
+    v_mt = do("v", [v_mn], ts(T.Mtri[:], T.Mneg[:], -1.0, None, A.mult))
+
+    SW0, SWs0 = B("SW", 0), B("SWs", 0)
+    uz = []
+    for b in range(4):
+        uz.append(do("v", [d_u, v_one], ts(T.uz[:, b:512:4], T.ones[:], T.u0[:, b:b + 1], None, A.mult)))
+    for b in range(4):
+        uz.append(do("s", [d_z, v_zer], act(T.uz[:, 512 + b:1024:4], T.zer[:], AF.Identity, bias=T.z0[:, b:b + 1])))
+    q_u = do("v", uz, quant(T.qU[:], T.sU[:], T.uz[:]))
+    q_l = do("v", [d_lv], quant(SW0[:, 0:256], SWs0[:, 0:256], T.t_lv[:]))
+    q_x = do("v", [d_dm], quant(SW0[:, 256:512], SWs0[:, 256:512], T.t_dm[:]))
+
+    cst = []
+    for c, src, a, b in ((SG, 5, -1 / 32, 1.0), (M1, 4, 1 / 32, 0.0), (M0, 4, -1 / 32, 1.0), (P4, 3, 4.0, 0.0), (PF, 3, 1 / 16, -7.5 / 16),
+                         (KB0, 2, -2048.0, 0.0), (KB1, 2, -2048.0, -65536.0), (AQ, 5, 4.0, 0.0), (D4, 5, 1 / 16, 0.0), (PK, 3, 2048.0, 0.0)):
+        cst.append(do("v", [v_fc], ts(C_(c), F_(src), a, b, A.mult, A.add)))
+    cst.append(do("v", [v_fc], ts(C_(H0), F_(0), F_(1), 0.0, A.subtract, A.add)))
+    cst.append(do("v", [v_fc], ts(C_(H1), F_(0), F_(1), 128.0, A.subtract, A.add)))
+    sst = []
+    for b in range(4):
+        t, h = divmod(b, 2)
+        sst.append(do("v", [v_ss, v_one, v_fc], ts(T.SS[:, 256 * t + b:256 * t + 256:4], T.ones[:, 0:64], F_(1), None, A.mult)))
+        sst.append(do("v", [cst[-2 + h]], ts(T.SS[:, 512 + 256 * t + b:768 + 256 * t:4], T.ones[:, 0:64], C_(H0 + h), None, A.mult)))
+    v_qs = do("v", sst, quant(T.qS[:], T.sS[:], T.SS[:]))
+
+    K = {}
+
+    def late_iotas():
+        K["io32"] = do("gc", [], iota(T.io32[:], [[0, 2], [1, 16]]))
+        K["OE"] = do("gc", [], iota(T.OE[:], [[1, 3], [64, 2]]))
+        K["io8"] = do("gc", [], iota(T.io8[:], [[0, 2], [16, 4]]))
+        K["pl"] = do("gc", [], iota(T.plrow[:], [[0, 2], [1, 256]]))
+        K["ur"] = do("gc", [], iota(T.urow[:], [[16, 16], [0, 2], [1, 16]]))
+
+    def late_consts():
+        K["sel"] = do("v", [K["io8"]], ts(T.sel[:], T.io8[:, 0:4], F_(6), None, A.is_equal))
+        K["DG"] = do("v", [K["io32"]], ts(T.DG[:], T.io32[:], F_(1), None, A.is_equal))
+        K["F"] = [do("v", [], fill(B("F", t)[:, 0:512], 0.0)) for t in range(ROUNDS)]
+        si = [do("v", [], fill(T.SI[:], 0.0))]
+        for n, (a, b) in enumerate(((0, 128), (0, 64), (64, 128))):
+            for d, val in enumerate((1.0, 16.0, 64.0)):
+                si.append(do("v", [si[0]], fill(T.SI[a:b, 512 * n + d:512 * n + 512:4], val)))
+        K["qI"] = do("v", si, quant(T.qI[:], T.sI[:], T.SI[:]))
+
+    def later_consts():
+        K["nz"] = [do("v", [d_nz], quant(B("SW", t)[:, 512:768], B("SWs", t)[:, 512:768], T.t_nz[:])) for t in range(ROUNDS)]
+        K["kk8"] = do("v", [K["io8"]], ts(T.kk8[:], T.io8[:], F_(1), None, A.add))
+        K["VO"] = [do("v", [K["DG"]], ts(T.VO[:, 32 * s:32 * s + 32], T.DG[:], 8.0 + s, None, A.mult)) for s in range(3)]
+        K["RC"] = do("v", [i_kn], ts(T.RC[:], T.Kn[:], 256.0, None, A.add))
+        K["Q4"] = [do("v", [], fill(T.cc[:, 12 + s:13 + s], 256.0 * q)) for s, q in enumerate(others + [rank])]
+        K["NEW"] = do("v", [], fill(B("NEW", 0)[:, 256:512], 0.0))
+        for t in range(ROUNDS):
+            K["U%d" % t] = [do("s", [K["ur"]], act(B(n, t)[:, 0:512], T.urow[:], AF.Copy)) for n in ("UL", "UX")]
+        ee = do("v", [], fill(T.EE[:], 0.0))
+        idt = do("v", [], ts(T.idt[:], T.dif[:, 0:128], 0.0, 0.5, A.is_equal, A.mult))
+        e = [do("v", [ee, idt], cp(T.EE[:, 512 * b + b:512 * b + 512:4], T.idt[:])) for b in range(4)]
+        K["qE"] = do("v", e, quant(T.qE[:], T.sE[:], T.EE[:]))
+        K["qW"] = do("v", [d_w], quant(T.qW[:], T.sW[:], T.t_w[:]))
+
+    st = {"prev": []}
+
+    def copies(t, lt, xt):
+        SW, SWs = B("SW", t), B("SWs", t)
+        r = {"L": [], "X": [], "W": []}
+        for dn, c0, c1, dep, key in (("LW", 0, 256, lt, "W"), ("LW", 256, 512, xt, "W"), ("XW", 256, 512, xt, "X"), ("LN", 0, 256, lt, "L")):
+            o = c0 if dn == "LW" else 0
+            r[key].append(dma("y", [dep], B(dn, t)[:, o:o + 256].bitcast(U8), SW[:, c0:c1].bitcast(U8)))
+            r[key].append(dma("y", [dep], B(dn + "s", t)[:, o:o + 256], SWs[:, c0:c1]))
+        return r
+
+    def order_and_send(t, lt, xt, pc):
+        SW, SWs, sC, Vc, yd, DD, rk, H = (B(n, t) for n in ("SW", "SWs", "sC", "Vc", "yd", "DD", "rk", "H"))
+        pr = st["prev"]
+        cols, rows, dg = [], [], []
+        for ty, tk in ((0, lt), (1, xt)):
+            qu, su = T.qU[:, 128 * ty:128 * ty + 128], T.sU[:, 128 * ty:128 * ty + 128]
+            for h in range(2):
+                c = 256 * ty + 128 * h
+                m = do("p", [q_u, tk, pc], mm(T.pC[:, 512 * (2 * ty + h):512 * (2 * ty + h) + 128], SW[:, c:c + 128], SWs[:, c:c + 128], qu, su))
+            cols.append(m)
+            rows.append(do("p", [], mm((T.pA, T.pB)[ty][:, 0:256], qu, su, SW[:, 256 * ty:256 * ty + 256], SWs[:, 256 * ty:256 * ty + 256])))
+        sct, rwt = [], []
+        for ty in range(2):
+            ca = do("s", [cols[ty], pr], act(sC[:, 2 * ty:2 * ty + 2], T.pC[:, 1024 * ty:1024 * ty + 1024:512], AF.Abs))
+            ra = do("s", [rows[ty]], act(Vc[:, 256 * ty:256 * ty + 256], (T.pA, T.pB)[ty][:, 0:256], AF.Abs))
+            ys = [do("s", [ca, ra], act(yd[:, 256 * ty + 128 * h:256 * ty + 128 * h + 128], Vc[:, 256 * ty + 128 * h:256 * ty + 128 * h + 128],
+                                        AF.Identity, bias=sC[:, 2 * ty + h:2 * ty + h + 1], scale=-1.0)) for h in range(2)]
+            sct.append(ca)
+            rwt.append(ra)
+            o = 512 * ty
+            f0, f1, f2 = ((A.is_lt, A.is_le, A.is_gt), (A.is_gt, A.is_ge, A.is_lt))[ty]
+            a = do("v", [ca, ra, pr], ts(DD[:, o:o + 128], Vc[:, 256 * ty + 128:256 * ty + 256], sC[:, 2 * ty:2 * ty + 1], None, f0))
+            b = do("v", [ca, ra], ts(DD[:, o + 384:o + 512], Vc[:, 256 * ty:256 * ty + 128], sC[:, 2 * ty + 1:2 * ty + 2], None, f1))
+            d = do("v", [ys, v_mt], tt(DD[:, o + 128:o + 384], yd[:, 256 * ty:256 * ty + 256], (T.Mneg, T.Mtri)[ty][:], f2))
+            dg.append([a, b, d])
+        rks = []
+        for ty in range(2):
+            o = 512 * ty
+            r0 = do("s", dg[ty], act(DD[:, o:o + 256], DD[:, o:o + 256], AF.Identity, accum_out=rk[:, 2 * ty:2 * ty + 1]))
+            r1 = do("v", dg[ty], red(rk[:, 2 * ty + 1:2 * ty + 2], DD[:, o + 256:o + 512]))
+            rks.append([r0, r1])
+        hs = [do("v", [rks[b // 2][b % 2], i_kn, pr], ts(H[:, b:512:4], T.Kn[:], rk[:, b:b + 1], None, A.is_equal)) for b in (1, 0, 3, 2)]
+        qh = do("v", hs, quant(B("qH", t)[:], B("sH", t)[:], H[:]))
+        do("p", [qh, v_qs, pr], mm(T.pD[:, 0:128], T.qS[:, 0:128], T.sS[:, 0:128], B("qH", t)[:], B("sH", t)[:], True, False))
+        m = do("p", [], mm(T.pD[:, 0:128], T.qS[:, 128:256], T.sS[:, 128:256], B("qH", t)[:], B("sH", t)[:], False, True))
+        trA, lo, G, trG = B("trA", t), B("lo16", t), B("Gs", t), B("trG", t)
+        a = do("v", [m], trn(trA[:], T.pD[:, 0:128]))
+        of = do("v", [a, cst], ts(lo[:, 0:4], trA[:, 0:128:32], C_(AQ), None, A.add))
+        gs = do("v", [of, rwt, pr], cp(G[:, 0:64], Vc[:, 0:512].indirect(lo[:, 0:4])))
+        tg = do("v", [gs], trn(trG[:, 0:64], G[:, 0:64]))
+        mt = do("v", [tg], ts(B("M", t)[:], trG[:, 0:64:32], C_(SG), None, A.mult))
+        send([mt], "aM%d" % t, B("M", t)[:], lambda s: B("landM", t)[:, 2 * s:2 * s + 2])
+        return {"trA": a, "of": of, "M": mt, "pC": sct, "rows": rwt}
+
+    def prepare(t, k):
+        M, own, wk, dg, VT, trA, G, trG, lo = (B(n, t) for n in ("M", "own", "wk", "dg", "VT", "trA", "Gs", "trG", "lo16"))
+        gp = do("v", [k["of"], K["pl"]], cp(G[:, 64:128], T.plrow[:, 0:512].indirect(lo[:, 0:4])))
+        a = do("v", [k["M"], cst], ts(own[:, 1:2], M[:, 1:2], C_(M1), None, A.mult))
+        x0 = do("v", [k["M"], v_one], ts(B("XR", t)[:, 192:224], T.ones[:, 0:32], M[:, 0:1], None, A.mult))
+        x1 = do("v", [], ts(B("XR", t)[:, 224:256], T.ones[:, 0:32], M[:, 1:2], None, A.mult))
+        tp = do("v", [gp], trn(trG[:, 64:128], G[:, 64:128]))
+        w = do("v", [k["trA"], K["sel"]], tt(wk[:], trA[:, 0:128:32], T.sel[:], A.mult))
+        k["MP"] = do("v", [tp], cp(B("MP", t)[:], trG[:, 64:128:32]))
+        send([k["MP"]], "aP%d" % t, B("MP", t)[:], lambda s: B("landP", t)[:, 2 * s:2 * s + 2])
+        k["s"] = do("v", [a], ts(own[:, 0:1], M[:, 0:1], C_(M0), own[:, 1:2], A.mult, A.add))
+        pl = do("v", [w], red(dg[:, 0:1], wk[:]))
+        k["Ro"] = do("v", [x0, x1], trn(B("R", t)[:, 192:256], B("XR", t)[:, 192:256]))
+        hi = do("v", [pl], ts(B("iw", t)[:, 20:21], dg[:, 0:1], 1 / 16, -7.5 / 16, A.mult, A.add))
+        v2 = do("v", [K["DG"]], ts(VT[:, 64:96], T.DG[:], C_(D4), None, A.mult))
+        hf = do("v", [hi], cp(dg[:, 1:2], B("iw", t)[:, 20:21]))
+        v1 = do("v", [hf], ts(VT[:, 32:64], T.DG[:], dg[:, 1:2], None, A.mult))
+        lo_ = do("v", [hf], ts(dg[:, 2:3], dg[:, 1:2], -16.0, dg[:, 0:1], A.mult, A.add))
+        v0 = do("v", [lo_], ts(VT[:, 0:32], T.DG[:], dg[:, 2:3], None, A.mult))
+        k["VT"] = [v0, v1, v2]
+        k["pl"] = pl
+
+    def merge_and_send(t, k):
+        LM, XR, R, Dc, cn, pw, lo, own, F = (B(n, t) for n in ("landM", "XR", "R", "Dc", "cn", "pw", "lo16", "own", "F"))
+        aM = ("aM%d" % t, arrive)
+        xs = []
+        for j in range(6):
+            if j % 2 == 0:
+                xs.append(do("v", [aM], ts(XR[:, 32 * j:32 * j + 32], T.ones[:, 0:32], LM[:, j:j + 1], None, A.mult)))
+            else:
+                xs.append(do("s", [aM, v_zer], act(XR[:, 32 * j:32 * j + 32], T.zer[:, 0:32], AF.Identity, bias=LM[:, j:j + 1])))
+        r = do("v", xs, trn(R[:, 0:192], XR[:, 0:192]))
+        k["R"] = r
+        d, e = [], 64 * rank
+        for a, b, op in ((0, e, A.is_le), (e, 192, A.is_lt)):
+            if b > a:
+                d.append(do("v", [r, k["s"], st["prev"]], ts(Dc[:, a:b], R[:, a:b], own[:, 0:1], None, op)))
+        c = do("v", d, red(cn[:, 3:4], Dc[:, 0:192]))
+        k["cn"] = c
+        fl = do("v", [c], ts(B("iw", t)[:, 21:22], cn[:, 3:4], 1 / 16, C_(PF), A.mult, A.add))
+        p4 = do("v", [c], ts(pw[:, 0:1], cn[:, 3:4], 4.0, C_(P4), A.mult, A.add))
+        n4 = do("v", [fl, p4], ts(pw[:, 1:2], B("iw", t)[:, 21:22], 64.0, pw[:, 0:1], A.mult, A.add))
+        of = do("v", [n4, K["OE"]], ts(lo[:, 4:10], T.OE[:], pw[:, 1:2], None, A.add))
+        sc = do("v", [of, k["VT"], K["F"]], cp(F[:, 0:2048].indirect(lo[:, 4:10]), B("VT", t)[:]))
+        k["qF"] = do("v", [sc], quant(B("qF", t)[:], B("sF", t)[:], F[:, 0:512]))
+        m = do("p", [k["qF"], K["qI"], st["prev"]], mm(T.pE[:, 0:128], T.qI[:, 0:128], T.sI[:, 0:128], B("qF", t)[:], B("sF", t)[:]))
+        a = do("v", [m], trn(B("tr2", t)[:, 0:128], T.pE[:, 0:128]))
+        of = do("v", [a], cp(lo[:, 10:14], B("tr2", t)[:, 0:128:32]))
+        k["pE"] = [a, of]
+        pd = [of, K["nz"][t], k["lt"], k["xt"]]
+        ps = do("v", pd, cp(B("PS", t)[:].bitcast(U32), B("SW", t)[:, 0:768].bitcast(U32).indirect(lo[:, 10:14])))
+        pss = do("s", pd, act(B("PSs", t)[:], B("SWs", t)[:, 0:768].indirect(lo[:, 10:14]), AF.Copy))
+        LW, LWs = B("LW", t), B("LWs", t)
+        send([ps], "aC%d" % t, B("PS", t)[:, 0:64].bitcast(U8), lambda s: LW[:, 512 + 64 * s:576 + 64 * s].bitcast(U8))
+        send([pss], "aC%d" % t, B("PSs", t)[:, 0:64], lambda s: LWs[:, 512 + 64 * s:576 + 64 * s])
+
+    def lists(t, k):
+        LM, R, Dc, cn, pw, ow, lo, F, iw, ix, tr2 = (B(n, t) for n in ("landM", "R", "Dc", "cn", "pw", "ow", "lo16", "F", "iw", "ix", "tr2"))
+        aM = ("aM%d" % t, arrive)
+        a = do("v", [aM], ts(ow[:, 0:3], LM[:, 0:6:2], C_(M0), None, A.mult))
+        b = do("v", [aM], ts(ow[:, 4:7], LM[:, 1:6:2], C_(M1), None, A.mult))
+        s3 = do("v", [a, b], tt(ow[:, 8:11], ow[:, 0:3], ow[:, 4:7], A.add))
+        acc = []
+        for s, q in enumerate(others):
+            seg = []
+            for x in [y for y in range(4) if y != s]:
+                op = A.is_le if (others + [rank])[x] < q else A.is_lt
+                if seg and seg[-1][1] == 64 * x and seg[-1][2] == op:
+                    seg[-1][1] += 64
+                else:
+                    seg.append([64 * x, 64 * x + 64, op])
+            at, dd = 256 * s, []
+            for (c0, c1, op) in seg:
+                dd.append(do("v", [s3, k["R"], k["Ro"], k["cn"], st["prev"]], ts(Dc[:, at:at + c1 - c0], R[:, c0:c1], ow[:, 8 + s:9 + s], None, op)))
+                at += c1 - c0
+            acc.append(do("s", dd, act(Dc[:, 256 * s:256 * s + 192], Dc[:, 256 * s:256 * s + 192], AF.Identity, accum_out=cn[:, s:s + 1])))
+        k["cnt"] = acc
+        fl = do("v", acc, ts(iw[:, 0:3], cn[:, 0:3], 1 / 16, C_(PF), A.mult, A.add))
+        p4 = do("v", acc, ts(pw[:, 4:7], cn[:, 0:3], 4.0, C_(P4), A.mult, A.add))
+        f6 = do("v", [fl], ts(pw[:, 8:11], iw[:, 0:3], 64.0, None, A.mult))
+        n4 = do("v", [p4, f6], tt(pw[:, 12:15], pw[:, 4:7], pw[:, 8:11], A.add))
+        of = [do("v", [n4], ts(lo[:, 16 + 2 * s:18 + 2 * s], T.OE[:, 4:6], pw[:, 12 + s:13 + s], None, A.add)) for s in range(3)]
+        sc = do("v", [of, K["VO"], k["qF"]], cp(F[:, 0:2048].indirect(lo[:, 16:22]), T.VO[:]))
+        qg = do("v", [sc], quant(B("qG", t)[:], B("sG", t)[:], F[:, 0:512]))
+        ml = do("p", [qg, k["trA"]], mm(T.pD[:, 0:128], T.qI[:, 128:256], T.sI[:, 128:256], B("qG", t)[:], B("sG", t)[:]))
+        md = do("p", [k["pE"]], mm(T.pE[:, 0:128], T.qI[:, 256:384], T.sI[:, 256:384], B("qG", t)[:], B("sG", t)[:]))
+        a = do("v", [ml, k["pE"]], trn(tr2[:, 0:128], T.pD[:, 0:128]))
+        nl = [do("v", [a], ts(lo[:, 24 + 4 * h:28 + 4 * h], tr2[:, 0:128:32], 255.0, None, A.min)) for h in range(2)]
+        b = do("v", [md], trn(tr2[:, 128:256], T.pE[:, 0:128]))
+        g8 = do("v", [a, b], ts(ix[:, 0:8], tr2[:, 0:256:32], 512.0, None, A.is_ge))
+        k8 = do("v", [g8, K["kk8"]], tt(ix[:, 8:16], ix[:, 0:8], T.kk8[:], A.mult))
+        i8 = do("v", [k8], tt(ix[:, 16:24], tr2[:, 0:256:32], ix[:, 8:16], A.add))
+        k["AB"] = do("v", [i8], cp(lo[:, 32:40], ix[:, 16:24]))
+        nd_ = [nl, K["nz"][t], st["prev"]]
+        k["np"] = [do("v", nd_, cp(B("NP", t)[:].bitcast(U32), B("SW", t)[:, 512:768].bitcast(U32).indirect(lo[:, 24:32]))),
+                   do("s", nd_, act(B("NPs", t)[:], B("SWs", t)[:, 512:768].indirect(lo[:, 24:32]), AF.Copy))]
+        fl = do("v", [i8], ts(iw[:, 8:16], ix[:, 16:24], 1 / 16, -7.5 / 16, A.mult, A.add))
+        f6 = do("v", [fl], ts(ix[:, 0:8], iw[:, 8:16], 16.0, None, A.mult))
+        n8 = do("v", [f6], tt(ix[:, 24:32], ix[:, 0:8], ix[:, 16:24], A.add))
+        k["uo"] = []
+        for x in range(2):
+            for h in range(2):
+                o = 48 + 8 * x
+                k["uo"].append(do("v", [n8], ts(lo[:, o + h:o + 8:2], ix[:, 24 + 4 * x:28 + 4 * x], 16.0 * h - 512.0 * x, None, A.add)))
+        k["dn"] = [do("p", [k["np"], K["qE"], k["pC"]], mm(T.pC[:, 512 * b:512 * b + 128], T.qE[:, 128 * b:128 * b + 128], T.sE[:, 128 * b:128 * b + 128],
+                                                           B("NP", t)[:], B("NPs", t)[:], True, False)) for b in range(4)]
+
+    def update_list(t, k, x):
+        U, tr, lo = B("UX" if x else "UL", t), B("trX" if x else "trU", t), B("lo16", t)
+        sc = do("v", [k["uo"], K["RC"], K["U%d" % t]], cp(U[:, 0:1408].indirect(lo[:, 48 + 8 * x:56 + 8 * x]), T.RC[:]))
+        a = do("v", [sc, st["prev"]], trn(tr[:], U[:, 0:512]))
+        k["ux" if x else "ul"] = do("v", [a], cp(lo[:, 64 + 16 * x:80 + 16 * x], tr[:, 0:512:32]))
+
+    def renew(t, k, oq, os_):
+        LW, LWs, XW, XWs, LN, LNs, NEW, lo = (B(n, t) for n in ("LW", "LWs", "XW", "XWs", "LN", "LNs", "NEW", "lo16"))
+        ad = [("aC%d" % t, 2 * arrive), k["AB"], k["cp"]["W"]]
+        a1 = do("v", ad, cp(XW[:, 256:384].bitcast(U32), LW[:, 0:704].bitcast(U32).indirect(lo[:, 32:40])))
+        a2 = do("s", ad, act(XWs[:, 256:384], LWs[:, 0:704].indirect(lo[:, 32:40]), AF.Copy))
+        dc = [do("p", [a1, a2], mm(T.pC[:, 512 * b:512 * b + 128], T.qE[:, 128 * b:128 * b + 128], T.sE[:, 128 * b:128 * b + 128],
+                                   XW[:, 256:384], XWs[:, 256:384], False, True)) for b in range(4)]
+        update_list(t, k, 1)
+        nw = []
+        for b in range(4):
+            i, o = T.pC[:, 512 * b + 64:512 * b + 128], NEW[:, b:256:4]
+            nw.append(do("v", [dc[b]], cp(o, i)) if b % 2 == 0 else do("s", [dc[b], st["prev"]], act(o, i, AF.Copy)))
+        qn = do("v", [nw, K["NEW"]], quant(LN[:, 256:384], LNs[:, 256:384], NEW[:]))
+        l1 = do("v", [qn, k["ul"], k["cp"]["L"]], cp(oq[:, 0:256].bitcast(U32), LN[:, 0:384].bitcast(U32).indirect(lo[:, 64:80])))
+        l2 = do("s", [qn, k["ul"], k["cp"]["L"]], act(os_[:, 0:256], LNs[:, 0:384].indirect(lo[:, 64:80]), AF.Copy))
+        x1 = do("v", [k["ux"], k["cp"]["X"]], cp(oq[:, 256:512].bitcast(U32), XW[:, 0:384].bitcast(U32).indirect(lo[:, 80:96])))
+        x2 = do("s", [k["ux"], k["cp"]["X"]], act(os_[:, 256:512], XWs[:, 0:384].indirect(lo[:, 80:96]), AF.Copy))
+        return [l1, l2], [x1, x2], nw
+
+    def outlists(t, k):
+        ky, KX, KT, dk, pt, LP, cn = (B(n, t) for n in ("ky", "KX", "KT", "dk", "pt", "landP", "cn"))
+        aP = ("aP%d" % t, arrive)
+        a = do("v", [aP], ts(ky[:, 0:3], LP[:, 0:6:2], C_(M0), None, A.mult))
+        b = do("v", [aP], ts(ky[:, 4:7], LP[:, 1:6:2], C_(M1), None, A.mult))
+        o = do("v", [k["pl"]], cp(ky[:, 3:4], B("dg", t)[:, 0:1]))
+        o2 = do("v", [], fill(ky[:, 7:8], 0.0))
+        c = do("v", [k["cnt"], k["cn"]], ts(ky[:, 8:12], cn[:, 0:4], 2048.0, C_(PK), A.mult, A.add))
+        d = do("v", [a, b, o, o2], tt(ky[:, 12:16], ky[:, 0:4], ky[:, 4:8], A.add))
+        e = do("v", [c, K["Q4"]], tt(ky[:, 16:20], ky[:, 8:12], T.cc[:, 12:16], A.add))
+        f = do("v", [d, e], tt(ky[:, 20:24], ky[:, 12:16], ky[:, 16:20], A.add))
+        x = [do("s", [f, k.get("kx")], act(KX[:, 32 * j:32 * j + 32], T.zer[:, 0:32], AF.Identity, bias=ky[:, 20 + j:21 + j])) for j in range(4)]
+        tr = do("v", x, trn(KT[:], KX[:]))
+        dd = [do("s", [tr, k.get("kx")], act(dk[:, 128 * c:128 * c + 128], KT[:], AF.Abs, bias=C_(KB0 + c))) for c in range(2)]
+        m = [do("v", [dd[c]], red(pt[:, c:c + 1], dk[:, 128 * c:128 * c + 128], A.min)) for c in range(2)]
+        h = [do("v", m, cp(pt[o:o + 32, 4:6], pt[o + 32:o + 64, 0:2])) for o in (0, 64)]
+        n = [do("v", h, tt(pt[o:o + 32, 6:8], pt[o:o + 32, 0:2], pt[o:o + 32, 4:6], A.min)) for o in (0, 64)]
+        for c in range(2):
+            dma("y", n, T.lw[t:t + 1, 32 * c:32 * c + 32], pt[0:32, 6 + c:7 + c])
+            dma("y", n, T.sw[t:t + 1, 32 * c:32 * c + 32], pt[64:96, 6 + c:7 + c])
+        return m
+
+    late_iotas()
+    lt, xt, pc, last, kx = q_l, q_x, None, None, None
+    for t in range(ROUNDS):
+        k = order_and_send(t, lt, xt, pc)
+        k["lt"], k["xt"] = lt, xt
+        k["cp"] = copies(t, lt, xt)
+        if t == 0:
+            late_consts()
+        prepare(t, k)
+        if t == 0:
+            later_consts()
+        else:
+            k["kx"] = outlists(t - 1, last)
+        merge_and_send(t, k)
+        lists(t, k)
+        update_list(t, k, 0)
+        if t + 1 < ROUNDS:
+            oq, os_ = B("SW", t + 1), B("SWs", t + 1)
+        else:
+            oq, os_ = T.FN, T.FNs
+        lt, xt, pc = renew(t, k, oq, os_)
+        st["prev"] = [lt, xt, pc]
+        last = k
+    my = do("p", [lt, K["qW"], last["rows"]], mm(T.pA[:, 0:256], T.qW[:], T.sW[:], T.FN[:, 0:256], T.FNs[:, 0:256]))
+    for o, tk in ((0, lt), (256, xt)):
+        dma("y", tk, T.oc[:, 4 * o:4 * o + 1024], T.FN[:, o:o + 256].bitcast(U8))
+        for q in range(4):
+            dma("y", tk, T.osc[4 * q:4 * q + 4, o:o + 256], T.FNs[32 * q:32 * q + 4, o:o + 256])
+    yc = do("s", [my], act(T.yt[:], T.pA[:, 0:256], AF.Copy))
+    dma("s", [yc], T.y[:], T.yt[:])
+    outlists(ROUNDS - 1, last)
+    for s, n in cnt.items():
+        if top.get(s, 0) < n:
+            g.wait_ge(T.sem[s], n)

@@ -3,53 +3,44 @@ from concourse.mybir import dt, AluOpType as A, AxisListType, ActivationFunction
 
 F8 = "float8_e4m3fn_x4"
 TINY = 2.0 ** -118
+R16, R64 = 1.5 * 2.0 ** 27, 1.5 * 2.0 ** 29
 ROUNDS = 2
+LB, XB = 192, 448
 
 SCRATCH = {
-    "t_lv": ("sbuf", [128, 1024], "bfloat16"), "t_dm": ("sbuf", [128, 1024], "bfloat16"),
-    "t_nz": ("sbuf", [128, 1024], "bfloat16"), "t_w": ("sbuf", [128, 512], "bfloat16"),
-    "u0": ("sbuf", [128, 4], "bfloat16"), "z0": ("sbuf", [128, 4], "bfloat16"),
-    "uz": ("sbuf", [128, 1024], "bfloat16"),
-    "qU": ("sbuf", [128, 256], F8), "sU": ("sbuf", [128, 256], "uint8"),
-    "qW": ("sbuf", [128, 128], F8), "sW": ("sbuf", [128, 128], "uint8"),
-    "ones": ("sbuf", [128, 128], "bfloat16"), "zer": ("sbuf", [128, 128], "bfloat16"),
-    "SS": ("sbuf", [128, 1024], "bfloat16"), "SI": ("sbuf", [128, 1536], "bfloat16"), "EE": ("sbuf", [128, 2048], "bfloat16"),
-    "qS": ("sbuf", [128, 256], F8), "sS": ("sbuf", [128, 256], "uint8"),
-    "qI": ("sbuf", [128, 384], F8), "sI": ("sbuf", [128, 384], "uint8"),
-    "qE": ("sbuf", [128, 512], F8), "sE": ("sbuf", [128, 512], "uint8"),
-    "pI": ("sbuf", [128, 1], "int32"), "ii": ("sbuf", [128, 8], "int32"), "fc": ("sbuf", [128, 8], "float32"),
-    "cc": ("sbuf", [128, 16], "float32"),
-    "dif": ("sbuf", [128, 256], "float32"), "Mneg": ("sbuf", [128, 256], "float32"), "Mtri": ("sbuf", [128, 256], "float32"),
-    "idt": ("sbuf", [128, 128], "bfloat16"),
-    "Kn": ("sbuf", [128, 128], "bfloat16"), "RC": ("sbuf", [128, 128], "float32"), "sel": ("sbuf", [128, 4], "float32"),
-    "io8": ("sbuf", [128, 8], "float32"), "kk8": ("sbuf", [128, 8], "float32"),
-    "io32": ("sbuf", [128, 32], "float32"), "DG": ("sbuf", [128, 32], "bfloat16"),
-    "VO": ("sbuf", [128, 96], "bfloat16"), "OE": ("sbuf", [128, 6], "float32"),
-    "plrow": ("sbuf", [128, 512], "float32"), "urow": ("sbuf", [128, 512], "float32"),
     "pA": ("psum", [128, 512], "float32"), "pB": ("psum", [128, 512], "float32"), "pC": ("psum", [128, 2048], "float32"),
     "pD": ("psum", [128, 512], "float32"), "pE": ("psum", [128, 512], "float32"),
-    "yt": ("sbuf", [128, 256], "float32"),
-    "FN": ("sbuf", [128, 512], F8), "FNs": ("sbuf", [128, 512], "uint8"),
 }
-ONCE = ("yd", "DD", "KX", "KT", "dk", "Dc", "tr2", "trU", "trX", "qH", "sH", "H", "Gs", "trG", "sC", "Vc", "rk", "trA", "wk",
-        "VT", "XR", "R", "pw", "ow", "ix", "own", "NEW", "iw", "lo16", "ky", "qF", "sF", "qG", "sG")
 for _n, _w, _d in (
-        ("SW", 768, F8), ("SWs", 768, "uint8"), ("LW", 704, F8), ("LWs", 704, "uint8"), ("XW", 384, F8), ("XWs", 384, "uint8"),
+        ("t_lv", 1024, "bfloat16"), ("t_dm", 1024, "bfloat16"), ("t_nz", 1024, "bfloat16"), ("t_w", 512, "bfloat16"),
+        ("u0", 4, "bfloat16"), ("z0", 4, "bfloat16"), ("uz", 1024, "bfloat16"), ("qU", 256, F8), ("sU", 256, "uint8"),
+        ("qW", 128, F8), ("sW", 128, "uint8"), ("ones", 512, "bfloat16"), ("zer", 128, "bfloat16"), ("half", 516, "bfloat16"),
+        ("SS", 1024, "bfloat16"), ("SI", 1024, "bfloat16"), ("EM", 516, "bfloat16"), ("qS", 256, F8), ("sS", 256, "uint8"),
+        ("qI", 384, F8), ("sI", 384, "uint8"), ("qE", 512, F8), ("sE", 512, "uint8"), ("NZ", 256, F8), ("NZs", 256, "uint8"),
+        ("pI", 1, "int32"), ("ii", 8, "int32"), ("fc", 8, "float32"), ("cc", 16, "float32"),
+        ("tin", 256, "float32"), ("Mneg", 256, "float32"), ("Mtri", 256, "float32"), ("Kn", 128, "bfloat16"), ("RC", 128, "float32"),
+        ("sel", 4, "float32"), ("io8", 8, "float32"), ("kk8", 8, "float32"), ("io32", 32, "float32"), ("DG", 32, "bfloat16"),
+        ("sgt", 32, "float32"), ("VO", 64, "bfloat16"), ("OE", 6, "float32"), ("BS", 2, "float32"), ("urow", 512, "float32"),
+        ("yt", 256, "float32"), ("FN", 512, F8), ("FNs", 512, "uint8")):
+    SCRATCH[_n] = ("sbuf", [128, _w], _d)
+ONCE = ("yd", "DD", "Dc", "tr2", "trU", "trX", "qH", "sH", "H", "Gs", "sC", "Vc", "rk", "trA", "wk",
+        "VT", "XR", "R", "pw", "ow", "ix", "own", "NEW", "iw", "lo16", "qF", "sF", "qG", "sG")
+for _n, _w, _d in (
+        ("SW", 704, F8), ("SWs", 704, "uint8"), ("LW", 704, F8), ("LWs", 704, "uint8"), ("XW", 384, F8), ("XWs", 384, "uint8"),
         ("LN", 384, F8), ("LNs", 384, "uint8"), ("PS", 64, F8), ("PSs", 64, "uint8"), ("NP", 128, F8), ("NPs", 128, "uint8"),
         ("qH", 128, F8), ("sH", 128, "uint8"), ("qF", 128, F8), ("sF", 128, "uint8"), ("qG", 128, F8), ("sG", 128, "uint8"),
         ("H", 512, "bfloat16"), ("F", 2048, "bfloat16"), ("NEW", 512, "bfloat16"), ("VT", 96, "bfloat16"),
         ("sC", 4, "float32"), ("Vc", 512, "float32"), ("yd", 512, "float32"), ("DD", 1024, "bfloat16"), ("rk", 4, "float32"),
-        ("trA", 128, "float32"), ("Gs", 128, "float32"), ("trG", 128, "float32"), ("M", 2, "float32"), ("MP", 2, "float32"),
-        ("dg", 8, "float32"), ("wk", 4, "float32"), ("own", 4, "float32"),
-        ("landM", 6, "float32"), ("landP", 6, "float32"), ("XR", 256, "float32"), ("R", 256, "float32"),
-        ("Dc", 768, "bfloat16"), ("cn", 4, "float32"), ("pw", 32, "float32"), ("ow", 16, "float32"),
-        ("tr2", 256, "float32"), ("ix", 32, "float32"), ("UL", 1408, "float32"), ("UX", 1408, "float32"),
-        ("trU", 512, "float32"), ("trX", 512, "float32"), ("lo16", 192, "uint16"), ("iw", 24, "int32"),
-        ("ky", 32, "float32"), ("KX", 128, "float32"), ("KT", 128, "float32"), ("dk", 256, "float32"), ("pt", 8, "float32")):
+        ("trA", 128, "float32"), ("Gs", 64, "float32"), ("trG", 64, "float32"), ("dg", 4, "float32"), ("wk", 5, "float32"),
+        ("own", 2, "float32"), ("landM", 6, "float32"), ("landP", 6, "float32"), ("XR", 256, "float32"), ("R", 256, "float32"),
+        ("Dc", 832, "bfloat16"), ("cn", 4, "float32"), ("pw", 8, "float32"), ("ow", 16, "float32"),
+        ("tr2", 256, "float32"), ("ix", 40, "float32"), ("UL", 896, "float32"), ("UX", 1408, "float32"),
+        ("trU", 512, "float32"), ("trX", 512, "float32"), ("lo16", 128, "uint16"), ("iw", 8, "int32"),
+        ("wl", 8, "float32"), ("fo", 4, "float32")):
     for _t in range(1 if _n in ONCE else ROUNDS):
         SCRATCH[_n + str(_t)] = ("sbuf", [128, _w], _d)
 
-SEMAPHORES = ["v", "s", "p", "gc", "ls"] + ["d%d" % k for k in range(60)] + \
+SEMAPHORES = ["v", "s", "p", "gc", "ls"] + ["d%d" % k for k in range(80)] + \
     [n + str(t) for n in ("aM", "aP", "aC") for t in range(ROUNDS)]
 
 
@@ -125,11 +116,11 @@ def rank_program(g, core, T, topo):
     def cp(o, i):
         return lambda q: q.tensor_copy(o, i)
 
-    def act(o, i, fn, **k):
+    def act(o, i, fn=AF.Identity, **k):
         return lambda q: q.activation(o, i, fn, **k)
 
-    def red(o, i, op=A.add):
-        return lambda q: q.tensor_reduce(o, i, AxisListType.X, op)
+    def red(o, i):
+        return lambda q: q.tensor_reduce(o, i, AxisListType.X, A.add)
 
     def trn(o, i):
         return lambda q: q.transpose(o, i)
@@ -148,327 +139,329 @@ def rank_program(g, core, T, topo):
 
     U8, U32 = dt.uint8, dt.uint32
 
-    d_lv = dma("y", [], T.t_lv[:], T.lv[:])
     d_u = dma("s", [], T.u0[:], T.u[:, 0:4])
     d_z = dma("s", [], T.z0[:], T.z[:, 0:4])
+    d_lv = dma("y", [], T.t_lv[:], T.lv[:])
     d_dm = dma("y", [], T.t_dm[:], T.dm[:])
     d_nz = dma("y", [], T.t_nz[:], T.nz[:])
     d_w = dma("y", [], T.t_w[:], T.w[:])
 
+    K = {}
     i_p = do("gc", [], lambda q: q.iota(T.pI[:], [[0, 1]], 0, 1))
-    i_df = do("gc", [], iota(T.dif[:], [[0, 2], [-1, 128]], 0, 1))
-    i_kn = do("gc", [], iota(T.Kn[:], [[16, 4], [0, 2], [1, 16]]))
-    v_one = do("v", [], fill(T.ones[:], 1.0))
     v_zer = do("v", [], fill(T.zer[:], 0.0))
-    v_ss = do("v", [], fill(T.SS[:], 0.0))
+    v_tin = do("v", [], fill(T.tin[:], TINY))
     bits = []
-    for c, m in enumerate((127, 15, 31, 63, 32, 64, 48, 127)):
+    for c, m in enumerate((15, 32, 64, 63, 48, 112)):
         bits.append(do("v", [i_p], ts(T.ii[:, c:c + 1], T.pI[:, 0:1], m, None, A.bitwise_and)))
-    v_fc = do("v", bits, cp(T.fc[:], T.ii[:]))
+    v_fc = do("v", bits, cp(T.fc[:, 0:6], T.ii[:, 0:6]))
+    v_one = do("v", [], fill(T.ones[:], 1.0))
+    v_ss = do("v", [], fill(T.SS[:], 0.0))
+    v_half = do("v", [], fill(T.half[:], 0.5))
+    i_mn = do("gc", [v_tin], lambda q: q.affine_select(T.Mneg[:], T.tin[:], [[0, 2], [1, 128]], A.is_ge, -TINY, 0, -1))
+    i_mt = do("gc", [v_tin], lambda q: q.affine_select(T.Mtri[:], T.tin[:], [[0, 2], [-1, 128]], A.is_gt, -TINY, 0, 1))
+    i_kn = do("gc", [], iota(T.Kn[:], [[16, 4], [0, 2], [1, 16]]))
+    K["io32"] = do("gc", [], iota(T.io32[:], [[0, 2], [1, 16]]))
+    K["io8"] = do("gc", [], iota(T.io8[:], [[0, 2], [16, 4]]))
+    K["OE"] = do("gc", [], iota(T.OE[:], [[1, 3], [64, 2]], 30))
+    K["EM"] = do("gc", [v_half], lambda q: q.affine_select(T.EM[:], T.half[:], [[1, 516]], A.is_equal, 0.0, -3, -4))
+    K["RC"] = do("gc", [], iota(T.RC[:], [[16, 4], [0, 2], [1, 16]], 256))
+    K["ur"] = do("gc", [], iota(T.urow[:], [[16, 16], [0, 2], [1, 16]]))
+    for t in range(ROUNDS):
+        K["U%d" % t] = [dma("y", [K["ur"]], B("UL", t)[:, 384:896], T.urow[:]), dma("y", [K["ur"]], B("UX", t)[:, 896:1408], T.urow[:])]
     F_ = lambda c: T.fc[:, c:c + 1]
     C_ = lambda c: T.cc[:, c:c + 1]
-    SG, M1, M0, P4, PF, KB0, KB1, AQ, D4, H0, H1, PK = range(12)
-    v_m1 = do("v", [i_df], ts(T.Mtri[:], T.dif[:], 0.0, 2 * TINY, A.is_gt, A.mult))
-    v_mn = do("v", [v_m1], ts(T.Mneg[:], T.Mtri[:], -1.0, TINY, A.mult, A.add))
-    v_mt = do("v", [v_mn], ts(T.Mtri[:], T.Mneg[:], -1.0, None, A.mult))
+    SG, M1, M0, SM1, SM0, AQ, CD, H1, ML, MD = range(10)
 
     SW0, SWs0 = B("SW", 0), B("SWs", 0)
-    uz = []
+    uz, cst = [], []
+    for c, src, a, b in ((H1, 5, 1.0, 128.0), (AQ, 2, 4.0, 0.0), (SG, 2, -1 / 32, 1.0)):
+        cst.append(do("s", [v_fc], act(C_(c), F_(src), scale=a, bias=b)))
     for b in range(4):
-        uz.append(do("v", [d_u, v_one], ts(T.uz[:, b:512:4], T.ones[:], T.u0[:, b:b + 1], None, A.mult)))
+        uz.append(do("v", [d_u, v_one], ts(T.uz[:, b:512:4], T.ones[:, 0:128], T.u0[:, b:b + 1], None, A.mult)))
     for b in range(4):
-        uz.append(do("s", [d_z, v_zer], act(T.uz[:, 512 + b:1024:4], T.zer[:], AF.Identity, bias=T.z0[:, b:b + 1])))
+        uz.append(do("s", [d_z, v_zer], act(T.uz[:, 512 + b:1024:4], T.zer[:], bias=T.z0[:, b:b + 1])))
     q_u = do("v", uz, quant(T.qU[:], T.sU[:], T.uz[:]))
-    q_l = do("v", [d_lv], quant(SW0[:, 0:256], SWs0[:, 0:256], T.t_lv[:]))
-    q_x = do("v", [d_dm], quant(SW0[:, 256:512], SWs0[:, 256:512], T.t_dm[:]))
-
-    cst = []
-    for c, src, a, b in ((SG, 5, -1 / 32, 1.0), (M1, 4, 1 / 32, 0.0), (M0, 4, -1 / 32, 1.0), (P4, 3, 4.0, 0.0), (PF, 3, 1 / 16, -7.5 / 16),
-                         (KB0, 2, -2048.0, 0.0), (KB1, 2, -2048.0, -65536.0), (AQ, 5, 4.0, 0.0), (D4, 5, 1 / 16, 0.0), (PK, 3, 2048.0, 0.0)):
-        cst.append(do("v", [v_fc], ts(C_(c), F_(src), a, b, A.mult, A.add)))
-    cst.append(do("v", [v_fc], ts(C_(H0), F_(0), F_(1), 0.0, A.subtract, A.add)))
-    cst.append(do("v", [v_fc], ts(C_(H1), F_(0), F_(1), 128.0, A.subtract, A.add)))
+    q_l = do("v", [d_lv], quant(SW0[:, LB:XB], SWs0[:, LB:XB], T.t_lv[:]))
+    q_x = do("v", [d_dm], quant(SW0[:, XB:704], SWs0[:, XB:704], T.t_dm[:]))
     sst = []
     for b in range(4):
         t, h = divmod(b, 2)
-        sst.append(do("v", [v_ss, v_one, v_fc], ts(T.SS[:, 256 * t + b:256 * t + 256:4], T.ones[:, 0:64], F_(1), None, A.mult)))
-        sst.append(do("v", [cst[-2 + h]], ts(T.SS[:, 512 + 256 * t + b:768 + 256 * t:4], T.ones[:, 0:64], C_(H0 + h), None, A.mult)))
+        hi = C_(H1) if h else F_(5)
+        sst.append(do("s", [v_ss, v_one, v_fc], act(T.SS[:, 256 * t + b:256 * t + 256:4], T.ones[:, 0:64], AF.Copy, scale=F_(0))))
+        sst.append(do("s", [cst], act(T.SS[:, 512 + 256 * t + b:768 + 256 * t:4], T.ones[:, 0:64], AF.Copy, scale=hi)))
+    K["DG"] = do("v", [K["io32"], v_fc], ts(T.DG[:], T.io32[:], F_(0), None, A.is_equal))
+    K["sel"] = do("v", [K["io8"]], ts(T.sel[:], T.io8[:, 0:4], F_(4), None, A.is_equal))
+    K["F"] = [do("v", [], fill(B("F", 0)[:, 0:512], 0.0))]
+    qi = [do("v", [v_one], quant(T.qI[:, 0:128], T.sI[:, 0:128], T.ones[:]))]
     v_qs = do("v", sst, quant(T.qS[:], T.sS[:], T.SS[:]))
 
-    K = {}
+    def consts_s():
+        for c, src, a, b in ((M1, 1, 1 / 32, 0.0), (M0, 1, -1 / 32, 1.0), (CD, 2, 4.0, float(LB)), (ML, 2, -1 / 64, 1.0), (MD, 2, 1 / 64, 0.0)):
+            cst.append(do("s", [v_fc], act(C_(c), F_(src), scale=a, bias=b)))
+        cst.append(do("s", [cst], act(C_(SM1), C_(M1), scale=C_(SG))))
+        cst.append(do("s", [], act(C_(SM0), C_(M0), scale=C_(SG))))
+        K["sgt"] = do("s", [v_one], act(T.sgt[:], T.ones[:, 0:32], AF.Copy, scale=C_(SG)))
+        Dc = B("Dc", 0)
+        K["Dc"] = [do("s", [], act(Dc[:, 208 * j + 192:208 * j + 193], F_(3), scale=4.0, bias=-30.0)) for j in (0, 1, 3)]
+        K["SI"] = [do("s", [cst], act(T.SI[:, 512 * j:512 * j + 512], T.ones[:], AF.Copy, scale=C_(ML + j))) for j in range(2)]
+        K["wk"] = do("v", [], fill(B("wk", 0)[:, 4:5], -7.5))
+        K["VTc"] = do("v", [K["DG"], cst], ts(B("VT", 0)[:, 64:96], T.DG[:], C_(CD), None, A.mult))
 
-    def late_iotas():
-        K["io32"] = do("gc", [], iota(T.io32[:], [[0, 2], [1, 16]]))
-        K["OE"] = do("gc", [], iota(T.OE[:], [[1, 3], [64, 2]]))
-        K["io8"] = do("gc", [], iota(T.io8[:], [[0, 2], [16, 4]]))
-        K["pl"] = do("gc", [], iota(T.plrow[:], [[0, 2], [1, 256]]))
-        K["ur"] = do("gc", [], iota(T.urow[:], [[16, 16], [0, 2], [1, 16]]))
-
-    def late_consts():
-        K["sel"] = do("v", [K["io8"]], ts(T.sel[:], T.io8[:, 0:4], F_(6), None, A.is_equal))
-        K["DG"] = do("v", [K["io32"]], ts(T.DG[:], T.io32[:], F_(1), None, A.is_equal))
-        K["F"] = [do("v", [], fill(B("F", t)[:, 0:512], 0.0)) for t in range(ROUNDS)]
-        si = [do("v", [], fill(T.SI[:], 0.0))]
-        for n, (a, b) in enumerate(((0, 128), (0, 64), (64, 128))):
-            for d, val in enumerate((1.0, 16.0, 64.0)):
-                si.append(do("v", [si[0]], fill(T.SI[a:b, 512 * n + d:512 * n + 512:4], val)))
-        K["qI"] = do("v", si, quant(T.qI[:], T.sI[:], T.SI[:]))
-
-    def later_consts():
-        K["nz"] = [do("v", [d_nz], quant(B("SW", t)[:, 512:768], B("SWs", t)[:, 512:768], T.t_nz[:])) for t in range(ROUNDS)]
-        K["kk8"] = do("v", [K["io8"]], ts(T.kk8[:], T.io8[:], F_(1), None, A.add))
-        K["VO"] = [do("v", [K["DG"]], ts(T.VO[:, 32 * s:32 * s + 32], T.DG[:], 8.0 + s, None, A.mult)) for s in range(3)]
-        K["RC"] = do("v", [i_kn], ts(T.RC[:], T.Kn[:], 256.0, None, A.add))
-        K["Q4"] = [do("v", [], fill(T.cc[:, 12 + s:13 + s], 256.0 * q)) for s, q in enumerate(others + [rank])]
+    def consts_v():
+        qi.append(do("v", [K["SI"]], quant(T.qI[:, 128:384], T.sI[:, 128:384], T.SI[:])))
+        K["VO"] = [do("v", [K["DG"]], ts(T.VO[:, 32 * s:32 * s + 32], T.DG[:], 64.0 * (s + 1), None, A.mult)) for s in range(2)]
+        K["nz"] = do("v", [d_nz], quant(T.NZ[:], T.NZs[:], T.t_nz[:]))
+        K["kk8"] = do("v", [K["io8"]], ts(T.kk8[:], T.io8[:], F_(0), None, A.add))
+        K["BS"] = [do("v", [], fill(T.BS[:, j:j + 1], 256.0 * rank - (LB, XB)[j])) for j in range(2)]
+        K["qE"] = [do("v", [K["EM"]], quant(T.qE[:, 128 * b:128 * b + 128], T.sE[:, 128 * b:128 * b + 128], T.EM[:, 3 - b:515 - b])) for b in range(4)]
+        K["np"] = [do("v", [d_nz], quant(B("NP", 0)[:], B("NPs", 0)[:], T.t_nz[:, 0:512]))]
         K["NEW"] = do("v", [], fill(B("NEW", 0)[:, 256:512], 0.0))
-        for t in range(ROUNDS):
-            K["U%d" % t] = [do("s", [K["ur"]], act(B(n, t)[:, 0:512], T.urow[:], AF.Copy)) for n in ("UL", "UX")]
-        ee = do("v", [], fill(T.EE[:], 0.0))
-        idt = do("v", [], ts(T.idt[:], T.dif[:, 0:128], 0.0, 0.5, A.is_equal, A.mult))
-        e = [do("v", [ee, idt], cp(T.EE[:, 512 * b + b:512 * b + 512:4], T.idt[:])) for b in range(4)]
-        K["qE"] = do("v", e, quant(T.qE[:], T.sE[:], T.EE[:]))
+
+    def consts_2():
+        K["F"].append(do("v", [], fill(B("F", 1)[:, 0:512], 0.0)))
         K["qW"] = do("v", [d_w], quant(T.qW[:], T.sW[:], T.t_w[:]))
+        K["np"].append(do("v", [d_nz], quant(B("NP", 1)[:], B("NPs", 1)[:], T.t_nz[:, 0:512])))
 
     st = {"prev": []}
 
-    def copies(t, lt, xt):
+    def copies(t, x, dep, r):
         SW, SWs = B("SW", t), B("SWs", t)
-        r = {"L": [], "X": [], "W": []}
-        for dn, c0, c1, dep, key in (("LW", 0, 256, lt, "W"), ("LW", 256, 512, xt, "W"), ("XW", 256, 512, xt, "X"), ("LN", 0, 256, lt, "L")):
-            o = c0 if dn == "LW" else 0
-            r[key].append(dma("y", [dep], B(dn, t)[:, o:o + 256].bitcast(U8), SW[:, c0:c1].bitcast(U8)))
-            r[key].append(dma("y", [dep], B(dn + "s", t)[:, o:o + 256], SWs[:, c0:c1]))
-        return r
+        c0 = XB if x else LB
+        for dn, o, key in ((("XW", 0, "X"), ("LW", XB, "W")) if x else (("LN", 0, "L"), ("LW", LB, "W"))):
+            r.setdefault(key, []).append(dma("y", [dep], B(dn, t)[:, o:o + 256].bitcast(U8), SW[:, c0:c0 + 256].bitcast(U8)))
+            r[key].append(dma("y", [dep], B(dn + "s", t)[:, o:o + 256], SWs[:, c0:c0 + 256]))
 
-    def order_and_send(t, lt, xt, pc):
-        SW, SWs, sC, Vc, yd, DD, rk, H = (B(n, t) for n in ("SW", "SWs", "sC", "Vc", "yd", "DD", "rk", "H"))
-        pr = st["prev"]
-        cols, rows, dg = [], [], []
-        for ty, tk in ((0, lt), (1, xt)):
-            qu, su = T.qU[:, 128 * ty:128 * ty + 128], T.sU[:, 128 * ty:128 * ty + 128]
-            for h in range(2):
-                c = 256 * ty + 128 * h
-                m = do("p", [q_u, tk, pc], mm(T.pC[:, 512 * (2 * ty + h):512 * (2 * ty + h) + 128], SW[:, c:c + 128], SWs[:, c:c + 128], qu, su))
-            cols.append(m)
-            rows.append(do("p", [], mm((T.pA, T.pB)[ty][:, 0:256], qu, su, SW[:, 256 * ty:256 * ty + 256], SWs[:, 256 * ty:256 * ty + 256])))
-        sct, rwt = [], []
+    def score(t, ty, tk, k):
+        SW, SWs, sC, Vc, yd = (B(n, t) for n in ("SW", "SWs", "sC", "Vc", "yd"))
+        pr, w = st["prev"], LB + 256 * ty
+        qu, su = T.qU[:, 128 * ty:128 * ty + 128], T.sU[:, 128 * ty:128 * ty + 128]
+        pX = (T.pA, T.pB)[ty]
+        for h in range(2):
+            c = do("p", [q_u, tk, pr], mm(T.pC[:, 512 * (2 * ty + h):512 * (2 * ty + h) + 128], SW[:, w + 128 * h:w + 128 * h + 128],
+                                          SWs[:, w + 128 * h:w + 128 * h + 128], qu, su))
+        r = do("p", [], mm(pX[:, 0:256], qu, su, SW[:, w:w + 256], SWs[:, w:w + 256]))
+        ca = do("s", [c, pr], act(sC[:, 2 * ty:2 * ty + 2], T.pC[:, 1024 * ty:1024 * ty + 1024:512], AF.Abs))
+        ra = do("s", [r], act(Vc[:, 256 * ty:256 * ty + 256], pX[:, 0:256], AF.Abs))
+        ys = [do("s", [ca, ra], act(yd[:, 256 * ty + 128 * h:256 * ty + 128 * h + 128], Vc[:, 256 * ty + 128 * h:256 * ty + 128 * h + 128],
+                                    bias=sC[:, 2 * ty + h:2 * ty + h + 1], scale=-1.0)) for h in range(2)]
+        k["sc"][ty] = (ca, ra, ys)
+
+    def ahead(t, ty, k):
+        sC, Vc, yd, DD = (B(n, t) for n in ("sC", "Vc", "yd", "DD"))
+        ca, ra, ys = k["sc"][ty]
+        o = 512 * ty
+        f0, f1, f2 = ((A.is_lt, A.is_le, A.is_gt), (A.is_gt, A.is_ge, A.is_lt))[ty]
+        a = do("v", [ca, ra, st["prev"]], ts(DD[:, o:o + 128], Vc[:, 256 * ty + 128:256 * ty + 256], sC[:, 2 * ty:2 * ty + 1], None, f0))
+        b = do("v", [ca, ra], ts(DD[:, o + 384:o + 512], Vc[:, 256 * ty:256 * ty + 128], sC[:, 2 * ty + 1:2 * ty + 2], None, f1))
+        d = do("v", [ys, i_mn, i_mt], tt(DD[:, o + 128:o + 384], yd[:, 256 * ty:256 * ty + 256], (T.Mneg, T.Mtri)[ty][:], f2))
+        k["dd"][ty] = [a, b, d]
+
+    def order_and_send(t, k):
+        Vc, DD, rk, H = (B(n, t) for n in ("Vc", "DD", "rk", "H"))
+        pr, rks = st["prev"], []
         for ty in range(2):
-            ca = do("s", [cols[ty], pr], act(sC[:, 2 * ty:2 * ty + 2], T.pC[:, 1024 * ty:1024 * ty + 1024:512], AF.Abs))
-            ra = do("s", [rows[ty]], act(Vc[:, 256 * ty:256 * ty + 256], (T.pA, T.pB)[ty][:, 0:256], AF.Abs))
-            ys = [do("s", [ca, ra], act(yd[:, 256 * ty + 128 * h:256 * ty + 128 * h + 128], Vc[:, 256 * ty + 128 * h:256 * ty + 128 * h + 128],
-                                        AF.Identity, bias=sC[:, 2 * ty + h:2 * ty + h + 1], scale=-1.0)) for h in range(2)]
-            sct.append(ca)
-            rwt.append(ra)
             o = 512 * ty
-            f0, f1, f2 = ((A.is_lt, A.is_le, A.is_gt), (A.is_gt, A.is_ge, A.is_lt))[ty]
-            a = do("v", [ca, ra, pr], ts(DD[:, o:o + 128], Vc[:, 256 * ty + 128:256 * ty + 256], sC[:, 2 * ty:2 * ty + 1], None, f0))
-            b = do("v", [ca, ra], ts(DD[:, o + 384:o + 512], Vc[:, 256 * ty:256 * ty + 128], sC[:, 2 * ty + 1:2 * ty + 2], None, f1))
-            d = do("v", [ys, v_mt], tt(DD[:, o + 128:o + 384], yd[:, 256 * ty:256 * ty + 256], (T.Mneg, T.Mtri)[ty][:], f2))
-            dg.append([a, b, d])
-        rks = []
-        for ty in range(2):
-            o = 512 * ty
-            r0 = do("s", dg[ty], act(DD[:, o:o + 256], DD[:, o:o + 256], AF.Identity, accum_out=rk[:, 2 * ty:2 * ty + 1]))
-            r1 = do("v", dg[ty], red(rk[:, 2 * ty + 1:2 * ty + 2], DD[:, o + 256:o + 512]))
+            r0 = do("s", k["dd"][ty], act(DD[:, o:o + 256], DD[:, o:o + 256], accum_out=rk[:, 2 * ty:2 * ty + 1]))
+            r1 = do("v", k["dd"][ty], red(rk[:, 2 * ty + 1:2 * ty + 2], DD[:, o + 256:o + 512]))
             rks.append([r0, r1])
         hs = [do("v", [rks[b // 2][b % 2], i_kn, pr], ts(H[:, b:512:4], T.Kn[:], rk[:, b:b + 1], None, A.is_equal)) for b in (1, 0, 3, 2)]
         qh = do("v", hs, quant(B("qH", t)[:], B("sH", t)[:], H[:]))
         do("p", [qh, v_qs, pr], mm(T.pD[:, 0:128], T.qS[:, 0:128], T.sS[:, 0:128], B("qH", t)[:], B("sH", t)[:], True, False))
         m = do("p", [], mm(T.pD[:, 0:128], T.qS[:, 128:256], T.sS[:, 128:256], B("qH", t)[:], B("sH", t)[:], False, True))
         trA, lo, G, trG = B("trA", t), B("lo16", t), B("Gs", t), B("trG", t)
-        a = do("v", [m], trn(trA[:], T.pD[:, 0:128]))
-        of = do("v", [a, cst], ts(lo[:, 0:4], trA[:, 0:128:32], C_(AQ), None, A.add))
-        gs = do("v", [of, rwt, pr], cp(G[:, 0:64], Vc[:, 0:512].indirect(lo[:, 0:4])))
-        tg = do("v", [gs], trn(trG[:, 0:64], G[:, 0:64]))
-        mt = do("v", [tg], ts(B("M", t)[:], trG[:, 0:64:32], C_(SG), None, A.mult))
-        send([mt], "aM%d" % t, B("M", t)[:], lambda s: B("landM", t)[:, 2 * s:2 * s + 2])
-        return {"trA": a, "of": of, "M": mt, "pC": sct, "rows": rwt}
+        k["trA"] = a = do("v", [m], trn(trA[:], T.pD[:, 0:128]))
+        of = do("v", [a, cst[1]], ts(lo[:, 0:4], trA[:, 0:128:32], C_(AQ), None, A.add))
+        gs = do("v", [of, k["sc"][0][1], k["sc"][1][1], pr], cp(G[:], Vc[:, 0:512].indirect(lo[:, 0:4])))
+        k["M"] = tg = do("v", [gs], trn(trG[:], G[:]))
+        send([tg], "aM%d" % t, trG[:, 31:33], lambda s: B("landM", t)[:, 2 * s:2 * s + 2])
 
     def prepare(t, k):
-        M, own, wk, dg, VT, trA, G, trG, lo = (B(n, t) for n in ("M", "own", "wk", "dg", "VT", "trA", "Gs", "trG", "lo16"))
-        gp = do("v", [k["of"], K["pl"]], cp(G[:, 64:128], T.plrow[:, 0:512].indirect(lo[:, 0:4])))
-        a = do("v", [k["M"], cst], ts(own[:, 1:2], M[:, 1:2], C_(M1), None, A.mult))
-        x0 = do("v", [k["M"], v_one], ts(B("XR", t)[:, 192:224], T.ones[:, 0:32], M[:, 0:1], None, A.mult))
-        x1 = do("v", [], ts(B("XR", t)[:, 224:256], T.ones[:, 0:32], M[:, 1:2], None, A.mult))
-        tp = do("v", [gp], trn(trG[:, 64:128], G[:, 64:128]))
-        w = do("v", [k["trA"], K["sel"]], tt(wk[:], trA[:, 0:128:32], T.sel[:], A.mult))
-        k["MP"] = do("v", [tp], cp(B("MP", t)[:], trG[:, 64:128:32]))
-        send([k["MP"]], "aP%d" % t, B("MP", t)[:], lambda s: B("landP", t)[:, 2 * s:2 * s + 2])
-        k["s"] = do("v", [a], ts(own[:, 0:1], M[:, 0:1], C_(M0), own[:, 1:2], A.mult, A.add))
-        pl = do("v", [w], red(dg[:, 0:1], wk[:]))
-        k["Ro"] = do("v", [x0, x1], trn(B("R", t)[:, 192:256], B("XR", t)[:, 192:256]))
-        hi = do("v", [pl], ts(B("iw", t)[:, 20:21], dg[:, 0:1], 1 / 16, -7.5 / 16, A.mult, A.add))
-        v2 = do("v", [K["DG"]], ts(VT[:, 64:96], T.DG[:], C_(D4), None, A.mult))
-        hf = do("v", [hi], cp(dg[:, 1:2], B("iw", t)[:, 20:21]))
-        v1 = do("v", [hf], ts(VT[:, 32:64], T.DG[:], dg[:, 1:2], None, A.mult))
-        lo_ = do("v", [hf], ts(dg[:, 2:3], dg[:, 1:2], -16.0, dg[:, 0:1], A.mult, A.add))
+        own, wk, dg, VT, trA, trG, XR = (B(n, t) for n in ("own", "wk", "dg", "VT", "trA", "trG", "XR"))
+        w = do("v", [k["trA"], K["sel"]], tt(wk[:, 0:4], trA[:, 0:128:32], T.sel[:], A.mult))
+        a = do("v", [k["M"], cst], ts(own[:, 1:2], trG[:, 32:33], C_(SM1), None, A.mult))
+        pl = do("v", [w, K["wk"]], red(dg[:, 0:1], wk[:]))
+        k["s"] = do("v", [a], ts(own[:, 0:1], trG[:, 31:32], C_(SM0), own[:, 1:2], A.mult, A.add))
+        hi = do("v", [pl], ts(dg[:, 1:2], dg[:, 0:1], R16, R16, A.add, A.subtract))
+        xo = [do("s", [k["M"], K["sgt"]], act(XR[:, 192 + 32 * j:224 + 32 * j], T.sgt[:], AF.Copy, scale=trG[:, 31 + j:32 + j])) for j in range(2)]
+        v1 = do("v", [hi], ts(VT[:, 32:64], T.DG[:], dg[:, 1:2], None, A.mult))
+        lo_ = do("v", [hi], ts(dg[:, 2:3], dg[:, 0:1], dg[:, 1:2], 7.5, A.subtract, A.add))
+        k["Ro"] = do("v", xo, trn(B("R", t)[:, 192:256], XR[:, 192:256]))
         v0 = do("v", [lo_], ts(VT[:, 0:32], T.DG[:], dg[:, 2:3], None, A.mult))
-        k["VT"] = [v0, v1, v2]
-        k["pl"] = pl
+        k["VT"] = [v0, v1, K["VTc"]]
+
+    def before(s, q, t, deps, at, x_of):
+        R, Dc, out, seg = B("R", t), B("Dc", t), [], []
+        for x in x_of:
+            op = A.is_le if (others + [rank])[x] < q else A.is_lt
+            if seg and seg[-1][1] == 64 * x and seg[-1][2] == op:
+                seg[-1][1] += 64
+            else:
+                seg.append([64 * x, 64 * x + 64, op])
+        for (c0, c1, op) in seg:
+            out.append(do("v", deps, ts(Dc[:, at:at + c1 - c0], R[:, c0:c1], s, 4.0, op, A.mult)))
+            at += c1 - c0
+        return out
 
     def merge_and_send(t, k):
-        LM, XR, R, Dc, cn, pw, lo, own, F = (B(n, t) for n in ("landM", "XR", "R", "Dc", "cn", "pw", "lo16", "own", "F"))
+        LM, XR, R, Dc, cn, pw, lo, own, F, ow = (B(n, t) for n in ("landM", "XR", "R", "Dc", "cn", "pw", "lo16", "own", "F", "ow"))
         aM = ("aM%d" % t, arrive)
         xs = []
         for j in range(6):
             if j % 2 == 0:
-                xs.append(do("v", [aM], ts(XR[:, 32 * j:32 * j + 32], T.ones[:, 0:32], LM[:, j:j + 1], None, A.mult)))
+                xs.append(do("v", [aM, cst], ts(XR[:, 32 * j:32 * j + 32], T.ones[:, 0:32], LM[:, j:j + 1], C_(SG), A.mult, A.mult)))
             else:
-                xs.append(do("s", [aM, v_zer], act(XR[:, 32 * j:32 * j + 32], T.zer[:, 0:32], AF.Identity, bias=LM[:, j:j + 1])))
-        r = do("v", xs, trn(R[:, 0:192], XR[:, 0:192]))
-        k["R"] = r
-        d, e = [], 64 * rank
-        for a, b, op in ((0, e, A.is_le), (e, 192, A.is_lt)):
-            if b > a:
-                d.append(do("v", [r, k["s"], st["prev"]], ts(Dc[:, a:b], R[:, a:b], own[:, 0:1], None, op)))
-        c = do("v", d, red(cn[:, 3:4], Dc[:, 0:192]))
-        k["cn"] = c
-        fl = do("v", [c], ts(B("iw", t)[:, 21:22], cn[:, 3:4], 1 / 16, C_(PF), A.mult, A.add))
-        p4 = do("v", [c], ts(pw[:, 0:1], cn[:, 3:4], 4.0, C_(P4), A.mult, A.add))
-        n4 = do("v", [fl, p4], ts(pw[:, 1:2], B("iw", t)[:, 21:22], 64.0, pw[:, 0:1], A.mult, A.add))
-        of = do("v", [n4, K["OE"]], ts(lo[:, 4:10], T.OE[:], pw[:, 1:2], None, A.add))
-        sc = do("v", [of, k["VT"], K["F"]], cp(F[:, 0:2048].indirect(lo[:, 4:10]), B("VT", t)[:]))
+                xs.append(do("s", [aM, K["sgt"]], act(XR[:, 32 * j:32 * j + 32], T.sgt[:], AF.Copy, scale=LM[:, j:j + 1])))
+        k["R"] = do("v", xs, trn(R[:, 0:192], XR[:, 0:192]))
+        d = before(own[:, 0:1], rank, t, [k["R"], k["s"], st["prev"]], 624, range(3))
+        k["cn"] = c = do("v", [d, K["Dc"]], red(cn[:, 3:4], Dc[:, 624:817]))
+        fl = do("v", [c], ts(pw[:, 0:1], cn[:, 3:4], R64, R64, A.add, A.subtract))
+        of = do("v", [fl, K["OE"]], ts(lo[:, 4:10], T.OE[:], pw[:, 0:1], cn[:, 3:4], A.add, A.add))
+        sc = do("v", [of, k["VT"], K["F"][t]], cp(F[:, 0:2048].indirect(lo[:, 4:10]), B("VT", t)[:]))
         k["qF"] = do("v", [sc], quant(B("qF", t)[:], B("sF", t)[:], F[:, 0:512]))
-        m = do("p", [k["qF"], K["qI"], st["prev"]], mm(T.pE[:, 0:128], T.qI[:, 0:128], T.sI[:, 0:128], B("qF", t)[:], B("sF", t)[:]))
-        a = do("v", [m], trn(B("tr2", t)[:, 0:128], T.pE[:, 0:128]))
-        of = do("v", [a], cp(lo[:, 10:14], B("tr2", t)[:, 0:128:32]))
+        m = do("p", [k["qF"], qi[0], st["prev"]], mm(T.pE[:, 0:128], T.qI[:, 0:128], T.sI[:, 0:128], B("qF", t)[:], B("sF", t)[:]))
+        k["own2"] = do("p", [qi, k["sc"][1][1]], mm(T.pB[:, 0:128], B("qF", t)[:], B("sF", t)[:], T.qI[:, 192:320], T.sI[:, 192:320]))
+        a = do("v", [aM], ts(ow[:, 0:2], LM[:, 0:4:2], C_(SM0), None, A.mult))
+        b = do("v", [aM], ts(ow[:, 2:4], LM[:, 1:4:2], C_(SM1), None, A.mult))
+        a = [a, b, do("v", [m], trn(B("tr2", t)[:, 0:128], T.pE[:, 0:128]))]
+        of = do("v", a, ts(lo[:, 10:14], B("tr2", t)[:, 0:128:32], float(LB), 703.0, A.max, A.min))
         k["pE"] = [a, of]
-        pd = [of, K["nz"][t], k["lt"], k["xt"]]
-        ps = do("v", pd, cp(B("PS", t)[:].bitcast(U32), B("SW", t)[:, 0:768].bitcast(U32).indirect(lo[:, 10:14])))
-        pss = do("s", pd, act(B("PSs", t)[:], B("SWs", t)[:, 0:768].indirect(lo[:, 10:14]), AF.Copy))
+        pd = [of, k["lt"], k["xt"]]
+        ps = do("v", pd, cp(B("PS", t)[:].bitcast(U32), B("SW", t)[:, 0:704].bitcast(U32).indirect(lo[:, 10:14])))
+        pss = do("s", pd, act(B("PSs", t)[:], B("SWs", t)[:, 0:704].indirect(lo[:, 10:14]), AF.Copy))
         LW, LWs = B("LW", t), B("LWs", t)
-        send([ps], "aC%d" % t, B("PS", t)[:, 0:64].bitcast(U8), lambda s: LW[:, 512 + 64 * s:576 + 64 * s].bitcast(U8))
-        send([pss], "aC%d" % t, B("PSs", t)[:, 0:64], lambda s: LWs[:, 512 + 64 * s:576 + 64 * s])
+        o = (64, 128, 0)
+        send([ps], "aC%d" % t, B("PS", t)[:, 0:64].bitcast(U8), lambda s: LW[:, o[s]:o[s] + 64].bitcast(U8))
+        send([pss], "aC%d" % t, B("PSs", t)[:, 0:64], lambda s: LWs[:, o[s]:o[s] + 64])
 
     def lists(t, k):
-        LM, R, Dc, cn, pw, ow, lo, F, iw, ix, tr2 = (B(n, t) for n in ("landM", "R", "Dc", "cn", "pw", "ow", "lo16", "F", "iw", "ix", "tr2"))
-        aM = ("aM%d" % t, arrive)
-        a = do("v", [aM], ts(ow[:, 0:3], LM[:, 0:6:2], C_(M0), None, A.mult))
-        b = do("v", [aM], ts(ow[:, 4:7], LM[:, 1:6:2], C_(M1), None, A.mult))
-        s3 = do("v", [a, b], tt(ow[:, 8:11], ow[:, 0:3], ow[:, 4:7], A.add))
-        acc = []
-        for s, q in enumerate(others):
-            seg = []
-            for x in [y for y in range(4) if y != s]:
-                op = A.is_le if (others + [rank])[x] < q else A.is_lt
-                if seg and seg[-1][1] == 64 * x and seg[-1][2] == op:
-                    seg[-1][1] += 64
-                else:
-                    seg.append([64 * x, 64 * x + 64, op])
-            at, dd = 256 * s, []
-            for (c0, c1, op) in seg:
-                dd.append(do("v", [s3, k["R"], k["Ro"], k["cn"], st["prev"]], ts(Dc[:, at:at + c1 - c0], R[:, c0:c1], ow[:, 8 + s:9 + s], None, op)))
-                at += c1 - c0
-            acc.append(do("s", dd, act(Dc[:, 256 * s:256 * s + 192], Dc[:, 256 * s:256 * s + 192], AF.Identity, accum_out=cn[:, s:s + 1])))
-        k["cnt"] = acc
-        fl = do("v", acc, ts(iw[:, 0:3], cn[:, 0:3], 1 / 16, C_(PF), A.mult, A.add))
-        p4 = do("v", acc, ts(pw[:, 4:7], cn[:, 0:3], 4.0, C_(P4), A.mult, A.add))
-        f6 = do("v", [fl], ts(pw[:, 8:11], iw[:, 0:3], 64.0, None, A.mult))
-        n4 = do("v", [p4, f6], tt(pw[:, 12:15], pw[:, 4:7], pw[:, 8:11], A.add))
-        of = [do("v", [n4], ts(lo[:, 16 + 2 * s:18 + 2 * s], T.OE[:, 4:6], pw[:, 12 + s:13 + s], None, A.add)) for s in range(3)]
-        sc = do("v", [of, K["VO"], k["qF"]], cp(F[:, 0:2048].indirect(lo[:, 16:22]), T.VO[:]))
+        cn, pw, ow, lo, F, iw, ix, tr2, Dc, wl = (B(n, t) for n in ("cn", "pw", "ow", "lo16", "F", "iw", "ix", "tr2", "Dc", "wl"))
+        s2 = do("v", k["pE"], tt(ow[:, 8:10], ow[:, 0:2], ow[:, 2:4], A.add))
+        dep = [s2, k["R"], k["Ro"], k["cn"], st["prev"]]
+        d0 = before(ow[:, 8:9], others[0], t, dep, 0, (1, 2, 3))
+        c0 = do("s", [d0, K["Dc"]], act(Dc[:, 0:193], Dc[:, 0:193], accum_out=cn[:, 0:1]))
+        d1 = before(ow[:, 9:10], others[1], t, dep, 208, (0, 2, 3))
+        c1 = do("v", [d1, K["Dc"]], red(cn[:, 1:2], Dc[:, 208:401]))
+        fl = do("v", [c0, c1], ts(pw[:, 2:4], cn[:, 0:2], R64, R64, A.add, A.subtract))
+        of = [do("v", [fl], ts(lo[:, 16 + 2 * s:18 + 2 * s], T.OE[:, 4:6], pw[:, 2 + s:3 + s], cn[:, s:s + 1], A.add, A.add)) for s in range(2)]
+        sc = do("v", [of, K["VO"], k["qF"]], cp(F[:, 0:2048].indirect(lo[:, 16:20]), T.VO[:]))
         qg = do("v", [sc], quant(B("qG", t)[:], B("sG", t)[:], F[:, 0:512]))
-        ml = do("p", [qg, k["trA"]], mm(T.pD[:, 0:128], T.qI[:, 128:256], T.sI[:, 128:256], B("qG", t)[:], B("sG", t)[:]))
+        ml = do("p", [qg, qi, k["trA"]], mm(T.pD[:, 0:128], T.qI[:, 128:256], T.sI[:, 128:256], B("qG", t)[:], B("sG", t)[:]))
         md = do("p", [k["pE"]], mm(T.pE[:, 0:128], T.qI[:, 256:384], T.sI[:, 256:384], B("qG", t)[:], B("sG", t)[:]))
+        w1 = do("v", [k["own2"]], ts(wl[:, 0:2], T.pB[:, 0:128:64], 0.0, None, A.is_gt))
+        w2 = do("v", [w1, K["BS"]], tt(wl[:, 2:4], wl[:, 0:2], T.BS[:], A.mult))
         a = do("v", [ml, k["pE"]], trn(tr2[:, 0:128], T.pD[:, 0:128]))
-        nl = [do("v", [a], ts(lo[:, 24 + 4 * h:28 + 4 * h], tr2[:, 0:128:32], 255.0, None, A.min)) for h in range(2)]
         b = do("v", [md], trn(tr2[:, 128:256], T.pE[:, 0:128]))
-        g8 = do("v", [a, b], ts(ix[:, 0:8], tr2[:, 0:256:32], 512.0, None, A.is_ge))
+        nl = do("v", [a], ts(lo[:, 24:28], tr2[:, 0:128:32], -float(LB), 255.0, A.add, A.min))
+        g8 = do("v", [a, b], ts(ix[:, 0:8], tr2[:, 0:256:32], float(LB), None, A.is_lt))
+        nd_ = [nl, K["nz"], K["np"][t], st["prev"]]
+        k["np"] = [do("v", nd_, cp(B("NP", t)[:, 64:128].bitcast(U32), T.NZ[:, 0:256].bitcast(U32).indirect(lo[:, 24:28]))),
+                   do("s", nd_, act(B("NPs", t)[:, 64:128], T.NZs[:, 0:256].indirect(lo[:, 24:28]), AF.Copy))]
         k8 = do("v", [g8, K["kk8"]], tt(ix[:, 8:16], ix[:, 0:8], T.kk8[:], A.mult))
+        k["w"] = do("v", [w2], tt(wl[:, 4:6], T.pB[:, 0:128:64], wl[:, 2:4], A.add))
         i8 = do("v", [k8], tt(ix[:, 16:24], tr2[:, 0:256:32], ix[:, 8:16], A.add))
         k["AB"] = do("v", [i8], cp(lo[:, 32:40], ix[:, 16:24]))
-        nd_ = [nl, K["nz"][t], st["prev"]]
-        k["np"] = [do("v", nd_, cp(B("NP", t)[:].bitcast(U32), B("SW", t)[:, 512:768].bitcast(U32).indirect(lo[:, 24:32]))),
-                   do("s", nd_, act(B("NPs", t)[:], B("SWs", t)[:, 512:768].indirect(lo[:, 24:32]), AF.Copy))]
-        fl = do("v", [i8], ts(iw[:, 8:16], ix[:, 16:24], 1 / 16, -7.5 / 16, A.mult, A.add))
-        f6 = do("v", [fl], ts(ix[:, 0:8], iw[:, 8:16], 16.0, None, A.mult))
+        send([k["w"]], "aP%d" % t, wl[:, 4:6], lambda s: B("landP", t)[:, 2 * s:2 * s + 2])
+        fl = do("v", [i8], ts(iw[:], ix[:, 16:24], 1 / 16, -7.5 / 16, A.mult, A.add))
+        k["i8"], k["fl"] = i8, fl
+        k["dn"] = [do("p", [k["np"], K["qE"], st["prev"]], mm(T.pC[:, 512 * b:512 * b + 128], T.qE[:, 128 * b:128 * b + 128], T.sE[:, 128 * b:128 * b + 128],
+                                                              B("NP", t)[:], B("NPs", t)[:], True, False)) for b in range(4)]
+
+    def place_offsets(t, k):
+        lo, iw, ix = B("lo16", t), B("iw", t), B("ix", t)
+        f6 = do("v", [k["fl"]], ts(ix[:, 0:8], iw[:], 16.0, None, A.mult))
         n8 = do("v", [f6], tt(ix[:, 24:32], ix[:, 0:8], ix[:, 16:24], A.add))
-        k["uo"] = []
-        for x in range(2):
-            for h in range(2):
-                o = 48 + 8 * x
-                k["uo"].append(do("v", [n8], ts(lo[:, o + h:o + 8:2], ix[:, 24 + 4 * x:28 + 4 * x], 16.0 * h - 512.0 * x, None, A.add)))
-        k["dn"] = [do("p", [k["np"], K["qE"], k["pC"]], mm(T.pC[:, 512 * b:512 * b + 128], T.qE[:, 128 * b:128 * b + 128], T.sE[:, 128 * b:128 * b + 128],
-                                                           B("NP", t)[:], B("NPs", t)[:], True, False)) for b in range(4)]
+        k["uo"] = [do("v", [n8], ts(lo[:, 48 + h:64:2], ix[:, 24:32], 16.0 * h, None, A.add)) for h in range(2)]
 
     def update_list(t, k, x):
         U, tr, lo = B("UX" if x else "UL", t), B("trX" if x else "trU", t), B("lo16", t)
-        sc = do("v", [k["uo"], K["RC"], K["U%d" % t]], cp(U[:, 0:1408].indirect(lo[:, 48 + 8 * x:56 + 8 * x]), T.RC[:]))
-        a = do("v", [sc, st["prev"]], trn(tr[:], U[:, 0:512]))
+        w = 1408 if x else 896
+        sc = do("v", [k["uo"], K["RC"], K["U%d" % t]], cp(U[:, 0:w].indirect(lo[:, 48 + 8 * x:56 + 8 * x]), T.RC[:]))
+        a = do("v", [sc, st["prev"]], trn(tr[:], U[:, w - 512:w]))
         k["ux" if x else "ul"] = do("v", [a], cp(lo[:, 64 + 16 * x:80 + 16 * x], tr[:, 0:512:32]))
 
-    def renew(t, k, oq, os_):
+    def renew(t, k, oq, os_, o):
         LW, LWs, XW, XWs, LN, LNs, NEW, lo = (B(n, t) for n in ("LW", "LWs", "XW", "XWs", "LN", "LNs", "NEW", "lo16"))
         ad = [("aC%d" % t, 2 * arrive), k["AB"], k["cp"]["W"]]
         a1 = do("v", ad, cp(XW[:, 256:384].bitcast(U32), LW[:, 0:704].bitcast(U32).indirect(lo[:, 32:40])))
         a2 = do("s", ad, act(XWs[:, 256:384], LWs[:, 0:704].indirect(lo[:, 32:40]), AF.Copy))
+        k["A"] = [a1, a2]
         dc = [do("p", [a1, a2], mm(T.pC[:, 512 * b:512 * b + 128], T.qE[:, 128 * b:128 * b + 128], T.sE[:, 128 * b:128 * b + 128],
                                    XW[:, 256:384], XWs[:, 256:384], False, True)) for b in range(4)]
-        update_list(t, k, 1)
+        update_list(t, k, 0)
         nw = []
         for b in range(4):
-            i, o = T.pC[:, 512 * b + 64:512 * b + 128], NEW[:, b:256:4]
-            nw.append(do("v", [dc[b]], cp(o, i)) if b % 2 == 0 else do("s", [dc[b], st["prev"]], act(o, i, AF.Copy)))
+            i, h = T.pC[:, 512 * b + 64:512 * b + 128], NEW[:, b:256:4]
+            nw.append(do("v", [dc[b]], cp(h, i)) if b % 2 == 0 else do("s", [dc[b], st["prev"]], act(h, i, AF.Copy)))
         qn = do("v", [nw, K["NEW"]], quant(LN[:, 256:384], LNs[:, 256:384], NEW[:]))
-        l1 = do("v", [qn, k["ul"], k["cp"]["L"]], cp(oq[:, 0:256].bitcast(U32), LN[:, 0:384].bitcast(U32).indirect(lo[:, 64:80])))
-        l2 = do("s", [qn, k["ul"], k["cp"]["L"]], act(os_[:, 0:256], LNs[:, 0:384].indirect(lo[:, 64:80]), AF.Copy))
-        x1 = do("v", [k["ux"], k["cp"]["X"]], cp(oq[:, 256:512].bitcast(U32), XW[:, 0:384].bitcast(U32).indirect(lo[:, 80:96])))
-        x2 = do("s", [k["ux"], k["cp"]["X"]], act(os_[:, 256:512], XWs[:, 0:384].indirect(lo[:, 80:96]), AF.Copy))
-        return [l1, l2], [x1, x2], nw
+        l1 = do("v", [qn, k["ul"], k["cp"]["L"]], cp(oq[:, o:o + 256].bitcast(U32), LN[:, 0:384].bitcast(U32).indirect(lo[:, 64:80])))
+        l2 = do("s", [qn, k["ul"], k["cp"]["L"]], act(os_[:, o:o + 256], LNs[:, 0:384].indirect(lo[:, 64:80]), AF.Copy))
+        return [l1, l2], nw
 
-    def outlists(t, k):
-        ky, KX, KT, dk, pt, LP, cn = (B(n, t) for n in ("ky", "KX", "KT", "dk", "pt", "landP", "cn"))
+    def renew_dormant(t, k, oq, os_, o):
+        XW, XWs, lo = B("XW", t), B("XWs", t), B("lo16", t)
+        update_list(t, k, 1)
+        xd = [k["ux"], k["cp"]["X"], k["A"]]
+        x1 = do("v", xd, cp(oq[:, o + 256:o + 512].bitcast(U32), XW[:, 0:384].bitcast(U32).indirect(lo[:, 80:96])))
+        x2 = do("s", xd, act(os_[:, o + 256:o + 512], XWs[:, 0:384].indirect(lo[:, 80:96]), AF.Copy))
+        return [x1, x2]
+
+    def numbers(t, k):
+        LP, fo, wl = B("landP", t), B("fo", t), B("wl", t)
         aP = ("aP%d" % t, arrive)
-        a = do("v", [aP], ts(ky[:, 0:3], LP[:, 0:6:2], C_(M0), None, A.mult))
-        b = do("v", [aP], ts(ky[:, 4:7], LP[:, 1:6:2], C_(M1), None, A.mult))
-        o = do("v", [k["pl"]], cp(ky[:, 3:4], B("dg", t)[:, 0:1]))
-        o2 = do("v", [], fill(ky[:, 7:8], 0.0))
-        c = do("v", [k["cnt"], k["cn"]], ts(ky[:, 8:12], cn[:, 0:4], 2048.0, C_(PK), A.mult, A.add))
-        d = do("v", [a, b, o, o2], tt(ky[:, 12:16], ky[:, 0:4], ky[:, 4:8], A.add))
-        e = do("v", [c, K["Q4"]], tt(ky[:, 16:20], ky[:, 8:12], T.cc[:, 12:16], A.add))
-        f = do("v", [d, e], tt(ky[:, 20:24], ky[:, 12:16], ky[:, 16:20], A.add))
-        x = [do("s", [f, k.get("kx")], act(KX[:, 32 * j:32 * j + 32], T.zer[:, 0:32], AF.Identity, bias=ky[:, 20 + j:21 + j])) for j in range(4)]
-        tr = do("v", x, trn(KT[:], KX[:]))
-        dd = [do("s", [tr, k.get("kx")], act(dk[:, 128 * c:128 * c + 128], KT[:], AF.Abs, bias=C_(KB0 + c))) for c in range(2)]
-        m = [do("v", [dd[c]], red(pt[:, c:c + 1], dk[:, 128 * c:128 * c + 128], A.min)) for c in range(2)]
-        h = [do("v", m, cp(pt[o:o + 32, 4:6], pt[o + 32:o + 64, 0:2])) for o in (0, 64)]
-        n = [do("v", h, tt(pt[o:o + 32, 6:8], pt[o:o + 32, 0:2], pt[o:o + 32, 4:6], A.min)) for o in (0, 64)]
-        for c in range(2):
-            dma("y", n, T.lw[t:t + 1, 32 * c:32 * c + 32], pt[0:32, 6 + c:7 + c])
-            dma("y", n, T.sw[t:t + 1, 32 * c:32 * c + 32], pt[64:96, 6 + c:7 + c])
-        return m
+        a = [do("v", [aP], red(fo[:, j:j + 1], LP[:, j:6:2])) for j in range(2)]
+        b = do("v", [a, k["w"]], tt(fo[:, 2:4], fo[:, 0:2], wl[:, 4:6], A.add))
+        for c in range(4):
+            dma("y", [b], T.lw[t:t + 1, 16 * c:16 * c + 16], fo[32 * c:32 * c + 16, 2:3])
+            dma("y", [b], T.sw[t:t + 1, 16 * c:16 * c + 16], fo[32 * c:32 * c + 16, 3:4])
 
-    late_iotas()
-    lt, xt, pc, last, kx = q_l, q_x, None, None, None
+    ks = [{"sc": {}, "dd": {}, "cp": {}} for t in range(ROUNDS)]
+    k = ks[0]
+    k["lt"], k["xt"] = q_l, q_x
+    for ty in range(2):
+        score(0, ty, (q_l, q_x)[ty], k)
+        ahead(0, ty, k)
+        copies(0, ty, (q_l, q_x)[ty], k["cp"])
     for t in range(ROUNDS):
-        k = order_and_send(t, lt, xt, pc)
-        k["lt"], k["xt"] = lt, xt
-        k["cp"] = copies(t, lt, xt)
+        k = ks[t]
+        last = t + 1 == ROUNDS
+        order_and_send(t, k)
         if t == 0:
-            late_consts()
+            consts_s()
         prepare(t, k)
         if t == 0:
-            later_consts()
+            consts_v()
         else:
-            k["kx"] = outlists(t - 1, last)
+            consts_2()
+            numbers(0, ks[0])
         merge_and_send(t, k)
         lists(t, k)
-        update_list(t, k, 0)
-        if t + 1 < ROUNDS:
-            oq, os_ = B("SW", t + 1), B("SWs", t + 1)
+        place_offsets(t, k)
+        oq, os_, o = (T.FN, T.FNs, 0) if last else (B("SW", t + 1), B("SWs", t + 1), LB)
+        lt, pc = renew(t, k, oq, os_, o)
+        st["prev"] = [lt, pc, k["w"]]
+        if last:
+            my = do("p", [lt, K["qW"], k["sc"][0][1]], mm(T.pA[:, 0:256], T.qW[:], T.sW[:], T.FN[:, 0:256], T.FNs[:, 0:256]))
+            dma("y", lt, T.oc[:, 0:1024], T.FN[:, 0:256].bitcast(U8))
+            for q in range(4):
+                dma("y", lt, T.osc[4 * q:4 * q + 4, 0:256], T.FNs[32 * q:32 * q + 4, 0:256])
+            xt = renew_dormant(t, k, oq, os_, o)
+            yc = do("s", [my], act(T.yt[:], T.pA[:, 0:256], AF.Copy))
+            dma("s", [yc], T.y[:], T.yt[:])
+            dma("y", xt, T.oc[:, 1024:2048], T.FN[:, 256:512].bitcast(U8))
+            for q in range(4):
+                dma("y", xt, T.osc[4 * q:4 * q + 4, 256:512], T.FNs[32 * q:32 * q + 4, 256:512])
+            numbers(t, k)
         else:
-            oq, os_ = T.FN, T.FNs
-        lt, xt, pc = renew(t, k, oq, os_)
-        st["prev"] = [lt, xt, pc]
-        last = k
-    my = do("p", [lt, K["qW"], last["rows"]], mm(T.pA[:, 0:256], T.qW[:], T.sW[:], T.FN[:, 0:256], T.FNs[:, 0:256]))
-    for o, tk in ((0, lt), (256, xt)):
-        dma("y", tk, T.oc[:, 4 * o:4 * o + 1024], T.FN[:, o:o + 256].bitcast(U8))
-        for q in range(4):
-            dma("y", tk, T.osc[4 * q:4 * q + 4, o:o + 256], T.FNs[32 * q:32 * q + 4, o:o + 256])
-    yc = do("s", [my], act(T.yt[:], T.pA[:, 0:256], AF.Copy))
-    dma("s", [yc], T.y[:], T.yt[:])
-    outlists(ROUNDS - 1, last)
+            n = ks[t + 1]
+            n["lt"] = lt
+            copies(t + 1, 0, lt, n["cp"])
+            score(t + 1, 0, lt, n)
+            n["xt"] = xt = renew_dormant(t, k, oq, os_, o)
+            st["prev"].append(xt)
+            copies(t + 1, 1, xt, n["cp"])
+            ahead(t + 1, 0, n)
+            score(t + 1, 1, xt, n)
+            ahead(t + 1, 1, n)
     for s, n in cnt.items():
         if top.get(s, 0) < n:
             g.wait_ge(T.sem[s], n)

@@ -18,9 +18,9 @@ for _n, _w, _d in (
         ("SS", 1024, "bfloat16"), ("SI", 1024, "bfloat16"), ("EM", 516, "bfloat16"), ("qS", 256, F8), ("sS", 256, "uint8"),
         ("qI", 384, F8), ("sI", 384, "uint8"), ("qE", 512, F8), ("sE", 512, "uint8"), ("NZ", 256, F8), ("NZs", 256, "uint8"),
         ("pI", 1, "int32"), ("ii", 8, "int32"), ("fc", 8, "float32"), ("cc", 16, "float32"),
-        ("tin", 256, "float32"), ("Mneg", 256, "float32"), ("Mtri", 256, "float32"), ("Kn", 128, "bfloat16"), ("RC", 128, "float32"),
+        ("tin", 256, "float32"), ("Mneg", 256, "float32"), ("Mtri", 256, "float32"), ("Kn", 128, "bfloat16"), ("RC", 128, "bfloat16"),
         ("sel", 4, "float32"), ("io8", 8, "float32"), ("kk8", 8, "float32"), ("io32", 32, "float32"), ("DG", 32, "bfloat16"),
-        ("sgt", 32, "float32"), ("VO", 64, "bfloat16"), ("OE", 6, "float32"), ("BS", 2, "float32"), ("urow", 512, "float32"),
+        ("sgt", 32, "float32"), ("VO", 64, "bfloat16"), ("OE", 6, "float32"), ("urow", 512, "bfloat16"),
         ("yt", 256, "float32"), ("FN", 512, F8), ("FNs", 512, "uint8")):
     SCRATCH[_n] = ("sbuf", [128, _w], _d)
 ONCE = ("yd", "DD", "Dc", "tr2", "trU", "trX", "qH", "sH", "H", "Gs", "sC", "Vc", "rk", "trA", "wk",
@@ -34,8 +34,8 @@ for _n, _w, _d in (
         ("trA", 128, "float32"), ("Gs", 64, "float32"), ("trG", 64, "float32"), ("dg", 4, "float32"), ("wk", 5, "float32"),
         ("own", 2, "float32"), ("landM", 6, "float32"), ("landP", 6, "float32"), ("XR", 256, "float32"), ("R", 256, "float32"),
         ("Dc", 832, "bfloat16"), ("cn", 4, "float32"), ("pw", 8, "float32"), ("ow", 16, "float32"),
-        ("tr2", 256, "float32"), ("ix", 40, "float32"), ("UL", 896, "float32"), ("UX", 1408, "float32"),
-        ("trU", 512, "float32"), ("trX", 512, "float32"), ("lo16", 128, "uint16"), ("iw", 8, "int32"),
+        ("tr2", 256, "float32"), ("ix", 40, "float32"), ("UL", 896, "bfloat16"), ("UX", 1408, "bfloat16"),
+        ("trU", 512, "bfloat16"), ("trX", 512, "bfloat16"), ("lo16", 128, "uint16"), ("iw", 8, "int32"),
         ("wl", 8, "float32"), ("fo", 4, "float32")):
     for _t in range(1 if _n in ONCE else ROUNDS):
         SCRATCH[_n + str(_t)] = ("sbuf", [128, _w], _d)
@@ -90,7 +90,7 @@ def rank_program(g, core, T, topo):
         eng[c] = fe[n * w:(n + 1) * w]
     for c in dst:
         if c not in eng:
-            eng[c] = [e for e in topo.engines(core, c) if e not in fe]
+            eng[c] = [e for e in topo.engines(core, c) if e not in fe][::len(far)]
     arrive = sum(len(e) for e in eng.values())
 
     def send(deps, sem, view, land):
@@ -164,8 +164,8 @@ def rank_program(g, core, T, topo):
     K["io8"] = do("gc", [], iota(T.io8[:], [[0, 2], [16, 4]]))
     K["OE"] = do("gc", [], iota(T.OE[:], [[1, 3], [64, 2]], 30))
     K["EM"] = do("gc", [v_half], lambda q: q.affine_select(T.EM[:], T.half[:], [[1, 516]], A.is_equal, 0.0, -3, -4))
-    K["RC"] = do("gc", [], iota(T.RC[:], [[16, 4], [0, 2], [1, 16]], 256))
-    K["ur"] = do("gc", [], iota(T.urow[:], [[16, 16], [0, 2], [1, 16]]))
+    K["RC"] = do("gc", [], iota(T.RC[:], [[16, 4], [0, 2], [1, 16]], 128))
+    K["ur"] = do("gc", [], iota(T.urow[:], [[16, 16], [0, 2], [1, 16]], -128))
     for t in range(ROUNDS):
         K["U%d" % t] = [dma("y", [K["ur"]], B("UL", t)[:, 384:896], T.urow[:]), dma("y", [K["ur"]], B("UX", t)[:, 896:1408], T.urow[:])]
     F_ = lambda c: T.fc[:, c:c + 1]
@@ -180,8 +180,9 @@ def rank_program(g, core, T, topo):
         uz.append(do("v", [d_u, v_one], ts(T.uz[:, b:512:4], T.ones[:, 0:128], T.u0[:, b:b + 1], None, A.mult)))
     for b in range(4):
         uz.append(do("s", [d_z, v_zer], act(T.uz[:, 512 + b:1024:4], T.zer[:], bias=T.z0[:, b:b + 1])))
-    q_u = do("v", uz, quant(T.qU[:], T.sU[:], T.uz[:]))
+    q_u = [do("v", uz[0:4], quant(T.qU[:, 0:128], T.sU[:, 0:128], T.uz[:, 0:512]))]
     q_l = do("v", [d_lv], quant(SW0[:, LB:XB], SWs0[:, LB:XB], T.t_lv[:]))
+    q_u.append(do("v", uz[4:8], quant(T.qU[:, 128:256], T.sU[:, 128:256], T.uz[:, 512:1024])))
     q_x = do("v", [d_dm], quant(SW0[:, XB:704], SWs0[:, XB:704], T.t_dm[:]))
     sst = []
     for b in range(4):
@@ -212,7 +213,6 @@ def rank_program(g, core, T, topo):
         K["VO"] = [do("v", [K["DG"]], ts(T.VO[:, 32 * s:32 * s + 32], T.DG[:], 64.0 * (s + 1), None, A.mult)) for s in range(2)]
         K["nz"] = do("v", [d_nz], quant(T.NZ[:], T.NZs[:], T.t_nz[:]))
         K["kk8"] = do("v", [K["io8"]], ts(T.kk8[:], T.io8[:], F_(0), None, A.add))
-        K["BS"] = [do("v", [], fill(T.BS[:, j:j + 1], 256.0 * rank - (LB, XB)[j])) for j in range(2)]
         K["qE"] = [do("v", [K["EM"]], quant(T.qE[:, 128 * b:128 * b + 128], T.sE[:, 128 * b:128 * b + 128], T.EM[:, 3 - b:515 - b])) for b in range(4)]
         K["np"] = [do("v", [d_nz], quant(B("NP", 0)[:], B("NPs", 0)[:], T.t_nz[:, 0:512]))]
         K["NEW"] = do("v", [], fill(B("NEW", 0)[:, 256:512], 0.0))
@@ -236,12 +236,12 @@ def rank_program(g, core, T, topo):
         pr, w = st["prev"], LB + 256 * ty
         qu, su = T.qU[:, 128 * ty:128 * ty + 128], T.sU[:, 128 * ty:128 * ty + 128]
         pX = (T.pA, T.pB)[ty]
+        r = do("p", [q_u[ty], tk, pr], mm(pX[:, 0:256], qu, su, SW[:, w:w + 256], SWs[:, w:w + 256]))
         for h in range(2):
-            c = do("p", [q_u, tk, pr], mm(T.pC[:, 512 * (2 * ty + h):512 * (2 * ty + h) + 128], SW[:, w + 128 * h:w + 128 * h + 128],
-                                          SWs[:, w + 128 * h:w + 128 * h + 128], qu, su))
-        r = do("p", [], mm(pX[:, 0:256], qu, su, SW[:, w:w + 256], SWs[:, w:w + 256]))
-        ca = do("s", [c, pr], act(sC[:, 2 * ty:2 * ty + 2], T.pC[:, 1024 * ty:1024 * ty + 1024:512], AF.Abs))
-        ra = do("s", [r], act(Vc[:, 256 * ty:256 * ty + 256], pX[:, 0:256], AF.Abs))
+            c = do("p", [], mm(T.pC[:, 512 * (2 * ty + h):512 * (2 * ty + h) + 128], SW[:, w + 128 * h:w + 128 * h + 128],
+                               SWs[:, w + 128 * h:w + 128 * h + 128], qu, su))
+        ra = do("s", [r, pr], act(Vc[:, 256 * ty:256 * ty + 256], pX[:, 0:256], AF.Abs))
+        ca = do("s", [c], act(sC[:, 2 * ty:2 * ty + 2], T.pC[:, 1024 * ty:1024 * ty + 1024:512], AF.Abs))
         ys = [do("s", [ca, ra], act(yd[:, 256 * ty + 128 * h:256 * ty + 128 * h + 128], Vc[:, 256 * ty + 128 * h:256 * ty + 128 * h + 128],
                                     bias=sC[:, 2 * ty + h:2 * ty + h + 1], scale=-1.0)) for h in range(2)]
         k["sc"][ty] = (ca, ra, ys)
@@ -254,17 +254,25 @@ def rank_program(g, core, T, topo):
         a = do("v", [ca, ra, st["prev"]], ts(DD[:, o:o + 128], Vc[:, 256 * ty + 128:256 * ty + 256], sC[:, 2 * ty:2 * ty + 1], None, f0))
         b = do("v", [ca, ra], ts(DD[:, o + 384:o + 512], Vc[:, 256 * ty:256 * ty + 128], sC[:, 2 * ty + 1:2 * ty + 2], None, f1))
         d = do("v", [ys, i_mn, i_mt], tt(DD[:, o + 128:o + 384], yd[:, 256 * ty:256 * ty + 256], (T.Mneg, T.Mtri)[ty][:], f2))
-        k["dd"][ty] = [a, b, d]
+        return [a, b, d]
 
     def order_and_send(t, k):
         Vc, DD, rk, H = (B(n, t) for n in ("Vc", "DD", "rk", "H"))
-        pr, rks = st["prev"], []
-        for ty in range(2):
-            o = 512 * ty
-            r0 = do("s", k["dd"][ty], act(DD[:, o:o + 256], DD[:, o:o + 256], accum_out=rk[:, 2 * ty:2 * ty + 1]))
-            r1 = do("v", k["dd"][ty], red(rk[:, 2 * ty + 1:2 * ty + 2], DD[:, o + 256:o + 512]))
-            rks.append([r0, r1])
-        hs = [do("v", [rks[b // 2][b % 2], i_kn, pr], ts(H[:, b:512:4], T.Kn[:], rk[:, b:b + 1], None, A.is_equal)) for b in (1, 0, 3, 2)]
+        pr, r = st["prev"], {}
+
+        def hot(b):
+            return do("v", [r[b], i_kn, pr], ts(H[:, b:512:4], T.Kn[:], rk[:, b:b + 1], None, A.is_equal))
+
+        def total(b, dd):
+            r[b] = do("s", dd, act(DD[:, 256 * b:256 * b + 256], DD[:, 256 * b:256 * b + 256], accum_out=rk[:, b:b + 1]))
+
+        dd = ahead(t, 0, k)
+        total(0, dd)
+        total(1, dd)
+        dd = ahead(t, 1, k)
+        total(2, dd)
+        r[3] = do("v", dd, red(rk[:, 3:4], DD[:, 768:1024]))
+        hs = [hot(b) for b in (0, 1, 3, 2)]
         qh = do("v", hs, quant(B("qH", t)[:], B("sH", t)[:], H[:]))
         do("p", [qh, v_qs, pr], mm(T.pD[:, 0:128], T.qS[:, 0:128], T.sS[:, 0:128], B("qH", t)[:], B("sH", t)[:], True, False))
         m = do("p", [], mm(T.pD[:, 0:128], T.qS[:, 128:256], T.sS[:, 128:256], B("qH", t)[:], B("sH", t)[:], False, True))
@@ -320,10 +328,11 @@ def rank_program(g, core, T, topo):
         k["qF"] = do("v", [sc], quant(B("qF", t)[:], B("sF", t)[:], F[:, 0:512]))
         m = do("p", [k["qF"], qi[0], st["prev"]], mm(T.pE[:, 0:128], T.qI[:, 0:128], T.sI[:, 0:128], B("qF", t)[:], B("sF", t)[:]))
         k["own2"] = do("p", [qi, k["sc"][1][1]], mm(T.pB[:, 0:128], B("qF", t)[:], B("sF", t)[:], T.qI[:, 192:320], T.sI[:, 192:320]))
-        a = do("v", [aM], ts(ow[:, 0:2], LM[:, 0:4:2], C_(SM0), None, A.mult))
-        b = do("v", [aM], ts(ow[:, 2:4], LM[:, 1:4:2], C_(SM1), None, A.mult))
-        a = [a, b, do("v", [m], trn(B("tr2", t)[:, 0:128], T.pE[:, 0:128]))]
-        of = do("v", a, ts(lo[:, 10:14], B("tr2", t)[:, 0:128:32], float(LB), 703.0, A.max, A.min))
+        for s in range(2):
+            a = do("s", [aM, cst], act(ow[:, s:s + 1], LM[:, 2 * s:2 * s + 1], scale=C_(SM0)))
+            k["s2"] = do("s", [a], act(ow[:, 8 + s:9 + s], LM[:, 2 * s + 1:2 * s + 2], scale=C_(SM1), bias=ow[:, s:s + 1]))
+        a = do("v", [m], trn(B("tr2", t)[:, 0:128], T.pE[:, 0:128]))
+        of = do("v", [a], ts(lo[:, 10:14], B("tr2", t)[:, 0:128:32], float(LB), 703.0, A.max, A.min))
         k["pE"] = [a, of]
         pd = [of, k["lt"], k["xt"]]
         ps = do("v", pd, cp(B("PS", t)[:].bitcast(U32), B("SW", t)[:, 0:704].bitcast(U32).indirect(lo[:, 10:14])))
@@ -335,8 +344,7 @@ def rank_program(g, core, T, topo):
 
     def lists(t, k):
         cn, pw, ow, lo, F, iw, ix, tr2, Dc, wl = (B(n, t) for n in ("cn", "pw", "ow", "lo16", "F", "iw", "ix", "tr2", "Dc", "wl"))
-        s2 = do("v", k["pE"], tt(ow[:, 8:10], ow[:, 0:2], ow[:, 2:4], A.add))
-        dep = [s2, k["R"], k["Ro"], k["cn"], st["prev"]]
+        dep = [k["s2"], k["R"], k["Ro"], k["cn"], st["prev"]]
         d0 = before(ow[:, 8:9], others[0], t, dep, 0, (1, 2, 3))
         c0 = do("s", [d0, K["Dc"]], act(Dc[:, 0:193], Dc[:, 0:193], accum_out=cn[:, 0:1]))
         d1 = before(ow[:, 9:10], others[1], t, dep, 208, (0, 2, 3))
@@ -347,8 +355,11 @@ def rank_program(g, core, T, topo):
         qg = do("v", [sc], quant(B("qG", t)[:], B("sG", t)[:], F[:, 0:512]))
         ml = do("p", [qg, qi, k["trA"]], mm(T.pD[:, 0:128], T.qI[:, 128:256], T.sI[:, 128:256], B("qG", t)[:], B("sG", t)[:]))
         md = do("p", [k["pE"]], mm(T.pE[:, 0:128], T.qI[:, 256:384], T.sI[:, 256:384], B("qG", t)[:], B("sG", t)[:]))
-        w1 = do("v", [k["own2"]], ts(wl[:, 0:2], T.pB[:, 0:128:64], 0.0, None, A.is_gt))
-        w2 = do("v", [w1, K["BS"]], tt(wl[:, 2:4], wl[:, 0:2], T.BS[:], A.mult))
+        w1 = do("s", [k["own2"]], act(wl[:, 0:2], T.pB[:, 0:128:64], AF.Sign))
+        k["w"] = []
+        for j in range(2):
+            w2 = do("s", [w1], act(wl[:, 2 + j:3 + j], wl[:, j:j + 1], AF.Copy, scale=256.0 * rank - (LB, XB)[j]))
+            k["w"].append(do("s", [w2], act(wl[:, 4 + j:5 + j], T.pB[:, 64 * j:64 * j + 1], bias=wl[:, 2 + j:3 + j])))
         a = do("v", [ml, k["pE"]], trn(tr2[:, 0:128], T.pD[:, 0:128]))
         b = do("v", [md], trn(tr2[:, 128:256], T.pE[:, 0:128]))
         nl = do("v", [a], ts(lo[:, 24:28], tr2[:, 0:128:32], -float(LB), 255.0, A.add, A.min))
@@ -357,50 +368,49 @@ def rank_program(g, core, T, topo):
         k["np"] = [do("v", nd_, cp(B("NP", t)[:, 64:128].bitcast(U32), T.NZ[:, 0:256].bitcast(U32).indirect(lo[:, 24:28]))),
                    do("s", nd_, act(B("NPs", t)[:, 64:128], T.NZs[:, 0:256].indirect(lo[:, 24:28]), AF.Copy))]
         k8 = do("v", [g8, K["kk8"]], tt(ix[:, 8:16], ix[:, 0:8], T.kk8[:], A.mult))
-        k["w"] = do("v", [w2], tt(wl[:, 4:6], T.pB[:, 0:128:64], wl[:, 2:4], A.add))
         i8 = do("v", [k8], tt(ix[:, 16:24], tr2[:, 0:256:32], ix[:, 8:16], A.add))
         k["AB"] = do("v", [i8], cp(lo[:, 32:40], ix[:, 16:24]))
         send([k["w"]], "aP%d" % t, wl[:, 4:6], lambda s: B("landP", t)[:, 2 * s:2 * s + 2])
-        fl = do("v", [i8], ts(iw[:], ix[:, 16:24], 1 / 16, -7.5 / 16, A.mult, A.add))
-        k["i8"], k["fl"] = i8, fl
         k["dn"] = [do("p", [k["np"], K["qE"], st["prev"]], mm(T.pC[:, 512 * b:512 * b + 128], T.qE[:, 128 * b:128 * b + 128], T.sE[:, 128 * b:128 * b + 128],
                                                               B("NP", t)[:], B("NPs", t)[:], True, False)) for b in range(4)]
-
-    def place_offsets(t, k):
-        lo, iw, ix = B("lo16", t), B("iw", t), B("ix", t)
-        f6 = do("v", [k["fl"]], ts(ix[:, 0:8], iw[:], 16.0, None, A.mult))
+        fl = do("v", [i8], ts(iw[:], ix[:, 16:24], 1 / 16, -7.5 / 16, A.mult, A.add))
+        f6 = do("v", [fl], ts(ix[:, 0:8], iw[:], 16.0, None, A.mult))
         n8 = do("v", [f6], tt(ix[:, 24:32], ix[:, 0:8], ix[:, 16:24], A.add))
         k["uo"] = [do("v", [n8], ts(lo[:, 48 + h:64:2], ix[:, 24:32], 16.0 * h, None, A.add)) for h in range(2)]
 
-    def update_list(t, k, x):
+    def place_scatter(t, k, x):
+        w = 1408 if x else 896
+        return do("v", [k["uo"], K["RC"], K["U%d" % t]], cp(B("UX" if x else "UL", t)[:, 0:w].indirect(B("lo16", t)[:, 48 + 8 * x:56 + 8 * x]), T.RC[:]))
+
+    def place_list(t, k, x, sc):
         U, tr, lo = B("UX" if x else "UL", t), B("trX" if x else "trU", t), B("lo16", t)
         w = 1408 if x else 896
-        sc = do("v", [k["uo"], K["RC"], K["U%d" % t]], cp(U[:, 0:w].indirect(lo[:, 48 + 8 * x:56 + 8 * x]), T.RC[:]))
         a = do("v", [sc, st["prev"]], trn(tr[:], U[:, w - 512:w]))
-        k["ux" if x else "ul"] = do("v", [a], cp(lo[:, 64 + 16 * x:80 + 16 * x], tr[:, 0:512:32]))
+        return do("v", [a], ts(lo[:, 64 + 16 * x:80 + 16 * x], tr[:, 0:512:32], 128.0, None, A.add))
 
     def renew(t, k, oq, os_, o):
         LW, LWs, XW, XWs, LN, LNs, NEW, lo = (B(n, t) for n in ("LW", "LWs", "XW", "XWs", "LN", "LNs", "NEW", "lo16"))
+        sc = place_scatter(t, k, 0)
         ad = [("aC%d" % t, 2 * arrive), k["AB"], k["cp"]["W"]]
         a1 = do("v", ad, cp(XW[:, 256:384].bitcast(U32), LW[:, 0:704].bitcast(U32).indirect(lo[:, 32:40])))
         a2 = do("s", ad, act(XWs[:, 256:384], LWs[:, 0:704].indirect(lo[:, 32:40]), AF.Copy))
         k["A"] = [a1, a2]
         dc = [do("p", [a1, a2], mm(T.pC[:, 512 * b:512 * b + 128], T.qE[:, 128 * b:128 * b + 128], T.sE[:, 128 * b:128 * b + 128],
                                    XW[:, 256:384], XWs[:, 256:384], False, True)) for b in range(4)]
-        update_list(t, k, 0)
+        ul = place_list(t, k, 0, sc)
         nw = []
         for b in range(4):
             i, h = T.pC[:, 512 * b + 64:512 * b + 128], NEW[:, b:256:4]
             nw.append(do("v", [dc[b]], cp(h, i)) if b % 2 == 0 else do("s", [dc[b], st["prev"]], act(h, i, AF.Copy)))
         qn = do("v", [nw, K["NEW"]], quant(LN[:, 256:384], LNs[:, 256:384], NEW[:]))
-        l1 = do("v", [qn, k["ul"], k["cp"]["L"]], cp(oq[:, o:o + 256].bitcast(U32), LN[:, 0:384].bitcast(U32).indirect(lo[:, 64:80])))
-        l2 = do("s", [qn, k["ul"], k["cp"]["L"]], act(os_[:, o:o + 256], LNs[:, 0:384].indirect(lo[:, 64:80]), AF.Copy))
+        l1 = do("v", [qn, ul, k["cp"]["L"]], cp(oq[:, o:o + 256].bitcast(U32), LN[:, 0:384].bitcast(U32).indirect(lo[:, 64:80])))
+        l2 = do("s", [qn, ul, k["cp"]["L"]], act(os_[:, o:o + 256], LNs[:, 0:384].indirect(lo[:, 64:80]), AF.Copy))
         return [l1, l2], nw
 
     def renew_dormant(t, k, oq, os_, o):
         XW, XWs, lo = B("XW", t), B("XWs", t), B("lo16", t)
-        update_list(t, k, 1)
-        xd = [k["ux"], k["cp"]["X"], k["A"]]
+        ux = place_list(t, k, 1, place_scatter(t, k, 1))
+        xd = [ux, k["cp"]["X"], k["A"]]
         x1 = do("v", xd, cp(oq[:, o + 256:o + 512].bitcast(U32), XW[:, 0:384].bitcast(U32).indirect(lo[:, 80:96])))
         x2 = do("s", xd, act(os_[:, o + 256:o + 512], XWs[:, 0:384].indirect(lo[:, 80:96]), AF.Copy))
         return [x1, x2]
@@ -414,12 +424,11 @@ def rank_program(g, core, T, topo):
             dma("y", [b], T.lw[t:t + 1, 16 * c:16 * c + 16], fo[32 * c:32 * c + 16, 2:3])
             dma("y", [b], T.sw[t:t + 1, 16 * c:16 * c + 16], fo[32 * c:32 * c + 16, 3:4])
 
-    ks = [{"sc": {}, "dd": {}, "cp": {}} for t in range(ROUNDS)]
+    ks = [{"sc": {}, "cp": {}} for t in range(ROUNDS)]
     k = ks[0]
     k["lt"], k["xt"] = q_l, q_x
     for ty in range(2):
         score(0, ty, (q_l, q_x)[ty], k)
-        ahead(0, ty, k)
         copies(0, ty, (q_l, q_x)[ty], k["cp"])
     for t in range(ROUNDS):
         k = ks[t]
@@ -435,7 +444,6 @@ def rank_program(g, core, T, topo):
             numbers(0, ks[0])
         merge_and_send(t, k)
         lists(t, k)
-        place_offsets(t, k)
         oq, os_, o = (T.FN, T.FNs, 0) if last else (B("SW", t + 1), B("SWs", t + 1), LB)
         lt, pc = renew(t, k, oq, os_, o)
         st["prev"] = [lt, pc, k["w"]]
@@ -444,9 +452,9 @@ def rank_program(g, core, T, topo):
             dma("y", lt, T.oc[:, 0:1024], T.FN[:, 0:256].bitcast(U8))
             for q in range(4):
                 dma("y", lt, T.osc[4 * q:4 * q + 4, 0:256], T.FNs[32 * q:32 * q + 4, 0:256])
-            xt = renew_dormant(t, k, oq, os_, o)
             yc = do("s", [my], act(T.yt[:], T.pA[:, 0:256], AF.Copy))
             dma("s", [yc], T.y[:], T.yt[:])
+            xt = renew_dormant(t, k, oq, os_, o)
             dma("y", xt, T.oc[:, 1024:2048], T.FN[:, 256:512].bitcast(U8))
             for q in range(4):
                 dma("y", xt, T.osc[4 * q:4 * q + 4, 256:512], T.FNs[32 * q:32 * q + 4, 256:512])
@@ -457,11 +465,9 @@ def rank_program(g, core, T, topo):
             copies(t + 1, 0, lt, n["cp"])
             score(t + 1, 0, lt, n)
             n["xt"] = xt = renew_dormant(t, k, oq, os_, o)
-            st["prev"].append(xt)
             copies(t + 1, 1, xt, n["cp"])
-            ahead(t + 1, 0, n)
             score(t + 1, 1, xt, n)
-            ahead(t + 1, 1, n)
+            st["prev"].append(xt)
     for s, n in cnt.items():
         if top.get(s, 0) < n:
             g.wait_ge(T.sem[s], n)

@@ -9,34 +9,33 @@ LB, XB = 192, 448
 
 SCRATCH = {
     "pA": ("psum", [128, 512], "float32"), "pB": ("psum", [128, 512], "float32"), "pC": ("psum", [128, 2048], "float32"),
-    "pD": ("psum", [128, 512], "float32"), "pE": ("psum", [128, 512], "float32"),
+    "pD": ("psum", [128, 1024], "float32"),
 }
 for _n, _w, _d in (
         ("t_lv", 1024, "bfloat16"), ("t_dm", 1024, "bfloat16"), ("t_nz", 1024, "bfloat16"), ("t_w", 512, "bfloat16"),
         ("u0", 4, "bfloat16"), ("z0", 4, "bfloat16"), ("uz", 1024, "bfloat16"), ("qU", 256, F8), ("sU", 256, "uint8"),
-        ("qW", 128, F8), ("sW", 128, "uint8"), ("ones", 512, "bfloat16"), ("zer", 128, "bfloat16"), ("half", 516, "bfloat16"),
+        ("qW", 128, F8), ("sW", 128, "uint8"), ("ones", 516, "bfloat16"), ("zer", 128, "bfloat16"),
         ("SS", 1024, "bfloat16"), ("SI", 1024, "bfloat16"), ("EM", 516, "bfloat16"), ("qS", 256, F8), ("sS", 256, "uint8"),
-        ("qI", 384, F8), ("sI", 384, "uint8"), ("qE", 512, F8), ("sE", 512, "uint8"), ("NZ", 256, F8), ("NZs", 256, "uint8"),
+        ("qI", 256, F8), ("sI", 256, "uint8"), ("qE", 512, F8), ("sE", 512, "uint8"), ("NZ", 256, F8), ("NZs", 256, "uint8"),
         ("pI", 1, "int32"), ("ii", 8, "int32"), ("fc", 8, "float32"), ("cc", 16, "float32"),
-        ("tin", 256, "float32"), ("Mneg", 256, "float32"), ("Mtri", 256, "float32"), ("Kn", 128, "bfloat16"), ("RC", 128, "bfloat16"),
-        ("sel", 4, "float32"), ("io8", 8, "float32"), ("kk8", 8, "float32"), ("io32", 32, "float32"), ("DG", 32, "bfloat16"),
-        ("sgt", 32, "float32"), ("VO", 64, "bfloat16"), ("OE", 6, "float32"), ("urow", 512, "bfloat16"),
+        ("tin", 256, "bfloat16"), ("Mneg", 256, "bfloat16"), ("Mtri", 256, "bfloat16"), ("Kn", 128, "bfloat16"), ("RC", 128, "bfloat16"),
+        ("sel", 4, "float32"), ("io8", 8, "float32"), ("dmp", 4, "float32"), ("io32", 32, "float32"), ("DG", 32, "bfloat16"),
+        ("sgt", 32, "float32"), ("VO", 64, "bfloat16"), ("OE", 8, "float32"), ("urow", 512, "bfloat16"),
         ("yt", 256, "float32"), ("FN", 512, F8), ("FNs", 512, "uint8")):
     SCRATCH[_n] = ("sbuf", [128, _w], _d)
-ONCE = ("yd", "DD", "Dc", "tr2", "trU", "trX", "qH", "sH", "H", "Gs", "sC", "Vc", "rk", "trA", "wk",
-        "VT", "XR", "R", "pw", "ow", "ix", "own", "NEW", "iw", "lo16", "qF", "sF", "qG", "sG")
+ONCE = ("yd", "yo", "DD", "Dc", "tr2", "trU", "qH", "sH", "H", "Gs", "sC", "Vc", "rk", "trA", "wk",
+        "VT", "XR", "R", "pw", "ow", "ix", "own", "NEW", "lo16", "qF", "sF", "qG", "sG")
 for _n, _w, _d in (
         ("SW", 704, F8), ("SWs", 704, "uint8"), ("LW", 704, F8), ("LWs", 704, "uint8"), ("XW", 384, F8), ("XWs", 384, "uint8"),
         ("LN", 384, F8), ("LNs", 384, "uint8"), ("PS", 64, F8), ("PSs", 64, "uint8"), ("NP", 128, F8), ("NPs", 128, "uint8"),
         ("qH", 128, F8), ("sH", 128, "uint8"), ("qF", 128, F8), ("sF", 128, "uint8"), ("qG", 128, F8), ("sG", 128, "uint8"),
-        ("H", 512, "bfloat16"), ("F", 2048, "bfloat16"), ("NEW", 512, "bfloat16"), ("VT", 96, "bfloat16"),
-        ("sC", 4, "float32"), ("Vc", 512, "float32"), ("yd", 512, "float32"), ("DD", 1024, "bfloat16"), ("rk", 4, "float32"),
-        ("trA", 128, "float32"), ("Gs", 64, "float32"), ("trG", 64, "float32"), ("dg", 4, "float32"), ("wk", 5, "float32"),
+        ("H", 512, "bfloat16"), ("F", 2560, "bfloat16"), ("NEW", 512, "bfloat16"), ("VT", 96, "bfloat16"),
+        ("sC", 4, "float32"), ("Vc", 512, "float32"), ("yd", 512, "float32"), ("yo", 512, "float32"), ("DD", 1024, "bfloat16"),
+        ("rk", 4, "float32"), ("trA", 128, "float32"), ("Gs", 64, "float32"), ("trG", 64, "float32"), ("dg", 4, "float32"), ("wk", 5, "float32"),
         ("own", 2, "float32"), ("landM", 6, "float32"), ("landP", 6, "float32"), ("XR", 256, "float32"), ("R", 256, "float32"),
-        ("Dc", 832, "bfloat16"), ("cn", 4, "float32"), ("pw", 8, "float32"), ("ow", 16, "float32"),
-        ("tr2", 256, "float32"), ("ix", 40, "float32"), ("UL", 896, "bfloat16"), ("UX", 1408, "bfloat16"),
-        ("trU", 512, "bfloat16"), ("trX", 512, "bfloat16"), ("lo16", 128, "uint16"), ("iw", 8, "int32"),
-        ("wl", 8, "float32"), ("fo", 4, "float32")):
+        ("Dc", 1040, "bfloat16"), ("cn", 4, "float32"), ("pw", 8, "float32"), ("ow", 16, "float32"),
+        ("tr2", 256, "float32"), ("ix", 40, "float32"), ("UL", 704, "bfloat16"),
+        ("trU", 512, "bfloat16"), ("lo16", 128, "uint16"), ("wl", 8, "float32"), ("fo", 4, "float32")):
     for _t in range(1 if _n in ONCE else ROUNDS):
         SCRATCH[_n + str(_t)] = ("sbuf", [128, _w], _d)
 
@@ -139,6 +138,9 @@ def rank_program(g, core, T, topo):
 
     U8, U32 = dt.uint8, dt.uint32
 
+    def after(p0):
+        return ("gc", cnt["gc"]) if p0 else None
+
     d_u = dma("s", [], T.u0[:], T.u[:, 0:4])
     d_z = dma("s", [], T.z0[:], T.z[:, 0:4])
     d_lv = dma("y", [], T.t_lv[:], T.lv[:])
@@ -151,26 +153,29 @@ def rank_program(g, core, T, topo):
     v_zer = do("v", [], fill(T.zer[:], 0.0))
     v_tin = do("v", [], fill(T.tin[:], TINY))
     bits = []
-    for c, m in enumerate((15, 32, 64, 63, 48, 112)):
+    for c, m in enumerate((15, 32, 64, 63, 48, 112, 16)):
         bits.append(do("v", [i_p], ts(T.ii[:, c:c + 1], T.pI[:, 0:1], m, None, A.bitwise_and)))
-    v_fc = do("v", bits, cp(T.fc[:, 0:6], T.ii[:, 0:6]))
+    v_fc = do("v", bits, cp(T.fc[:, 0:7], T.ii[:, 0:7]))
     v_one = do("v", [], fill(T.ones[:], 1.0))
     v_ss = do("v", [], fill(T.SS[:], 0.0))
-    v_half = do("v", [], fill(T.half[:], 0.5))
+    v_si = do("v", [], fill(T.SI[:], 0.0))
     i_mn = do("gc", [v_tin], lambda q: q.affine_select(T.Mneg[:], T.tin[:], [[0, 2], [1, 128]], A.is_ge, -TINY, 0, -1))
     i_mt = do("gc", [v_tin], lambda q: q.affine_select(T.Mtri[:], T.tin[:], [[0, 2], [-1, 128]], A.is_gt, -TINY, 0, 1))
     i_kn = do("gc", [], iota(T.Kn[:], [[16, 4], [0, 2], [1, 16]]))
     K["io32"] = do("gc", [], iota(T.io32[:], [[0, 2], [1, 16]]))
-    K["io8"] = do("gc", [], iota(T.io8[:], [[0, 2], [16, 4]]))
-    K["OE"] = do("gc", [], iota(T.OE[:], [[1, 3], [64, 2]], 30))
-    K["EM"] = do("gc", [v_half], lambda q: q.affine_select(T.EM[:], T.half[:], [[1, 516]], A.is_equal, 0.0, -3, -4))
-    K["RC"] = do("gc", [], iota(T.RC[:], [[16, 4], [0, 2], [1, 16]], 128))
-    K["ur"] = do("gc", [], iota(T.urow[:], [[16, 16], [0, 2], [1, 16]], -128))
-    for t in range(ROUNDS):
-        K["U%d" % t] = [dma("y", [K["ur"]], B("UL", t)[:, 384:896], T.urow[:]), dma("y", [K["ur"]], B("UX", t)[:, 896:1408], T.urow[:])]
+    K["io8"] = do("gc", [], iota(T.io8[:], [[16, 8]]))
+    K["OE"] = [do("gc", [], iota(T.OE[:, 0:6], [[1, 3], [64, 2]], 542)), do("gc", [], iota(T.OE[:, 6:8], [[64, 2]], 32))]
+    K["EM"] = do("gc", [v_one], lambda q: q.affine_select(T.EM[:], T.ones[:], [[1, 516]], A.is_equal, 0.0, -3, -4))
+    K["SI"] = [v_si]
+    for p0, p1, at, end, step, c in ((0, 128, 0, 512, 32, 1), (0, 128, 1, 512, 32, 1), (0, 128, 2, 512, 32, 1), (0, 64, 4, 512, 32, 1), (0, 64, 5, 512, 64, 2),
+                                     (0, 64, 37, 512, 64, 1), (0, 64, 6, 512, 64, 1), (0, 64, 38, 512, 128, 1), (0, 1, 15, 512, 32, 1), (0, 64, 526, 1024, 128, 1),
+                                     (64, 128, 8, 512, 32, 1), (64, 128, 9, 512, 64, 2), (64, 128, 41, 512, 64, 1), (64, 128, 10, 512, 32, 1),
+                                     (64, 128, 558, 1024, 128, 1), (64, 65, 15, 512, 32, 1)):
+        K["SI"].append(do("gc", [v_si, after(p0)], iota(T.SI[p0:p1, at:end:step], [[0, len(range(at, end, step))]], c)))
+    K["177"] = [do("gc", [K["SI"]], iota(B("Dc", 0)[:, 208 * j + 193:208 * j + 194], [[0, 1]], 177)) for j in range(2)]
     F_ = lambda c: T.fc[:, c:c + 1]
     C_ = lambda c: T.cc[:, c:c + 1]
-    SG, M1, M0, SM1, SM0, AQ, CD, H1, ML, MD = range(10)
+    SG, M1, M0, SM1, SM0, AQ, CD, H1, EV, OD, OB = range(11)
 
     SW0, SWs0 = B("SW", 0), B("SWs", 0)
     uz, cst = [], []
@@ -192,33 +197,46 @@ def rank_program(g, core, T, topo):
         sst.append(do("s", [cst], act(T.SS[:, 512 + 256 * t + b:768 + 256 * t:4], T.ones[:, 0:64], AF.Copy, scale=hi)))
     K["DG"] = do("v", [K["io32"], v_fc], ts(T.DG[:], T.io32[:], F_(0), None, A.is_equal))
     K["sel"] = do("v", [K["io8"]], ts(T.sel[:], T.io8[:, 0:4], F_(4), None, A.is_equal))
-    K["F"] = [do("v", [], fill(B("F", 0)[:, 0:512], 0.0))]
-    qi = [do("v", [v_one], quant(T.qI[:, 0:128], T.sI[:, 0:128], T.ones[:]))]
     v_qs = do("v", sst, quant(T.qS[:], T.sS[:], T.SS[:]))
 
     def consts_s():
-        for c, src, a, b in ((M1, 1, 1 / 32, 0.0), (M0, 1, -1 / 32, 1.0), (CD, 2, 4.0, float(LB)), (ML, 2, -1 / 64, 1.0), (MD, 2, 1 / 64, 0.0)):
+        for c, src, a, b in ((M1, 1, 1 / 32, 0.0), (M0, 1, -1 / 32, 1.0), (CD, 2, 4.0, float(LB)),
+                             (EV, 6, -1 / 16, 1.0), (OD, 6, 1 / 16, 0.0), (OB, 6, -16.0, 0.0)):
             cst.append(do("s", [v_fc], act(C_(c), F_(src), scale=a, bias=b)))
         cst.append(do("s", [cst], act(C_(SM1), C_(M1), scale=C_(SG))))
         cst.append(do("s", [], act(C_(SM0), C_(M0), scale=C_(SG))))
         K["sgt"] = do("s", [v_one], act(T.sgt[:], T.ones[:, 0:32], AF.Copy, scale=C_(SG)))
         Dc = B("Dc", 0)
-        K["Dc"] = [do("s", [], act(Dc[:, 208 * j + 192:208 * j + 193], F_(3), scale=4.0, bias=-30.0)) for j in (0, 1, 3)]
-        K["SI"] = [do("s", [cst], act(T.SI[:, 512 * j:512 * j + 512], T.ones[:], AF.Copy, scale=C_(ML + j))) for j in range(2)]
+        K["Dc"] = K["177"] + [do("s", [], act(Dc[:, 816:817], F_(3), scale=4.0, bias=-30.0))]
+        for j in range(2):
+            K["Dc"].append(do("s", [], act(Dc[:, 208 * j + 192:208 * j + 193], F_(3), scale=2.0)))
         K["wk"] = do("v", [], fill(B("wk", 0)[:, 4:5], -7.5))
         K["VTc"] = do("v", [K["DG"], cst], ts(B("VT", 0)[:, 64:96], T.DG[:], C_(CD), None, A.mult))
 
+    def slots(t):
+        F = B("F", t)
+        z = do("v", [], fill(F[:, 0:1024], 0.0))
+        return [z, do("gc", [z], iota(F[0:64, 515:1024:4], [[0, 4], [0, 2], [1, 16]])),
+                do("gc", [z, after(64)], iota(F[64:128, 515:1024:4], [[16, 4], [0, 2], [0, 16]]))]
+
     def consts_v():
-        qi.append(do("v", [K["SI"]], quant(T.qI[:, 128:384], T.sI[:, 128:384], T.SI[:])))
+        K["F"] = [slots(0)]
         K["VO"] = [do("v", [K["DG"]], ts(T.VO[:, 32 * s:32 * s + 32], T.DG[:], 64.0 * (s + 1), None, A.mult)) for s in range(2)]
         K["nz"] = do("v", [d_nz], quant(T.NZ[:], T.NZs[:], T.t_nz[:]))
-        K["kk8"] = do("v", [K["io8"]], ts(T.kk8[:], T.io8[:], F_(0), None, A.add))
+        K["dmp"] = do("v", [K["io8"]], ts(T.dmp[:], T.io8[:, 0:8:2], F_(0), None, A.add))
         K["qE"] = [do("v", [K["EM"]], quant(T.qE[:, 128 * b:128 * b + 128], T.sE[:, 128 * b:128 * b + 128], T.EM[:, 3 - b:515 - b])) for b in range(4)]
         K["np"] = [do("v", [d_nz], quant(B("NP", 0)[:], B("NPs", 0)[:], T.t_nz[:, 0:512]))]
         K["NEW"] = do("v", [], fill(B("NEW", 0)[:, 256:512], 0.0))
+        K["qI"] = do("v", K["SI"], quant(T.qI[:], T.sI[:], T.SI[:]))
+
+    def rows():
+        K["RC"] = do("gc", K["F"][0], iota(T.RC[:], [[16, 4], [0, 2], [1, 16]], 128))
+        K["ur"] = do("gc", [], iota(T.urow[:], [[16, 16], [0, 2], [1, 16]], -128))
+        for t in range(ROUNDS):
+            K["U%d" % t] = dma("y", [K["ur"]], B("UL", t)[:, 192:704], T.urow[:])
 
     def consts_2():
-        K["F"].append(do("v", [], fill(B("F", 1)[:, 0:512], 0.0)))
+        K["F"].append(slots(1))
         K["qW"] = do("v", [d_w], quant(T.qW[:], T.sW[:], T.t_w[:]))
         K["np"].append(do("v", [d_nz], quant(B("NP", 1)[:], B("NPs", 1)[:], T.t_nz[:, 0:512])))
 
@@ -235,13 +253,13 @@ def rank_program(g, core, T, topo):
         SW, SWs, sC, Vc, yd = (B(n, t) for n in ("SW", "SWs", "sC", "Vc", "yd"))
         pr, w = st["prev"], LB + 256 * ty
         qu, su = T.qU[:, 128 * ty:128 * ty + 128], T.sU[:, 128 * ty:128 * ty + 128]
-        pX = (T.pA, T.pB)[ty]
+        pX, pY = ((T.pA, T.pC), (T.pB, T.pD))[ty]
         r = do("p", [q_u[ty], tk, pr], mm(pX[:, 0:256], qu, su, SW[:, w:w + 256], SWs[:, w:w + 256]))
         for h in range(2):
-            c = do("p", [], mm(T.pC[:, 512 * (2 * ty + h):512 * (2 * ty + h) + 128], SW[:, w + 128 * h:w + 128 * h + 128],
+            c = do("p", [], mm(pY[:, 512 * h:512 * h + 128], SW[:, w + 128 * h:w + 128 * h + 128],
                                SWs[:, w + 128 * h:w + 128 * h + 128], qu, su))
         ra = do("s", [r, pr], act(Vc[:, 256 * ty:256 * ty + 256], pX[:, 0:256], AF.Abs))
-        ca = do("s", [c], act(sC[:, 2 * ty:2 * ty + 2], T.pC[:, 1024 * ty:1024 * ty + 1024:512], AF.Abs))
+        ca = do("s", [c], act(sC[:, 2 * ty:2 * ty + 2], pY[:, 0:1024:512], AF.Abs))
         ys = [do("s", [ca, ra], act(yd[:, 256 * ty + 128 * h:256 * ty + 128 * h + 128], Vc[:, 256 * ty + 128 * h:256 * ty + 128 * h + 128],
                                     bias=sC[:, 2 * ty + h:2 * ty + h + 1], scale=-1.0)) for h in range(2)]
         k["sc"][ty] = (ca, ra, ys)
@@ -266,13 +284,14 @@ def rank_program(g, core, T, topo):
         def total(b, dd):
             r[b] = do("s", dd, act(DD[:, 256 * b:256 * b + 256], DD[:, 256 * b:256 * b + 256], accum_out=rk[:, b:b + 1]))
 
-        dd = ahead(t, 0, k)
-        total(0, dd)
-        total(1, dd)
-        dd = ahead(t, 1, k)
-        total(2, dd)
-        r[3] = do("v", dd, red(rk[:, 3:4], DD[:, 768:1024]))
-        hs = [hot(b) for b in (0, 1, 3, 2)]
+        f, l = k["first"], 1 - k["first"]
+        dd = ahead(t, f, k)
+        total(2 * f, dd)
+        total(2 * f + 1, dd)
+        dd = ahead(t, l, k)
+        total(2 * l, dd)
+        r[2 * l + 1] = do("v", dd, red(rk[:, 2 * l + 1:2 * l + 2], DD[:, 512 * l + 256:512 * l + 512]))
+        hs = [hot(b) for b in (2 * f, 2 * f + 1, 2 * l + 1, 2 * l)]
         qh = do("v", hs, quant(B("qH", t)[:], B("sH", t)[:], H[:]))
         do("p", [qh, v_qs, pr], mm(T.pD[:, 0:128], T.qS[:, 0:128], T.sS[:, 0:128], B("qH", t)[:], B("sH", t)[:], True, False))
         m = do("p", [], mm(T.pD[:, 0:128], T.qS[:, 128:256], T.sS[:, 128:256], B("qH", t)[:], B("sH", t)[:], False, True))
@@ -297,7 +316,7 @@ def rank_program(g, core, T, topo):
         v0 = do("v", [lo_], ts(VT[:, 0:32], T.DG[:], dg[:, 2:3], None, A.mult))
         k["VT"] = [v0, v1, K["VTc"]]
 
-    def before(s, q, t, deps, at, x_of):
+    def before(s, q, t, deps, at, x_of, neg=None):
         R, Dc, out, seg = B("R", t), B("Dc", t), [], []
         for x in x_of:
             op = A.is_le if (others + [rank])[x] < q else A.is_lt
@@ -306,12 +325,15 @@ def rank_program(g, core, T, topo):
             else:
                 seg.append([64 * x, 64 * x + 64, op])
         for (c0, c1, op) in seg:
-            out.append(do("v", deps, ts(Dc[:, at:at + c1 - c0], R[:, c0:c1], s, 4.0, op, A.mult)))
+            if neg is None:
+                out.append(do("v", deps, ts(Dc[:, at:at + c1 - c0], R[:, c0:c1], s, 4.0, op, A.mult)))
+            else:
+                out.append(do("s", deps, act(Dc[:, at:at + c1 - c0], neg[0][:, neg[1] + c0:neg[1] + c1], AF.Sign, bias=TINY if op == A.is_le else -TINY)))
             at += c1 - c0
         return out
 
     def merge_and_send(t, k):
-        LM, XR, R, Dc, cn, pw, lo, own, F, ow = (B(n, t) for n in ("landM", "XR", "R", "Dc", "cn", "pw", "lo16", "own", "F", "ow"))
+        LM, XR, R, Dc, cn, pw, lo, own, F, ow, yo = (B(n, t) for n in ("landM", "XR", "R", "Dc", "cn", "pw", "lo16", "own", "F", "ow", "yo"))
         aM = ("aM%d" % t, arrive)
         xs = []
         for j in range(6):
@@ -323,17 +345,20 @@ def rank_program(g, core, T, topo):
         d = before(own[:, 0:1], rank, t, [k["R"], k["s"], st["prev"]], 624, range(3))
         k["cn"] = c = do("v", [d, K["Dc"]], red(cn[:, 3:4], Dc[:, 624:817]))
         fl = do("v", [c], ts(pw[:, 0:1], cn[:, 3:4], R64, R64, A.add, A.subtract))
-        of = do("v", [fl, K["OE"]], ts(lo[:, 4:10], T.OE[:], pw[:, 0:1], cn[:, 3:4], A.add, A.add))
-        sc = do("v", [of, k["VT"], K["F"][t]], cp(F[:, 0:2048].indirect(lo[:, 4:10]), B("VT", t)[:]))
-        k["qF"] = do("v", [sc], quant(B("qF", t)[:], B("sF", t)[:], F[:, 0:512]))
-        m = do("p", [k["qF"], qi[0], st["prev"]], mm(T.pE[:, 0:128], T.qI[:, 0:128], T.sI[:, 0:128], B("qF", t)[:], B("sF", t)[:]))
-        k["own2"] = do("p", [qi, k["sc"][1][1]], mm(T.pB[:, 0:128], B("qF", t)[:], B("sF", t)[:], T.qI[:, 192:320], T.sI[:, 192:320]))
+        of = do("v", [fl, K["OE"]], ts(lo[:, 4:10], T.OE[:, 0:6], pw[:, 0:1], cn[:, 3:4], A.add, A.add))
+        sc = do("v", [of, k["VT"], K["F"][t]], cp(F[:, 0:2560].indirect(lo[:, 4:10]), B("VT", t)[:]))
+        k["qF"] = do("v", [sc], quant(B("qF", t)[:], B("sF", t)[:], F[:, 512:1024]))
+        m = do("p", [k["qF"], K["qI"], st["prev"]], mm(T.pD[:, 512:640], T.qI[:, 0:128], T.sI[:, 0:128], B("qF", t)[:], B("sF", t)[:]))
+        k["own2"] = do("p", [k["sc"][1][1]], mm(T.pB[:, 0:128], B("qF", t)[:], B("sF", t)[:], T.qI[:, 0:128], T.sI[:, 0:128]))
+        o2 = [do("s", [aM, cst], act(ow[:, s:s + 1], LM[:, 2 * s:2 * s + 1], scale=C_(SM0))) for s in range(2)]
         for s in range(2):
-            a = do("s", [aM, cst], act(ow[:, s:s + 1], LM[:, 2 * s:2 * s + 1], scale=C_(SM0)))
-            k["s2"] = do("s", [a], act(ow[:, 8 + s:9 + s], LM[:, 2 * s + 1:2 * s + 2], scale=C_(SM1), bias=ow[:, s:s + 1]))
-        a = do("v", [m], trn(B("tr2", t)[:, 0:128], T.pE[:, 0:128]))
+            o2[s] = do("s", [o2[s]], act(ow[:, 8 + s:9 + s], LM[:, 2 * s + 1:2 * s + 2], scale=C_(SM1), bias=ow[:, s:s + 1]))
+        ys = [do("s", [o2[s], k["R"], k["Ro"]], act(yo[:, 256 * s + 64 - 64 * s:256 * s + 256], R[:, 64 - 64 * s:256], bias=ow[:, 8 + s:9 + s], scale=-1.0)) for s in range(2)]
+        sg = [before(None, others[s], t, [ys[s], st["prev"]], 208 * s, [x for x in range(4) if x != s], (yo, 256 * s)) for s in range(2)]
+        k["c2"] = [do("s", [sg[s], K["Dc"]], act(Dc[:, 416 + 416 * s:610 + 416 * s], Dc[:, 208 * s:208 * s + 194], scale=2.0, accum_out=cn[:, s:s + 1])) for s in range(2)]
+        a = do("v", [m], trn(B("tr2", t)[:, 0:128], T.pD[:, 512:640]))
         of = do("v", [a], ts(lo[:, 10:14], B("tr2", t)[:, 0:128:32], float(LB), 703.0, A.max, A.min))
-        k["pE"] = [a, of]
+        k["tr2"] = a
         pd = [of, k["lt"], k["xt"]]
         ps = do("v", pd, cp(B("PS", t)[:].bitcast(U32), B("SW", t)[:, 0:704].bitcast(U32).indirect(lo[:, 10:14])))
         pss = do("s", pd, act(B("PSs", t)[:], B("SWs", t)[:, 0:704].indirect(lo[:, 10:14]), AF.Copy))
@@ -343,77 +368,62 @@ def rank_program(g, core, T, topo):
         send([pss], "aC%d" % t, B("PSs", t)[:, 0:64], lambda s: LWs[:, o[s]:o[s] + 64])
 
     def lists(t, k):
-        cn, pw, ow, lo, F, iw, ix, tr2, Dc, wl = (B(n, t) for n in ("cn", "pw", "ow", "lo16", "F", "iw", "ix", "tr2", "Dc", "wl"))
-        dep = [k["s2"], k["R"], k["Ro"], k["cn"], st["prev"]]
-        d0 = before(ow[:, 8:9], others[0], t, dep, 0, (1, 2, 3))
-        c0 = do("s", [d0, K["Dc"]], act(Dc[:, 0:193], Dc[:, 0:193], accum_out=cn[:, 0:1]))
-        d1 = before(ow[:, 9:10], others[1], t, dep, 208, (0, 2, 3))
-        c1 = do("v", [d1, K["Dc"]], red(cn[:, 1:2], Dc[:, 208:401]))
-        fl = do("v", [c0, c1], ts(pw[:, 2:4], cn[:, 0:2], R64, R64, A.add, A.subtract))
-        of = [do("v", [fl], ts(lo[:, 16 + 2 * s:18 + 2 * s], T.OE[:, 4:6], pw[:, 2 + s:3 + s], cn[:, s:s + 1], A.add, A.add)) for s in range(2)]
-        sc = do("v", [of, K["VO"], k["qF"]], cp(F[:, 0:2048].indirect(lo[:, 16:20]), T.VO[:]))
+        cn, pw, lo, F, ix, tr2, wl, UL, trU = (B(n, t) for n in ("cn", "pw", "lo16", "F", "ix", "tr2", "wl", "UL", "trU"))
+        tok = k["tr2"]
+        row = lambda r, g=0: tr2[:, 128 * g + r:128 * g + 128:32]
+        nl = do("v", [tok], cp(lo[:, 24:28], row(25)))
+        e = [do("s", [tok, cst], act(ix[:, 0:4], row(1), AF.Copy, scale=C_(EV))),
+             do("s", [tok, cst], act(ix[:, 4:8], row(2), scale=C_(OD), bias=C_(OB)))]
+        fl = do("v", k["c2"], ts(pw[:, 2:4], cn[:, 0:2], R64, R64, A.add, A.subtract))
+        nd_ = [nl, K["nz"], K["np"][t], st["prev"]]
+        k["np"] = [do("s", nd_, act(B("NPs", t)[:, 64:128], T.NZs[:, 0:256].indirect(lo[:, 24:28]), AF.Copy))]
+        of = [do("v", [fl, K["OE"]], ts(lo[:, 16 + 2 * s:18 + 2 * s], T.OE[:, 6:8], pw[:, 2 + s:3 + s], cn[:, s:s + 1], A.add, A.add)) for s in range(2)]
+        u1 = do("v", e, tt(ix[:, 8:12], ix[:, 0:4], ix[:, 4:8], A.max))
+        sc = do("v", [of, K["VO"], k["qF"]], cp(F[:, 0:2560].indirect(lo[:, 16:20]), T.VO[:]))
+        u2 = do("v", [u1, K["dmp"]], tt(ix[:, 12:16], ix[:, 8:12], T.dmp[:], A.max))
         qg = do("v", [sc], quant(B("qG", t)[:], B("sG", t)[:], F[:, 0:512]))
-        ml = do("p", [qg, qi, k["trA"]], mm(T.pD[:, 0:128], T.qI[:, 128:256], T.sI[:, 128:256], B("qG", t)[:], B("sG", t)[:]))
-        md = do("p", [k["pE"]], mm(T.pE[:, 0:128], T.qI[:, 256:384], T.sI[:, 256:384], B("qG", t)[:], B("sG", t)[:]))
-        w1 = do("s", [k["own2"]], act(wl[:, 0:2], T.pB[:, 0:128:64], AF.Sign))
+        do("p", [k["qF"], k["trA"]], mm(T.pD[:, 0:128], T.qI[:, 0:128], T.sI[:, 0:128], B("qF", t)[:], B("sF", t)[:], True, False))
+        mo = do("p", [qg], mm(T.pD[:, 0:128], T.qI[:, 128:256], T.sI[:, 128:256], B("qG", t)[:], B("sG", t)[:], False, True))
+        uo = [do("v", [u2], ts(lo[:, 48 + h:56:2], ix[:, 12:16], 16.0 * h, None, A.add)) for h in range(2)]
+        k["np"].append(do("v", nd_, cp(B("NP", t)[:, 64:128].bitcast(U32), T.NZ[:, 0:256].bitcast(U32).indirect(lo[:, 24:28]))))
+        k["dn"] = [do("p", [k["np"], K["qE"], st["prev"]], mm(T.pC[:, 512 * b:512 * b + 128], T.qE[:, 128 * b:128 * b + 128], T.sE[:, 128 * b:128 * b + 128],
+                                                              B("NP", t)[:], B("NPs", t)[:], True, False)) for b in range(4)]
+        w1 = do("s", [k["own2"]], act(wl[:, 0:2], T.pB[:, 9:11], AF.Sign))
         k["w"] = []
         for j in range(2):
             w2 = do("s", [w1], act(wl[:, 2 + j:3 + j], wl[:, j:j + 1], AF.Copy, scale=256.0 * rank - (LB, XB)[j]))
-            k["w"].append(do("s", [w2], act(wl[:, 4 + j:5 + j], T.pB[:, 64 * j:64 * j + 1], bias=wl[:, 2 + j:3 + j])))
-        a = do("v", [ml, k["pE"]], trn(tr2[:, 0:128], T.pD[:, 0:128]))
-        b = do("v", [md], trn(tr2[:, 128:256], T.pE[:, 0:128]))
-        nl = do("v", [a], ts(lo[:, 24:28], tr2[:, 0:128:32], -float(LB), 255.0, A.add, A.min))
-        g8 = do("v", [a, b], ts(ix[:, 0:8], tr2[:, 0:256:32], float(LB), None, A.is_lt))
-        nd_ = [nl, K["nz"], K["np"][t], st["prev"]]
-        k["np"] = [do("v", nd_, cp(B("NP", t)[:, 64:128].bitcast(U32), T.NZ[:, 0:256].bitcast(U32).indirect(lo[:, 24:28]))),
-                   do("s", nd_, act(B("NPs", t)[:, 64:128], T.NZs[:, 0:256].indirect(lo[:, 24:28]), AF.Copy))]
-        k8 = do("v", [g8, K["kk8"]], tt(ix[:, 8:16], ix[:, 0:8], T.kk8[:], A.mult))
-        i8 = do("v", [k8], tt(ix[:, 16:24], tr2[:, 0:256:32], ix[:, 8:16], A.add))
-        k["AB"] = do("v", [i8], cp(lo[:, 32:40], ix[:, 16:24]))
+            k["w"].append(do("s", [w2], act(wl[:, 4 + j:5 + j], T.pB[:, 9 + j:10 + j], bias=wl[:, 2 + j:3 + j])))
         send([k["w"]], "aP%d" % t, wl[:, 4:6], lambda s: B("landP", t)[:, 2 * s:2 * s + 2])
-        k["dn"] = [do("p", [k["np"], K["qE"], st["prev"]], mm(T.pC[:, 512 * b:512 * b + 128], T.qE[:, 128 * b:128 * b + 128], T.sE[:, 128 * b:128 * b + 128],
-                                                              B("NP", t)[:], B("NPs", t)[:], True, False)) for b in range(4)]
-        fl = do("v", [i8], ts(iw[:], ix[:, 16:24], 1 / 16, -7.5 / 16, A.mult, A.add))
-        f6 = do("v", [fl], ts(ix[:, 0:8], iw[:], 16.0, None, A.mult))
-        n8 = do("v", [f6], tt(ix[:, 24:32], ix[:, 0:8], ix[:, 16:24], A.add))
-        k["uo"] = [do("v", [n8], ts(lo[:, 48 + h:64:2], ix[:, 24:32], 16.0 * h, None, A.add)) for h in range(2)]
-
-    def place_scatter(t, k, x):
-        w = 1408 if x else 896
-        return do("v", [k["uo"], K["RC"], K["U%d" % t]], cp(B("UX" if x else "UL", t)[:, 0:w].indirect(B("lo16", t)[:, 48 + 8 * x:56 + 8 * x]), T.RC[:]))
-
-    def place_list(t, k, x, sc):
-        U, tr, lo = B("UX" if x else "UL", t), B("trX" if x else "trU", t), B("lo16", t)
-        w = 1408 if x else 896
-        a = do("v", [sc, st["prev"]], trn(tr[:], U[:, w - 512:w]))
-        return do("v", [a], ts(lo[:, 64 + 16 * x:80 + 16 * x], tr[:, 0:512:32], 128.0, None, A.add))
+        us = do("v", [uo, K["RC"], K["U%d" % t]], cp(UL[:, 0:704].indirect(lo[:, 48:56]), T.RC[:]))
+        a = do("v", [mo], trn(tr2[:, 128:256], T.pD[:, 0:128]))
+        m = [do("v", [a], tt(ix[:, 16 + 4 * j:20 + 4 * j], row(9 + j), row(3 + 8 * j, 1), A.max)) for j in range(2)]
+        k["AB"] = do("v", m, cp(lo[:, 32:40], ix[:, 16:24]))
+        a = do("v", [us], trn(trU[:], UL[:, 192:704]))
+        k["pl"] = [do("v", [a], ts(lo[:, 64 + 16 * x:80 + 16 * x], trU[:, 16 * x:512:32], 128.0, None, A.add)) for x in range(2)]
 
     def renew(t, k, oq, os_, o):
         LW, LWs, XW, XWs, LN, LNs, NEW, lo = (B(n, t) for n in ("LW", "LWs", "XW", "XWs", "LN", "LNs", "NEW", "lo16"))
-        sc = place_scatter(t, k, 0)
         ad = [("aC%d" % t, 2 * arrive), k["AB"], k["cp"]["W"]]
-        a1 = do("v", ad, cp(XW[:, 256:384].bitcast(U32), LW[:, 0:704].bitcast(U32).indirect(lo[:, 32:40])))
         a2 = do("s", ad, act(XWs[:, 256:384], LWs[:, 0:704].indirect(lo[:, 32:40]), AF.Copy))
-        k["A"] = [a1, a2]
+        a1 = do("v", ad, cp(XW[:, 256:384].bitcast(U32), LW[:, 0:704].bitcast(U32).indirect(lo[:, 32:40])))
         dc = [do("p", [a1, a2], mm(T.pC[:, 512 * b:512 * b + 128], T.qE[:, 128 * b:128 * b + 128], T.sE[:, 128 * b:128 * b + 128],
                                    XW[:, 256:384], XWs[:, 256:384], False, True)) for b in range(4)]
-        ul = place_list(t, k, 0, sc)
+        xd = [k["pl"], k["cp"]["X"], a1, a2]
+        x1 = do("v", xd, cp(oq[:, o + 256:o + 512].bitcast(U32), XW[:, 0:384].bitcast(U32).indirect(lo[:, 80:96])))
+        x2 = do("s", xd, act(os_[:, o + 256:o + 512], XWs[:, 0:384].indirect(lo[:, 80:96]), AF.Copy))
         nw = []
         for b in range(4):
             i, h = T.pC[:, 512 * b + 64:512 * b + 128], NEW[:, b:256:4]
-            nw.append(do("v", [dc[b]], cp(h, i)) if b % 2 == 0 else do("s", [dc[b], st["prev"]], act(h, i, AF.Copy)))
+            nw.append(do("v", [dc[b]], ts(h, i, 0.5, None, A.mult)) if b % 2 else do("s", [dc[b], st["prev"]], act(h, i, AF.Copy, scale=0.5)))
         qn = do("v", [nw, K["NEW"]], quant(LN[:, 256:384], LNs[:, 256:384], NEW[:]))
-        l1 = do("v", [qn, ul, k["cp"]["L"]], cp(oq[:, o:o + 256].bitcast(U32), LN[:, 0:384].bitcast(U32).indirect(lo[:, 64:80])))
-        l2 = do("s", [qn, ul, k["cp"]["L"]], act(os_[:, o:o + 256], LNs[:, 0:384].indirect(lo[:, 64:80]), AF.Copy))
-        return [l1, l2], nw
+        return qn, nw, [x1, x2]
 
-    def renew_dormant(t, k, oq, os_, o):
-        XW, XWs, lo = B("XW", t), B("XWs", t), B("lo16", t)
-        ux = place_list(t, k, 1, place_scatter(t, k, 1))
-        xd = [ux, k["cp"]["X"], k["A"]]
-        x1 = do("v", xd, cp(oq[:, o + 256:o + 512].bitcast(U32), XW[:, 0:384].bitcast(U32).indirect(lo[:, 80:96])))
-        x2 = do("s", xd, act(os_[:, o + 256:o + 512], XWs[:, 0:384].indirect(lo[:, 80:96]), AF.Copy))
-        return [x1, x2]
+    def renew_live(t, k, qn, oq, os_, o):
+        LN, LNs, lo = B("LN", t), B("LNs", t), B("lo16", t)
+        ld = [qn, k["pl"], k["cp"]["L"]]
+        l2 = do("s", ld, act(os_[:, o:o + 256], LNs[:, 0:384].indirect(lo[:, 64:80]), AF.Copy))
+        l1 = do("v", ld, cp(oq[:, o:o + 256].bitcast(U32), LN[:, 0:384].bitcast(U32).indirect(lo[:, 64:80])))
+        return [l1, l2]
 
     def numbers(t, k):
         LP, fo, wl = B("landP", t), B("fo", t), B("wl", t)
@@ -426,7 +436,7 @@ def rank_program(g, core, T, topo):
 
     ks = [{"sc": {}, "cp": {}} for t in range(ROUNDS)]
     k = ks[0]
-    k["lt"], k["xt"] = q_l, q_x
+    k["lt"], k["xt"], k["first"] = q_l, q_x, 0
     for ty in range(2):
         score(0, ty, (q_l, q_x)[ty], k)
         copies(0, ty, (q_l, q_x)[ty], k["cp"])
@@ -439,35 +449,36 @@ def rank_program(g, core, T, topo):
         prepare(t, k)
         if t == 0:
             consts_v()
+            rows()
         else:
             consts_2()
             numbers(0, ks[0])
         merge_and_send(t, k)
         lists(t, k)
         oq, os_, o = (T.FN, T.FNs, 0) if last else (B("SW", t + 1), B("SWs", t + 1), LB)
-        lt, pc = renew(t, k, oq, os_, o)
-        st["prev"] = [lt, pc, k["w"]]
+        qn, nw, xt = renew(t, k, oq, os_, o)
         if last:
+            lt = renew_live(t, k, qn, oq, os_, o)
+            dma("y", xt, T.oc[:, 1024:2048], T.FN[:, 256:512].bitcast(U8))
+            for q in range(4):
+                dma("y", xt, T.osc[4 * q:4 * q + 4, 256:512], T.FNs[32 * q:32 * q + 4, 256:512])
             my = do("p", [lt, K["qW"], k["sc"][0][1]], mm(T.pA[:, 0:256], T.qW[:], T.sW[:], T.FN[:, 0:256], T.FNs[:, 0:256]))
             dma("y", lt, T.oc[:, 0:1024], T.FN[:, 0:256].bitcast(U8))
             for q in range(4):
                 dma("y", lt, T.osc[4 * q:4 * q + 4, 0:256], T.FNs[32 * q:32 * q + 4, 0:256])
             yc = do("s", [my], act(T.yt[:], T.pA[:, 0:256], AF.Copy))
             dma("s", [yc], T.y[:], T.yt[:])
-            xt = renew_dormant(t, k, oq, os_, o)
-            dma("y", xt, T.oc[:, 1024:2048], T.FN[:, 256:512].bitcast(U8))
-            for q in range(4):
-                dma("y", xt, T.osc[4 * q:4 * q + 4, 256:512], T.FNs[32 * q:32 * q + 4, 256:512])
             numbers(t, k)
         else:
             n = ks[t + 1]
-            n["lt"] = lt
+            n["xt"], n["first"] = xt, 1
+            st["prev"] = [xt, nw, k["w"]]
+            copies(t + 1, 1, xt, n["cp"])
+            n["lt"] = lt = renew_live(t, k, qn, oq, os_, o)
+            score(t + 1, 1, xt, n)
             copies(t + 1, 0, lt, n["cp"])
             score(t + 1, 0, lt, n)
-            n["xt"] = xt = renew_dormant(t, k, oq, os_, o)
-            copies(t + 1, 1, xt, n["cp"])
-            score(t + 1, 1, xt, n)
-            st["prev"].append(xt)
+            st["prev"] = [lt, xt, nw, k["w"]]
     for s, n in cnt.items():
         if top.get(s, 0) < n:
             g.wait_ge(T.sem[s], n)

from concourse.bass import DstId, RemoteDMATransfer
from concourse.mybir import dt, AluOpType as A, AxisListType, ActivationFunctionType as AF

F8 = "float8_e4m3fn_x4"
TINY = 2.0 ** -118
R16, R64 = 1.5 * 2.0 ** 27, 1.5 * 2.0 ** 29
ROUNDS = 2
LB, XB = 192, 448

SCRATCH = {
    "pA": ("psum", [128, 512], "float32"), "pB": ("psum", [128, 512], "float32"), "pC": ("psum", [128, 2048], "float32"),
    "pD": ("psum", [128, 1024], "float32"),
}
for _n, _w, _d in (
        ("t_lv", 1024, "bfloat16"), ("t_dm", 1024, "bfloat16"), ("t_nz", 1024, "bfloat16"), ("t_w", 512, "bfloat16"),
        ("u0", 4, "bfloat16"), ("z0", 4, "bfloat16"), ("uz", 1024, "bfloat16"), ("qU", 256, F8), ("sU", 256, "uint8"),
        ("qW", 128, F8), ("sW", 128, "uint8"), ("ones", 516, "bfloat16"), ("zer", 128, "bfloat16"),
        ("SS", 1024, "bfloat16"), ("SI", 1024, "bfloat16"), ("EM", 516, "bfloat16"), ("qS", 256, F8), ("sS", 256, "uint8"),
        ("qI", 256, F8), ("sI", 256, "uint8"), ("qE", 512, F8), ("sE", 512, "uint8"), ("NZ", 256, F8), ("NZs", 256, "uint8"),
        ("pI", 1, "int32"), ("ii", 8, "int32"), ("fc", 8, "float32"), ("cc", 16, "float32"),
        ("tin", 256, "bfloat16"), ("Mneg", 256, "bfloat16"), ("Mtri", 256, "bfloat16"), ("Kn", 128, "bfloat16"), ("RC", 128, "bfloat16"),
        ("sel", 4, "float32"), ("io8", 8, "float32"), ("dmp", 4, "float32"), ("io32", 32, "float32"), ("DG", 32, "bfloat16"),
        ("sgt", 32, "float32"), ("VO", 64, "bfloat16"), ("OE", 8, "float32"), ("urow", 512, "bfloat16"),
        ("yt", 256, "float32"), ("FN", 512, F8), ("FNs", 512, "uint8")):
    SCRATCH[_n] = ("sbuf", [128, _w], _d)
ONCE = ("yd", "yo", "DD", "Dc", "tr2", "trU", "qH", "sH", "H", "Gs", "sC", "Vc", "rk", "trA", "wk",
        "VT", "XR", "R", "pw", "ow", "ix", "own", "NEW", "lo16", "qF", "sF", "qG", "sG")
for _n, _w, _d in (
        ("SW", 704, F8), ("SWs", 704, "uint8"), ("LW", 704, F8), ("LWs", 704, "uint8"), ("XW", 384, F8), ("XWs", 384, "uint8"),
        ("LN", 384, F8), ("LNs", 384, "uint8"), ("PS", 64, F8), ("PSs", 64, "uint8"), ("NP", 128, F8), ("NPs", 128, "uint8"),
        ("qH", 128, F8), ("sH", 128, "uint8"), ("qF", 128, F8), ("sF", 128, "uint8"), ("qG", 128, F8), ("sG", 128, "uint8"),
        ("H", 512, "bfloat16"), ("F", 2560, "bfloat16"), ("NEW", 512, "bfloat16"), ("VT", 96, "bfloat16"),
        ("sC", 4, "float32"), ("Vc", 512, "float32"), ("yd", 512, "float32"), ("yo", 512, "float32"), ("DD", 1024, "bfloat16"),
        ("rk", 4, "float32"), ("trA", 128, "float32"), ("Gs", 64, "float32"), ("trG", 64, "float32"), ("dg", 4, "float32"), ("wk", 5, "float32"),
        ("own", 2, "float32"), ("landM", 6, "float32"), ("landP", 6, "float32"), ("XR", 256, "float32"), ("R", 256, "float32"),
        ("Dc", 1040, "bfloat16"), ("cn", 4, "float32"), ("pw", 8, "float32"), ("ow", 16, "float32"),
        ("tr2", 256, "float32"), ("ix", 40, "float32"), ("UL", 704, "bfloat16"),
        ("trU", 512, "bfloat16"), ("lo16", 128, "uint16"), ("wl", 8, "float32"), ("fo", 4, "float32")):
    for _t in range(1 if _n in ONCE else ROUNDS):
        SCRATCH[_n + str(_t)] = ("sbuf", [128, _w], _d)

SEMAPHORES = ["v", "s", "p", "gc", "ls"] + ["d%d" % k for k in range(80)] + \
    [n + str(t) for n in ("aM", "aP", "aC") for t in range(ROUNDS)]


def rank_program(g, core, T, topo):
    rank = T.rank_of(core)
    if rank is None:
        return
    cores = list(T.cores)
    others = [q for q in range(4) if q != rank]
    Q = {"v": g.vector, "s": g.scalar, "p": g.tensor, "gc": g, "y": g.sync}
    cnt, seen, top, nd = {}, {}, {}, [0]

    def need(qn, deps):
        for d in deps:
            if d is None:
                continue
            if isinstance(d, list):
                need(qn, d)
            elif seen.get((qn, d[0]), 0) < d[1]:
                Q[qn].wait_ge(T.sem[d[0]], d[1])
                seen[(qn, d[0])] = d[1]
                top[d[0]] = max(top.get(d[0], 0), d[1])

    def do(qn, deps, f):
        need(qn, deps)
        f(Q[qn]).then_inc(T.sem[qn], 1)
        cnt[qn] = cnt.get(qn, 0) + 1
        return (qn, cnt[qn])

    def dma(qn, deps, out, in_):
        need(qn, deps)
        s = "d%d" % nd[0]
        nd[0] += 1
        Q[qn].dma_start(out, in_).then_inc(T.sem[s], 16)
        cnt[s] = 16
        return (s, 16)

    def B(n, t):
        return T[n + ("0" if n in ONCE else str(t))]

    dst = [cores[q] for q in others]
    far = [c for c in dst if topo.chip(c) != topo.chip(core)]
    fe = topo.engines(core, far[0])
    eng = {}
    for n, c in enumerate(far):
        w = len(fe) // len(far)
        eng[c] = fe[n * w:(n + 1) * w]
    for c in dst:
        if c not in eng:
            eng[c] = [e for e in topo.engines(core, c) if e not in fe][::len(far)]
    arrive = sum(len(e) for e in eng.values())

    def send(deps, sem, view, land):
        need("gc", deps)
        tr = []
        for q, c in zip(others, dst):
            rid, pid, _ = topo.addr(c)
            s = [x for x in range(4) if x != q].index(rank)
            tr.append(RemoteDMATransfer(dst_ids=[DstId(rid=rid, pnc=pid)], dma_engine_mask=sum(1 << e for e in eng[c]),
                                        remote_sem=T.sem[sem], src=view, dst=land(s)))
        g.remote_dma_fused(tr, local_sem=T.sem["ls"])
        cnt["ls"] = cnt.get("ls", 0) + arrive
        cnt[sem] = cnt.get(sem, 0) + arrive

    def ts(o, i, s1, s2, *ops):
        if len(ops) == 1:
            return lambda q: q.tensor_scalar(o, i, s1, None, ops[0])
        return lambda q: q.tensor_scalar(o, i, s1, s2, ops[0], ops[1])

    def tt(o, a, b, op):
        return lambda q: q.tensor_tensor(o, a, b, op)

    def cp(o, i):
        return lambda q: q.tensor_copy(o, i)

    def act(o, i, fn=AF.Identity, **k):
        return lambda q: q.activation(o, i, fn, **k)

    def red(o, i):
        return lambda q: q.tensor_reduce(o, i, AxisListType.X, A.add)

    def trn(o, i):
        return lambda q: q.transpose(o, i)

    def fill(o, c):
        return lambda q: q.memset(o, c)

    def iota(o, pat, base=0, cm=0):
        return lambda q: q.iota(o, pat, base, cm, allow_small_or_imprecise_dtypes=True)

    def quant(o, s, i):
        return lambda q: q.quantize_mx(o, s, i)

    def mm(o, a, sa, b, sb, st=True, sp=True):
        return lambda q: q.matmul_mx(o, a, sa, b, sb, st, sp)

    U8, U32 = dt.uint8, dt.uint32

    def after(p0):
        return ("gc", cnt["gc"]) if p0 else None

    d_u = dma("s", [], T.u0[:], T.u[:, 0:4])
    d_z = dma("s", [], T.z0[:], T.z[:, 0:4])
    d_lv = dma("y", [], T.t_lv[:], T.lv[:])
    d_dm = dma("y", [], T.t_dm[:], T.dm[:])
    d_nz = dma("y", [], T.t_nz[:], T.nz[:])
    d_w = dma("y", [], T.t_w[:], T.w[:])

    K = {}
    i_p = do("gc", [], lambda q: q.iota(T.pI[:], [[0, 1]], 0, 1))
    v_zer = do("v", [], fill(T.zer[:], 0.0))
    v_tin = do("v", [], fill(T.tin[:], TINY))
    bits = []
    for c, m in enumerate((15, 32, 64, 63, 48, 112, 16)):
        bits.append(do("v", [i_p], ts(T.ii[:, c:c + 1], T.pI[:, 0:1], m, None, A.bitwise_and)))
    v_fc = do("v", bits, cp(T.fc[:, 0:7], T.ii[:, 0:7]))
    v_one = do("v", [], fill(T.ones[:], 1.0))
    v_ss = do("v", [], fill(T.SS[:], 0.0))
    v_si = do("v", [], fill(T.SI[:], 0.0))
    i_mn = do("gc", [v_tin], lambda q: q.affine_select(T.Mneg[:], T.tin[:], [[0, 2], [1, 128]], A.is_ge, -TINY, 0, -1))
    i_mt = do("gc", [v_tin], lambda q: q.affine_select(T.Mtri[:], T.tin[:], [[0, 2], [-1, 128]], A.is_gt, -TINY, 0, 1))
    i_kn = do("gc", [], iota(T.Kn[:], [[16, 4], [0, 2], [1, 16]]))
    K["io32"] = do("gc", [], iota(T.io32[:], [[0, 2], [1, 16]]))
    K["io8"] = do("gc", [], iota(T.io8[:], [[16, 8]]))
    K["OE"] = [do("gc", [], iota(T.OE[:, 0:6], [[1, 3], [64, 2]], 542)), do("gc", [], iota(T.OE[:, 6:8], [[64, 2]], 32))]
    K["EM"] = do("gc", [v_one], lambda q: q.affine_select(T.EM[:], T.ones[:], [[1, 516]], A.is_equal, 0.0, -3, -4))
    K["SI"] = [v_si]
    for p0, p1, at, end, step, c in ((0, 128, 0, 512, 32, 1), (0, 128, 1, 512, 32, 1), (0, 128, 2, 512, 32, 1), (0, 64, 4, 512, 32, 1), (0, 64, 5, 512, 64, 2),
                                     (0, 64, 37, 512, 64, 1), (0, 64, 6, 512, 64, 1), (0, 64, 38, 512, 128, 1), (0, 1, 15, 512, 32, 1), (0, 64, 526, 1024, 128, 1),
                                     (64, 128, 8, 512, 32, 1), (64, 128, 9, 512, 64, 2), (64, 128, 41, 512, 64, 1), (64, 128, 10, 512, 32, 1),
                                     (64, 128, 558, 1024, 128, 1), (64, 65, 15, 512, 32, 1)):
        K["SI"].append(do("gc", [v_si, after(p0)], iota(T.SI[p0:p1, at:end:step], [[0, len(range(at, end, step))]], c)))
    K["177"] = [do("gc", [K["SI"]], iota(B("Dc", 0)[:, 208 * j + 193:208 * j + 194], [[0, 1]], 177)) for j in range(2)]
    F_ = lambda c: T.fc[:, c:c + 1]
    C_ = lambda c: T.cc[:, c:c + 1]
    SG, M1, M0, SM1, SM0, AQ, CD, H1, EV, OD, OB = range(11)

    SW0, SWs0 = B("SW", 0), B("SWs", 0)
    uz, cst = [], []
    for c, src, a, b in ((H1, 5, 1.0, 128.0), (AQ, 2, 4.0, 0.0), (SG, 2, -1 / 32, 1.0)):
        cst.append(do("s", [v_fc], act(C_(c), F_(src), scale=a, bias=b)))
    for b in range(4):
        uz.append(do("v", [d_u, v_one], ts(T.uz[:, b:512:4], T.ones[:, 0:128], T.u0[:, b:b + 1], None, A.mult)))
    for b in range(4):
        uz.append(do("s", [d_z, v_zer], act(T.uz[:, 512 + b:1024:4], T.zer[:], bias=T.z0[:, b:b + 1])))
    q_u = [do("v", uz[0:4], quant(T.qU[:, 0:128], T.sU[:, 0:128], T.uz[:, 0:512]))]
    q_l = do("v", [d_lv], quant(SW0[:, LB:XB], SWs0[:, LB:XB], T.t_lv[:]))
    q_u.append(do("v", uz[4:8], quant(T.qU[:, 128:256], T.sU[:, 128:256], T.uz[:, 512:1024])))
    q_x = do("v", [d_dm], quant(SW0[:, XB:704], SWs0[:, XB:704], T.t_dm[:]))
    sst = []
    for b in range(4):
        t, h = divmod(b, 2)
        hi = C_(H1) if h else F_(5)
        sst.append(do("s", [v_ss, v_one, v_fc], act(T.SS[:, 256 * t + b:256 * t + 256:4], T.ones[:, 0:64], AF.Copy, scale=F_(0))))
        sst.append(do("s", [cst], act(T.SS[:, 512 + 256 * t + b:768 + 256 * t:4], T.ones[:, 0:64], AF.Copy, scale=hi)))
    K["DG"] = do("v", [K["io32"], v_fc], ts(T.DG[:], T.io32[:], F_(0), None, A.is_equal))
    K["sel"] = do("v", [K["io8"]], ts(T.sel[:], T.io8[:, 0:4], F_(4), None, A.is_equal))
    v_qs = do("v", sst, quant(T.qS[:], T.sS[:], T.SS[:]))

    def consts_s():
        for c, src, a, b in ((M1, 1, 1 / 32, 0.0), (M0, 1, -1 / 32, 1.0), (CD, 2, 4.0, float(LB)),
                             (EV, 6, -1 / 16, 1.0), (OD, 6, 1 / 16, 0.0), (OB, 6, -16.0, 0.0)):
            cst.append(do("s", [v_fc], act(C_(c), F_(src), scale=a, bias=b)))
        cst.append(do("s", [cst], act(C_(SM1), C_(M1), scale=C_(SG))))
        cst.append(do("s", [], act(C_(SM0), C_(M0), scale=C_(SG))))
        K["sgt"] = do("s", [v_one], act(T.sgt[:], T.ones[:, 0:32], AF.Copy, scale=C_(SG)))
        Dc = B("Dc", 0)
        K["Dc"] = K["177"] + [do("s", [], act(Dc[:, 816:817], F_(3), scale=4.0, bias=-30.0))]
        for j in range(2):
            K["Dc"].append(do("s", [], act(Dc[:, 208 * j + 192:208 * j + 193], F_(3), scale=2.0)))
        K["wk"] = do("v", [], fill(B("wk", 0)[:, 4:5], -7.5))
        K["VTc"] = do("v", [K["DG"], cst], ts(B("VT", 0)[:, 64:96], T.DG[:], C_(CD), None, A.mult))

    def slots(t):
        F = B("F", t)
        z = do("v", [], fill(F[:, 0:1024], 0.0))
        return [z, do("gc", [z], iota(F[0:64, 515:1024:4], [[0, 4], [0, 2], [1, 16]])),
                do("gc", [z, after(64)], iota(F[64:128, 515:1024:4], [[16, 4], [0, 2], [0, 16]]))]

    def consts_v():
        K["F"] = [slots(0)]
        K["VO"] = [do("v", [K["DG"]], ts(T.VO[:, 32 * s:32 * s + 32], T.DG[:], 64.0 * (s + 1), None, A.mult)) for s in range(2)]
        K["nz"] = do("v", [d_nz], quant(T.NZ[:], T.NZs[:], T.t_nz[:]))
        K["dmp"] = do("v", [K["io8"]], ts(T.dmp[:], T.io8[:, 0:8:2], F_(0), None, A.add))
        K["qE"] = [do("v", [K["EM"]], quant(T.qE[:, 128 * b:128 * b + 128], T.sE[:, 128 * b:128 * b + 128], T.EM[:, 3 - b:515 - b])) for b in range(4)]
        K["np"] = [do("v", [d_nz], quant(B("NP", 0)[:], B("NPs", 0)[:], T.t_nz[:, 0:512]))]
        K["NEW"] = do("v", [], fill(B("NEW", 0)[:, 256:512], 0.0))
        K["qI"] = do("v", K["SI"], quant(T.qI[:], T.sI[:], T.SI[:]))

    def rows():
        K["RC"] = do("gc", K["F"][0], iota(T.RC[:], [[16, 4], [0, 2], [1, 16]], 128))
        K["ur"] = do("gc", [], iota(T.urow[:], [[16, 16], [0, 2], [1, 16]], -128))
        for t in range(ROUNDS):
            K["U%d" % t] = dma("y", [K["ur"]], B("UL", t)[:, 192:704], T.urow[:])

    def consts_2():
        K["F"].append(slots(1))
        K["qW"] = do("v", [d_w], quant(T.qW[:], T.sW[:], T.t_w[:]))
        K["np"].append(do("v", [d_nz], quant(B("NP", 1)[:], B("NPs", 1)[:], T.t_nz[:, 0:512])))

    st = {"prev": []}

    def copies(t, x, dep, r):
        SW, SWs = B("SW", t), B("SWs", t)
        c0 = XB if x else LB
        for dn, o, key in ((("XW", 0, "X"), ("LW", XB, "W")) if x else (("LN", 0, "L"), ("LW", LB, "W"))):
            r.setdefault(key, []).append(dma("y", [dep], B(dn, t)[:, o:o + 256].bitcast(U8), SW[:, c0:c0 + 256].bitcast(U8)))
            r[key].append(dma("y", [dep], B(dn + "s", t)[:, o:o + 256], SWs[:, c0:c0 + 256]))

    def score(t, ty, tk, k):
        SW, SWs, sC, Vc, yd = (B(n, t) for n in ("SW", "SWs", "sC", "Vc", "yd"))
        pr, w = st["prev"], LB + 256 * ty
        qu, su = T.qU[:, 128 * ty:128 * ty + 128], T.sU[:, 128 * ty:128 * ty + 128]
        pX, pY = ((T.pA, T.pC), (T.pB, T.pD))[ty]
        r = do("p", [q_u[ty], tk, pr], mm(pX[:, 0:256], qu, su, SW[:, w:w + 256], SWs[:, w:w + 256]))
        for h in range(2):
            c = do("p", [], mm(pY[:, 512 * h:512 * h + 128], SW[:, w + 128 * h:w + 128 * h + 128],
                               SWs[:, w + 128 * h:w + 128 * h + 128], qu, su))
        ra = do("s", [r, pr], act(Vc[:, 256 * ty:256 * ty + 256], pX[:, 0:256], AF.Abs))
        ca = do("s", [c], act(sC[:, 2 * ty:2 * ty + 2], pY[:, 0:1024:512], AF.Abs))
        ys = [do("s", [ca, ra], act(yd[:, 256 * ty + 128 * h:256 * ty + 128 * h + 128], Vc[:, 256 * ty + 128 * h:256 * ty + 128 * h + 128],
                                    bias=sC[:, 2 * ty + h:2 * ty + h + 1], scale=-1.0)) for h in range(2)]
        k["sc"][ty] = (ca, ra, ys)

    def ahead(t, ty, k):
        sC, Vc, yd, DD = (B(n, t) for n in ("sC", "Vc", "yd", "DD"))
        ca, ra, ys = k["sc"][ty]
        o = 512 * ty
        f0, f1, f2 = ((A.is_lt, A.is_le, A.is_gt), (A.is_gt, A.is_ge, A.is_lt))[ty]
        a = do("v", [ca, ra, st["prev"]], ts(DD[:, o:o + 128], Vc[:, 256 * ty + 128:256 * ty + 256], sC[:, 2 * ty:2 * ty + 1], None, f0))
        b = do("v", [ca, ra], ts(DD[:, o + 384:o + 512], Vc[:, 256 * ty:256 * ty + 128], sC[:, 2 * ty + 1:2 * ty + 2], None, f1))
        d = do("v", [ys, i_mn, i_mt], tt(DD[:, o + 128:o + 384], yd[:, 256 * ty:256 * ty + 256], (T.Mneg, T.Mtri)[ty][:], f2))
        return [a, b, d]

    def order_and_send(t, k):
        Vc, DD, rk, H = (B(n, t) for n in ("Vc", "DD", "rk", "H"))
        pr, r = st["prev"], {}

        def hot(b):
            return do("v", [r[b], i_kn, pr], ts(H[:, b:512:4], T.Kn[:], rk[:, b:b + 1], None, A.is_equal))

        def total(b, dd):
            r[b] = do("s", dd, act(DD[:, 256 * b:256 * b + 256], DD[:, 256 * b:256 * b + 256], accum_out=rk[:, b:b + 1]))

        f, l = k["first"], 1 - k["first"]
        dd = ahead(t, f, k)
        total(2 * f, dd)
        total(2 * f + 1, dd)
        dd = ahead(t, l, k)
        total(2 * l, dd)
        r[2 * l + 1] = do("v", dd, red(rk[:, 2 * l + 1:2 * l + 2], DD[:, 512 * l + 256:512 * l + 512]))
        hs = [hot(b) for b in (2 * f, 2 * f + 1, 2 * l + 1, 2 * l)]
        qh = do("v", hs, quant(B("qH", t)[:], B("sH", t)[:], H[:]))
        do("p", [qh, v_qs, pr], mm(T.pD[:, 0:128], T.qS[:, 0:128], T.sS[:, 0:128], B("qH", t)[:], B("sH", t)[:], True, False))
        m = do("p", [], mm(T.pD[:, 0:128], T.qS[:, 128:256], T.sS[:, 128:256], B("qH", t)[:], B("sH", t)[:], False, True))
        trA, lo, G, trG = B("trA", t), B("lo16", t), B("Gs", t), B("trG", t)
        k["trA"] = a = do("v", [m], trn(trA[:], T.pD[:, 0:128]))
        of = do("v", [a, cst[1]], ts(lo[:, 0:4], trA[:, 0:128:32], C_(AQ), None, A.add))
        gs = do("v", [of, k["sc"][0][1], k["sc"][1][1], pr], cp(G[:], Vc[:, 0:512].indirect(lo[:, 0:4])))
        k["M"] = tg = do("v", [gs], trn(trG[:], G[:]))
        send([tg], "aM%d" % t, trG[:, 31:33], lambda s: B("landM", t)[:, 2 * s:2 * s + 2])

    def prepare(t, k):
        own, wk, dg, VT, trA, trG, XR = (B(n, t) for n in ("own", "wk", "dg", "VT", "trA", "trG", "XR"))
        w = do("v", [k["trA"], K["sel"]], tt(wk[:, 0:4], trA[:, 0:128:32], T.sel[:], A.mult))
        a = do("v", [k["M"], cst], ts(own[:, 1:2], trG[:, 32:33], C_(SM1), None, A.mult))
        pl = do("v", [w, K["wk"]], red(dg[:, 0:1], wk[:]))
        k["s"] = do("v", [a], ts(own[:, 0:1], trG[:, 31:32], C_(SM0), own[:, 1:2], A.mult, A.add))
        hi = do("v", [pl], ts(dg[:, 1:2], dg[:, 0:1], R16, R16, A.add, A.subtract))
        xo = [do("s", [k["M"], K["sgt"]], act(XR[:, 192 + 32 * j:224 + 32 * j], T.sgt[:], AF.Copy, scale=trG[:, 31 + j:32 + j])) for j in range(2)]
        v1 = do("v", [hi], ts(VT[:, 32:64], T.DG[:], dg[:, 1:2], None, A.mult))
        lo_ = do("v", [hi], ts(dg[:, 2:3], dg[:, 0:1], dg[:, 1:2], 7.5, A.subtract, A.add))
        k["Ro"] = do("v", xo, trn(B("R", t)[:, 192:256], XR[:, 192:256]))
        v0 = do("v", [lo_], ts(VT[:, 0:32], T.DG[:], dg[:, 2:3], None, A.mult))
        k["VT"] = [v0, v1, K["VTc"]]

    def before(s, q, t, deps, at, x_of, neg=None):
        R, Dc, out, seg = B("R", t), B("Dc", t), [], []
        for x in x_of:
            op = A.is_le if (others + [rank])[x] < q else A.is_lt
            if seg and seg[-1][1] == 64 * x and seg[-1][2] == op:
                seg[-1][1] += 64
            else:
                seg.append([64 * x, 64 * x + 64, op])
        for (c0, c1, op) in seg:
            if neg is None:
                out.append(do("v", deps, ts(Dc[:, at:at + c1 - c0], R[:, c0:c1], s, 4.0, op, A.mult)))
            else:
                out.append(do("s", deps, act(Dc[:, at:at + c1 - c0], neg[0][:, neg[1] + c0:neg[1] + c1], AF.Sign, bias=TINY if op == A.is_le else -TINY)))
            at += c1 - c0
        return out

    def merge_and_send(t, k):
        LM, XR, R, Dc, cn, pw, lo, own, F, ow, yo = (B(n, t) for n in ("landM", "XR", "R", "Dc", "cn", "pw", "lo16", "own", "F", "ow", "yo"))
        aM = ("aM%d" % t, arrive)
        xs = []
        for j in range(6):
            if j % 2 == 0:
                xs.append(do("v", [aM, cst], ts(XR[:, 32 * j:32 * j + 32], T.ones[:, 0:32], LM[:, j:j + 1], C_(SG), A.mult, A.mult)))
            else:
                xs.append(do("s", [aM, K["sgt"]], act(XR[:, 32 * j:32 * j + 32], T.sgt[:], AF.Copy, scale=LM[:, j:j + 1])))
        k["R"] = do("v", xs, trn(R[:, 0:192], XR[:, 0:192]))
        d = before(own[:, 0:1], rank, t, [k["R"], k["s"], st["prev"]], 624, range(3))
        k["cn"] = c = do("v", [d, K["Dc"]], red(cn[:, 3:4], Dc[:, 624:817]))
        fl = do("v", [c], ts(pw[:, 0:1], cn[:, 3:4], R64, R64, A.add, A.subtract))
        of = do("v", [fl, K["OE"]], ts(lo[:, 4:10], T.OE[:, 0:6], pw[:, 0:1], cn[:, 3:4], A.add, A.add))
        sc = do("v", [of, k["VT"], K["F"][t]], cp(F[:, 0:2560].indirect(lo[:, 4:10]), B("VT", t)[:]))
        k["qF"] = do("v", [sc], quant(B("qF", t)[:], B("sF", t)[:], F[:, 512:1024]))
        m = do("p", [k["qF"], K["qI"], st["prev"]], mm(T.pD[:, 512:640], T.qI[:, 0:128], T.sI[:, 0:128], B("qF", t)[:], B("sF", t)[:]))
        k["own2"] = do("p", [k["sc"][1][1]], mm(T.pB[:, 0:128], B("qF", t)[:], B("sF", t)[:], T.qI[:, 0:128], T.sI[:, 0:128]))
        o2 = [do("s", [aM, cst], act(ow[:, s:s + 1], LM[:, 2 * s:2 * s + 1], scale=C_(SM0))) for s in range(2)]
        for s in range(2):
            o2[s] = do("s", [o2[s]], act(ow[:, 8 + s:9 + s], LM[:, 2 * s + 1:2 * s + 2], scale=C_(SM1), bias=ow[:, s:s + 1]))
        ys = [do("s", [o2[s], k["R"], k["Ro"]], act(yo[:, 256 * s + 64 - 64 * s:256 * s + 256], R[:, 64 - 64 * s:256], bias=ow[:, 8 + s:9 + s], scale=-1.0)) for s in range(2)]
        sg = [before(None, others[s], t, [ys[s], st["prev"]], 208 * s, [x for x in range(4) if x != s], (yo, 256 * s)) for s in range(2)]
        k["c2"] = [do("s", [sg[s], K["Dc"]], act(Dc[:, 416 + 416 * s:610 + 416 * s], Dc[:, 208 * s:208 * s + 194], scale=2.0, accum_out=cn[:, s:s + 1])) for s in range(2)]
        a = do("v", [m], trn(B("tr2", t)[:, 0:128], T.pD[:, 512:640]))
        of = do("v", [a], ts(lo[:, 10:14], B("tr2", t)[:, 0:128:32], float(LB), 703.0, A.max, A.min))
        k["tr2"] = a
        pd = [of, k["lt"], k["xt"]]
        ps = do("v", pd, cp(B("PS", t)[:].bitcast(U32), B("SW", t)[:, 0:704].bitcast(U32).indirect(lo[:, 10:14])))
        pss = do("s", pd, act(B("PSs", t)[:], B("SWs", t)[:, 0:704].indirect(lo[:, 10:14]), AF.Copy))
        LW, LWs = B("LW", t), B("LWs", t)
        o = (64, 128, 0)
        send([ps], "aC%d" % t, B("PS", t)[:, 0:64].bitcast(U8), lambda s: LW[:, o[s]:o[s] + 64].bitcast(U8))
        send([pss], "aC%d" % t, B("PSs", t)[:, 0:64], lambda s: LWs[:, o[s]:o[s] + 64])

    def lists(t, k):
        cn, pw, lo, F, ix, tr2, wl, UL, trU = (B(n, t) for n in ("cn", "pw", "lo16", "F", "ix", "tr2", "wl", "UL", "trU"))
        tok = k["tr2"]
        row = lambda r, g=0: tr2[:, 128 * g + r:128 * g + 128:32]
        nl = do("v", [tok], cp(lo[:, 24:28], row(25)))
        e = [do("s", [tok, cst], act(ix[:, 0:4], row(1), AF.Copy, scale=C_(EV))),
             do("s", [tok, cst], act(ix[:, 4:8], row(2), scale=C_(OD), bias=C_(OB)))]
        fl = do("v", k["c2"], ts(pw[:, 2:4], cn[:, 0:2], R64, R64, A.add, A.subtract))
        nd_ = [nl, K["nz"], K["np"][t], st["prev"]]
        k["np"] = [do("s", nd_, act(B("NPs", t)[:, 64:128], T.NZs[:, 0:256].indirect(lo[:, 24:28]), AF.Copy))]
        of = [do("v", [fl, K["OE"]], ts(lo[:, 16 + 2 * s:18 + 2 * s], T.OE[:, 6:8], pw[:, 2 + s:3 + s], cn[:, s:s + 1], A.add, A.add)) for s in range(2)]
        u1 = do("v", e, tt(ix[:, 8:12], ix[:, 0:4], ix[:, 4:8], A.max))
        sc = do("v", [of, K["VO"], k["qF"]], cp(F[:, 0:2560].indirect(lo[:, 16:20]), T.VO[:]))
        u2 = do("v", [u1, K["dmp"]], tt(ix[:, 12:16], ix[:, 8:12], T.dmp[:], A.max))
        qg = do("v", [sc], quant(B("qG", t)[:], B("sG", t)[:], F[:, 0:512]))
        do("p", [k["qF"], k["trA"]], mm(T.pD[:, 0:128], T.qI[:, 0:128], T.sI[:, 0:128], B("qF", t)[:], B("sF", t)[:], True, False))
        mo = do("p", [qg], mm(T.pD[:, 0:128], T.qI[:, 128:256], T.sI[:, 128:256], B("qG", t)[:], B("sG", t)[:], False, True))
        uo = [do("v", [u2], ts(lo[:, 48 + h:56:2], ix[:, 12:16], 16.0 * h, None, A.add)) for h in range(2)]
        k["np"].append(do("v", nd_, cp(B("NP", t)[:, 64:128].bitcast(U32), T.NZ[:, 0:256].bitcast(U32).indirect(lo[:, 24:28]))))
        k["dn"] = [do("p", [k["np"], K["qE"], st["prev"]], mm(T.pC[:, 512 * b:512 * b + 128], T.qE[:, 128 * b:128 * b + 128], T.sE[:, 128 * b:128 * b + 128],
                                                              B("NP", t)[:], B("NPs", t)[:], True, False)) for b in range(4)]
        w1 = do("s", [k["own2"]], act(wl[:, 0:2], T.pB[:, 9:11], AF.Sign))
        k["w"] = []
        for j in range(2):
            w2 = do("s", [w1], act(wl[:, 2 + j:3 + j], wl[:, j:j + 1], AF.Copy, scale=256.0 * rank - (LB, XB)[j]))
            k["w"].append(do("s", [w2], act(wl[:, 4 + j:5 + j], T.pB[:, 9 + j:10 + j], bias=wl[:, 2 + j:3 + j])))
        send([k["w"]], "aP%d" % t, wl[:, 4:6], lambda s: B("landP", t)[:, 2 * s:2 * s + 2])
        us = do("v", [uo, K["RC"], K["U%d" % t]], cp(UL[:, 0:704].indirect(lo[:, 48:56]), T.RC[:]))
        a = do("v", [mo], trn(tr2[:, 128:256], T.pD[:, 0:128]))
        m = [do("v", [a], tt(ix[:, 16 + 4 * j:20 + 4 * j], row(9 + j), row(3 + 8 * j, 1), A.max)) for j in range(2)]
        k["AB"] = do("v", m, cp(lo[:, 32:40], ix[:, 16:24]))
        a = do("v", [us], trn(trU[:], UL[:, 192:704]))
        k["pl"] = [do("v", [a], ts(lo[:, 64 + 16 * x:80 + 16 * x], trU[:, 16 * x:512:32], 128.0, None, A.add)) for x in range(2)]

    def renew(t, k, oq, os_, o):
        LW, LWs, XW, XWs, LN, LNs, NEW, lo = (B(n, t) for n in ("LW", "LWs", "XW", "XWs", "LN", "LNs", "NEW", "lo16"))
        ad = [("aC%d" % t, 2 * arrive), k["AB"], k["cp"]["W"]]
        a2 = do("s", ad, act(XWs[:, 256:384], LWs[:, 0:704].indirect(lo[:, 32:40]), AF.Copy))
        a1 = do("v", ad, cp(XW[:, 256:384].bitcast(U32), LW[:, 0:704].bitcast(U32).indirect(lo[:, 32:40])))
        dc = [do("p", [a1, a2], mm(T.pC[:, 512 * b:512 * b + 128], T.qE[:, 128 * b:128 * b + 128], T.sE[:, 128 * b:128 * b + 128],
                                   XW[:, 256:384], XWs[:, 256:384], False, True)) for b in range(4)]
        xd = [k["pl"], k["cp"]["X"], a1, a2]
        x1 = do("v", xd, cp(oq[:, o + 256:o + 512].bitcast(U32), XW[:, 0:384].bitcast(U32).indirect(lo[:, 80:96])))
        x2 = do("s", xd, act(os_[:, o + 256:o + 512], XWs[:, 0:384].indirect(lo[:, 80:96]), AF.Copy))
        nw = []
        for b in range(4):
            i, h = T.pC[:, 512 * b + 64:512 * b + 128], NEW[:, b:256:4]
            nw.append(do("v", [dc[b]], ts(h, i, 0.5, None, A.mult)) if b % 2 else do("s", [dc[b], st["prev"]], act(h, i, AF.Copy, scale=0.5)))
        qn = do("v", [nw, K["NEW"]], quant(LN[:, 256:384], LNs[:, 256:384], NEW[:]))
        return qn, nw, [x1, x2]

    def renew_live(t, k, qn, oq, os_, o):
        LN, LNs, lo = B("LN", t), B("LNs", t), B("lo16", t)
        ld = [qn, k["pl"], k["cp"]["L"]]
        l2 = do("s", ld, act(os_[:, o:o + 256], LNs[:, 0:384].indirect(lo[:, 64:80]), AF.Copy))
        l1 = do("v", ld, cp(oq[:, o:o + 256].bitcast(U32), LN[:, 0:384].bitcast(U32).indirect(lo[:, 64:80])))
        return [l1, l2]

    def numbers(t, k):
        LP, fo, wl = B("landP", t), B("fo", t), B("wl", t)
        aP = ("aP%d" % t, arrive)
        a = [do("v", [aP], red(fo[:, j:j + 1], LP[:, j:6:2])) for j in range(2)]
        b = do("v", [a, k["w"]], tt(fo[:, 2:4], fo[:, 0:2], wl[:, 4:6], A.add))
        for c in range(4):
            dma("y", [b], T.lw[t:t + 1, 16 * c:16 * c + 16], fo[32 * c:32 * c + 16, 2:3])
            dma("y", [b], T.sw[t:t + 1, 16 * c:16 * c + 16], fo[32 * c:32 * c + 16, 3:4])

    ks = [{"sc": {}, "cp": {}} for t in range(ROUNDS)]
    k = ks[0]
    k["lt"], k["xt"], k["first"] = q_l, q_x, 0
    for ty in range(2):
        score(0, ty, (q_l, q_x)[ty], k)
        copies(0, ty, (q_l, q_x)[ty], k["cp"])
    for t in range(ROUNDS):
        k = ks[t]
        last = t + 1 == ROUNDS
        order_and_send(t, k)
        if t == 0:
            consts_s()
        prepare(t, k)
        if t == 0:
            consts_v()
            rows()
        else:
            consts_2()
            numbers(0, ks[0])
        merge_and_send(t, k)
        lists(t, k)
        oq, os_, o = (T.FN, T.FNs, 0) if last else (B("SW", t + 1), B("SWs", t + 1), LB)
        qn, nw, xt = renew(t, k, oq, os_, o)
        if last:
            lt = renew_live(t, k, qn, oq, os_, o)
            dma("y", xt, T.oc[:, 1024:2048], T.FN[:, 256:512].bitcast(U8))
            for q in range(4):
                dma("y", xt, T.osc[4 * q:4 * q + 4, 256:512], T.FNs[32 * q:32 * q + 4, 256:512])
            my = do("p", [lt, K["qW"], k["sc"][0][1]], mm(T.pA[:, 0:256], T.qW[:], T.sW[:], T.FN[:, 0:256], T.FNs[:, 0:256]))
            dma("y", lt, T.oc[:, 0:1024], T.FN[:, 0:256].bitcast(U8))
            for q in range(4):
                dma("y", lt, T.osc[4 * q:4 * q + 4, 0:256], T.FNs[32 * q:32 * q + 4, 0:256])
            yc = do("s", [my], act(T.yt[:], T.pA[:, 0:256], AF.Copy))
            dma("s", [yc], T.y[:], T.yt[:])
            numbers(t, k)
        else:
            n = ks[t + 1]
            n["xt"], n["first"] = xt, 1
            st["prev"] = [xt, nw, k["w"]]
            copies(t + 1, 1, xt, n["cp"])
            n["lt"] = lt = renew_live(t, k, qn, oq, os_, o)
            score(t + 1, 1, xt, n)
            copies(t + 1, 0, lt, n["cp"])
            score(t + 1, 0, lt, n)
            st["prev"] = [lt, xt, nw, k["w"]]
    for s, n in cnt.items():
        if top.get(s, 0) < n:
            g.wait_ge(T.sem[s], n)
